import numpy as np
import ml_dtypes


def mxq(x, axis, fmt="e4m3"):
    dtype, down = {"e4m3": (ml_dtypes.float8_e4m3fn, 7), "e5m2": (ml_dtypes.float8_e5m2, 14)}[fmt]
    v = np.moveaxis(np.asarray(x, np.float32).astype(ml_dtypes.bfloat16).astype(np.float64), axis, -1)
    blocks = v.reshape(v.shape[:-1] + (-1, 32))
    amax = np.abs(blocks).max(-1, keepdims=True)
    byte = np.maximum(np.where(amax > 0, np.frexp(amax)[1] - 1 + 127, 0) - down, 1)
    scale = np.exp2(byte - 127.0)
    codes = (blocks / scale).astype(np.float32).astype(dtype).astype(np.float64)
    return np.moveaxis((codes * scale).reshape(v.shape), -1, axis)


WIDE = False


def mx_kscale(k):
    if not WIDE:
        return np.ones(k)
    levels = np.array([10, -10, 5, -5, 0])
    if k % 512:
        return np.exp2(np.random.permutation(np.resize(levels, k // 32))).repeat(32)
    a = np.empty((k // 512, 16))
    for p in range(k // 512):
        a[p, :8] = np.random.permutation(np.resize(levels, 8))
        for g in range(8):
            far = levels[np.abs(levels - a[p, g]) >= 10]
            a[p, g + 8] = far[np.random.randint(len(far))]
    return np.exp2(a.ravel()).repeat(32)


BF16 = ml_dtypes.bfloat16


def bf(x):
    return np.asarray(x, np.float32).astype(BF16)


def f64(x):
    return np.asarray(x).astype(np.float64)

E4M3FN = np.array([(-1.0 if i & 128 else 1.0) * ((1.0 + (i & 7) / 8.0) * 2.0 ** (((i >> 3) & 15) - 7) if i & 120 else (i & 7) * 2.0 ** -9) for i in range(256)])


def e4m3fn_bytes(y):
    return np.clip(np.asarray(y, np.float64), -448.0, 448.0).astype(np.float32).astype(ml_dtypes.float8_e4m3fn).view(np.uint8)


def e4m3fn_values(b):
    return E4M3FN[b]


M, K, R, B = 4096, 2048, 512, 128

FMAX = 448.0
BETA = 0.9


def setup_inputs():
    s = mx_kscale(K)
    grad = np.random.standard_normal((M, K)) * s
    basis = np.random.standard_normal((R, K)) / np.sqrt(K) / s
    grad_scale = (np.abs(grad).reshape(M, K // B, B).max(axis=2) / FMAX).astype(np.float32)
    basis_scale = (np.abs(basis).reshape(R // B, B, K // B, B).max(axis=(1, 3)) / FMAX).astype(np.float32)
    grad_bytes = e4m3fn_bytes(grad / np.repeat(f64(grad_scale), B, axis=1))
    basis_bytes = e4m3fn_bytes(basis / np.repeat(np.repeat(f64(basis_scale), B, axis=0), B, axis=1))
    return {"grad_bytes": grad_bytes, "grad_scale": grad_scale,
            "basis_bytes": basis_bytes, "basis_scale": basis_scale,
            "mom": bf(np.random.standard_normal((M, R))),
            "lr": bf(0.5 + np.random.random_sample(M))}


def reference(grad_bytes, grad_scale, basis_bytes, basis_scale, mom, lr):
    grad = e4m3fn_values(grad_bytes) * np.repeat(f64(grad_scale), B, axis=1)
    basis = e4m3fn_values(basis_bytes) * np.repeat(np.repeat(f64(basis_scale), B, axis=0), B, axis=1)
    low = mxq(grad, 1, "e4m3") @ mxq(basis, 1, "e4m3").T
    mom_new = BETA * f64(mom) + low
    step = f64(lr)[:, None] * mom_new
    return step, mom_new

@@ -1,0 +1,278 @@
+from contextlib import ExitStack
+
+import concourse.mybir as mybir
+from concourse.masks import make_identity
+
+TOKENS, K, RANK = 4096, 2048, 512
+P = 128
+TILES = TOKENS // P
+PASSES = K // 512
+SCALES = K // 128
+BETA = 0.9
+FLOPS = 2 * TOKENS * K * RANK
+
+F32 = mybir.dt.float32
+BF16 = mybir.dt.bfloat16
+U32 = mybir.dt.uint32
+U8 = mybir.dt.uint8
+FP8 = mybir.dt.float8_e4m3fn
+FP8X4 = mybir.dt.float8_e4m3fn_x4
+MULT = mybir.AluOpType.mult
+ADD = mybir.AluOpType.add
+COPY = mybir.ActivationFunctionType.Copy
+
+V_PASSES = 3
+AHEAD = 8
+
+
+def tile_galore_projected_step_d2_kernel(tc, grad_bytes, grad_scale, basis_bytes, basis_scale, mom, lr, out_0, out_1):
+    nc = tc.nc
+    grad_rows = grad_bytes.rearrange("(p i) k -> p i k", p=P)
+    mom_rows = mom.rearrange("(p i) n -> p i n", p=P)
+    step_rows = out_0.rearrange("(p i) n -> p i n", p=P)
+    new_rows = out_1.rearrange("(p i) n -> p i n", p=P)
+
+    with ExitStack() as ctx:
+        keep = ctx.enter_context(tc.tile_pool(name="keep", bufs=1))
+        load = ctx.enter_context(tc.tile_pool(name="load", bufs=AHEAD + 3))
+        work = ctx.enter_context(tc.tile_pool(name="work", bufs=3))
+        outs = ctx.enter_context(tc.tile_pool(name="outs", bufs=5))
+        psum_t = ctx.enter_context(tc.psum_pool(name="psum_t", bufs=5))
+        psum_m = ctx.enter_context(tc.psum_pool(name="psum_m", bufs=3))
+        ctx.enter_context(tc.manual_schedule())
+
+        ident = keep.tile([P, P], F32, name="ident")
+        make_identity(nc, ident[:])
+
+        basis_sc = keep.tile([P, (RANK // P) * SCALES], F32, name="basis_sc")
+        nc.sync.dma_start(out=basis_sc[:], in_=basis_scale.rearrange("b c -> (b c)").partition_broadcast(P))
+        basis_raw = {}
+        basis_rows = basis_bytes.rearrange("(b p) k -> p b k", p=P)
+        for h in (1, 0):
+            braw = keep.tile([P, RANK // P, K // 2], U8, name="braw%d" % h)
+            nc.sync.dma_start(out=braw[:], in_=basis_rows[:, :, h * (K // 2) : (h + 1) * (K // 2)])
+            basis_raw[h] = braw
+        grad_sc = keep.tile([P, TILES * SCALES], F32, name="grad_sc")
+        nc.sync.dma_start(out=grad_sc[:], in_=grad_scale.rearrange("(p i) c -> p (i c)", p=P))
+
+        graw = {}
+        momt = {}
+
+        def load_grad(m):
+            if m >= TILES // 2:
+                return
+            g = load.tile([P, 2, K], U8, name="g")
+            nc.sync.dma_start(out=g[:], in_=grad_rows[:, 2 * m : 2 * m + 2, :])
+            graw[m] = g
+
+        def load_mom(m):
+            if m >= TILES // 4:
+                return
+            mo = keep.tile([P, 4, RANK], BF16, name="mo%d" % m)
+            nc.sync.dma_start(out=mo[:], in_=mom_rows[:, 4 * m : 4 * m + 4, :])
+            momt[m] = mo
+
+        load_grad(0)
+        lr_raw = keep.tile([P, TILES], BF16, name="lr_raw")
+        nc.sync.dma_start(out=lr_raw[:], in_=lr.rearrange("(p i) -> p i", p=P))
+        load_mom(0)
+        for m in range(1, AHEAD):
+            load_grad(m)
+        load_mom(1)
+
+        dummy = keep.tile([P, 1], F32, name="dummy")
+        nc.scalar.activation(out=dummy[:], in_=ident[:, 0:1], func=COPY)
+
+        def widen_v(dst, src, sc):
+            for q in range(4):
+                nc.vector.tensor_scalar(
+                    out=dst.rearrange("p (u b j) -> p b u j", u=2, j=16)[:, 4 * q : 4 * q + 4],
+                    in0=src[:, 128 * q : 128 * q + 128].bitcast(FP8).rearrange("p (b u j) -> p b u j", u=2, j=16),
+                    scalar1=sc[:, q : q + 1],
+                    scalar2=None,
+                    op0=MULT,
+                )
+
+        def widen_s(dst, src, sc):
+            for q in range(4):
+                nc.scalar.activation(out=dst[:, 128 * q : 128 * q + 128], in_=src[:, 128 * q : 128 * q + 128].bitcast(FP8), func=COPY, scale=sc[:, q : q + 1])
+
+        def words_of(wide, g):
+            w = wide.bitcast(F32)
+            if g < V_PASSES:
+                return w[:, 0:128], w[:, 128:256]
+            return w[:, 0:256:2], w[:, 1:256:2]
+
+        nb = RANK // P
+        bwide = {}
+        for g in range(PASSES):
+            bw = keep.tile([P, nb, 512], BF16, name="bw%d" % g, align_bytes=64)
+            bwide[g] = bw
+        bgroup = {}
+        for g in range(PASSES):
+            bg = keep.tile([P, RANK * 4], BF16, name="bg%d" % g, align_bytes=64)
+            bgroup[g] = bg
+        bcodes = keep.tile([P, PASSES, RANK], U32, name="bcodes", align_bytes=64)
+        bscales = keep.tile([P, PASSES, RANK], U8, name="bscales", align_bytes=64)
+
+        def basis_widen(g):
+            for b in range(nb):
+                src = basis_raw[g // 2][:, b, 512 * (g % 2) : 512 * (g % 2) + 512]
+                sc = basis_sc[:, SCALES * b + 4 * g : SCALES * b + 4 * g + 4]
+                (widen_v if g < V_PASSES else widen_s)(bwide[g][:, b, :], src, sc)
+
+        bbank = {}
+
+        def basis_turn(g):
+            for h in range(2):
+                xt = psum_t.tile([P, 2, 2, P], F32, name="xt")
+                for b in range(2):
+                    for u, w in enumerate(words_of(bwide[g][:, 2 * h + b, :], g)):
+                        nc.tensor.transpose(xt[:, b, u, :], w, ident[:])
+                bbank[g, h] = xt
+
+        def basis_out(g, copy):
+            for h in range(2):
+                copy(
+                    out=bgroup[g][:, 1024 * h : 1024 * h + 1024].bitcast(F32).rearrange("p (b r u) -> p b r u", b=2, u=2),
+                    in_=bbank[g, h][:].rearrange("p b u r -> p b r u"),
+                )
+
+        def basis_quant(g):
+            nc.vector.quantize_mx(out=bcodes[:, g, :].bitcast(FP8X4), scales=bscales[:, g, :], in_=bgroup[g][:])
+
+        wide = {}
+        bank = {}
+        group = {}
+        codes = {}
+        acc = {}
+        new = {}
+        step = {}
+        lr_f = keep.tile([P, TILES], F32, name="lr_f")
+
+        def wv(i):
+            if i >= TILES:
+                return
+            wide_v = work.tile([P, V_PASSES, 512], BF16, name="wide_v", align_bytes=64)
+            for g in range(V_PASSES):
+                widen_v(wide_v[:, g, :], graw[i // 2][:, i % 2, 512 * g : 512 * g + 512], grad_sc[:, SCALES * i + 4 * g : SCALES * i + 4 * g + 4])
+            for g in range(V_PASSES):
+                wide[i, g] = wide_v[:, g, :]
+
+        def ws(i):
+            if i >= TILES:
+                return
+            wide_s = work.tile([P, 512], BF16, name="wide_s", align_bytes=64)
+            g = V_PASSES
+            widen_s(wide_s[:], graw[i // 2][:, i % 2, 512 * g : 512 * g + 512], grad_sc[:, SCALES * i + 4 * g : SCALES * i + 4 * g + 4])
+            wide[i, g] = wide_s[:]
+
+        def turn(i):
+            for h in range(2):
+                xt = psum_t.tile([P, 2, 2, P], F32, name="xt")
+                for gg in range(2):
+                    for u, w in enumerate(words_of(wide[i, 2 * h + gg], 2 * h + gg)):
+                        nc.tensor.transpose(xt[:, gg, u, :], w, ident[:])
+                bank[i, h] = xt
+
+        def out_of_psum(i):
+            grp = work.tile([P, K], BF16, name="grp", align_bytes=64)
+            for h in range(2):
+                nc.scalar.copy(
+                    out=grp[:, 1024 * h : 1024 * h + 1024].bitcast(F32).rearrange("p (g r u) -> p g r u", g=2, u=2),
+                    in_=bank[i, h][:].rearrange("p g u r -> p g r u"),
+                )
+            group[i] = grp
+
+        def quant(i):
+            cod = work.tile([P, PASSES * P], U32, name="cod", align_bytes=64)
+            scl = work.tile([P, PASSES * P], U8, name="scl", align_bytes=64)
+            nc.vector.quantize_mx(out=cod[:].bitcast(FP8X4), scales=scl[:], in_=group[i][:])
+            codes[i] = (cod, scl)
+
+        def mm(i):
+            a = psum_m.tile([P, RANK], F32, name="a")
+            cod, scl = codes[i]
+            for g in range(PASSES):
+                nc.tensor.matmul_mx(
+                    out=a[:],
+                    lhsT=cod[:, P * g : P * g + P].bitcast(FP8X4),
+                    lhsT_scale=scl[:, P * g : P * g + P],
+                    rhs=bcodes[:, g, :].bitcast(FP8X4),
+                    rhs_scale=bscales[:, g, :],
+                    start=(g == 0),
+                    stop=(g == PASSES - 1),
+                )
+            acc[i] = a
+
+        def halves(i):
+            return [slice(0, 256), slice(256, 512)] if i == TILES - 1 else [slice(0, 512)]
+
+        def momentum(i):
+            if i % 2 == 0:
+                nw = outs.tile([P, 2, RANK], F32, name="nw")
+                new[i // 2] = nw
+            for c in halves(i):
+                nc.vector.scalar_tensor_tensor(
+                    out=new[i // 2][:, i % 2, c], in0=momt[i // 4][:, i % 4, c], scalar=BETA, in1=acc[i][:, c], op0=MULT, op1=ADD)
+
+        def stepped(i):
+            if i % 2 == 0:
+                sp = outs.tile([P, 2, RANK], F32, name="sp")
+                step[i // 2] = sp
+            for c in halves(i):
+                nc.scalar.activation(out=step[i // 2][:, i % 2, c], in_=new[i // 2][:, i % 2, c], func=COPY, scale=lr_f[:, i : i + 1])
+
+        def store(i):
+            m = i // 2
+            if m == TILES // 2 - 1:
+                for c in halves(i):
+                    nc.sync.dma_start(out=new_rows[:, i, c], in_=new[m][:, i % 2, c])
+                    nc.sync.dma_start(out=step_rows[:, i, c], in_=step[m][:, i % 2, c])
+            elif i % 2 == 1:
+                nc.sync.dma_start(out=new_rows[:, 2 * m : 2 * m + 2, :], in_=new[m][:])
+                nc.sync.dma_start(out=step_rows[:, 2 * m : 2 * m + 2, :], in_=step[m][:])
+
+        basis_widen(2)
+        basis_widen(3)
+        basis_turn(2)
+        basis_widen(0)
+        basis_turn(0)
+        basis_out(2, nc.scalar.copy)
+        basis_turn(3)
+        basis_widen(1)
+        basis_turn(1)
+        basis_quant(2)
+        basis_out(0, nc.scalar.copy)
+        basis_out(1, nc.vector.tensor_copy)
+        basis_out(3, nc.scalar.copy)
+        ws(0)
+        wv(0)
+        basis_quant(0)
+        turn(0)
+        basis_quant(1)
+        ws(1)
+        wv(1)
+        basis_quant(3)
+        nc.vector.tensor_copy(out=lr_f[:], in_=lr_raw[:])
+
+        for j in range(TILES + 3):
+            if j % 2 == 0:
+                load_grad(j // 2 + AHEAD)
+            if j % 4 == 2:
+                load_mom(j // 4 + 2)
+            if j < TILES:
+                out_of_psum(j)
+            wv(j + 2)
+            ws(j + 2)
+            if j + 1 < TILES:
+                turn(j + 1)
+            if 2 <= j < TILES + 2:
+                momentum(j - 2)
+            if j < TILES:
+                quant(j)
+            if 1 <= j <= TILES:
+                mm(j - 1)
+            if j >= 3:
+                stepped(j - 3)
+                store(j - 3)

@@ -8,6 +8,7 @@ P = 128
 TILES = TOKENS // P
 PASSES = K // 512
 SCALES = K // 128
+ROW_TILES = RANK // P
 BETA = 0.9
 FLOPS = 2 * TOKENS * K * RANK
 
@@ -21,125 +22,108 @@ MULT = mybir.AluOpType.mult
 ADD = mybir.AluOpType.add
 COPY = mybir.ActivationFunctionType.Copy
 
-V_PASSES = 3
-AHEAD = 8
+LEAD = 2
+WIDEN_AHEAD = 3
+LOAD_AHEAD = 8
+FIRST_SCALES = 4
+ORDER = (0, 2, 3, 1)
+SINGLE_STORES = 6
 
 
 def tile_galore_projected_step_d2_kernel(tc, grad_bytes, grad_scale, basis_bytes, basis_scale, mom, lr, out_0, out_1):
     nc = tc.nc
     grad_rows = grad_bytes.rearrange("(p i) k -> p i k", p=P)
+    scale_rows = grad_scale.rearrange("(p i) c -> p (i c)", p=P)
+    basis_rows = basis_bytes.rearrange("(b p) k -> p b k", p=P)
     mom_rows = mom.rearrange("(p i) n -> p i n", p=P)
     step_rows = out_0.rearrange("(p i) n -> p i n", p=P)
     new_rows = out_1.rearrange("(p i) n -> p i n", p=P)
 
     with ExitStack() as ctx:
         keep = ctx.enter_context(tc.tile_pool(name="keep", bufs=1))
-        load = ctx.enter_context(tc.tile_pool(name="load", bufs=AHEAD + 3))
+        load = ctx.enter_context(tc.tile_pool(name="load", bufs=LOAD_AHEAD + 3))
+        wides = ctx.enter_context(tc.tile_pool(name="wides", bufs=WIDEN_AHEAD + 1))
         work = ctx.enter_context(tc.tile_pool(name="work", bufs=3))
         outs = ctx.enter_context(tc.tile_pool(name="outs", bufs=5))
         psum_t = ctx.enter_context(tc.psum_pool(name="psum_t", bufs=5))
         psum_m = ctx.enter_context(tc.psum_pool(name="psum_m", bufs=3))
         ctx.enter_context(tc.manual_schedule())
 
+        basis_col = keep.tile([P, 1], F32, name="basis_col")
+        nc.gpsimd.memset(basis_col[64:128, :], 0.0)
         ident = keep.tile([P, P], F32, name="ident")
         make_identity(nc, ident[:])
 
-        basis_sc = keep.tile([P, (RANK // P) * SCALES], F32, name="basis_sc")
-        nc.sync.dma_start(out=basis_sc[:], in_=basis_scale.rearrange("b c -> (b c)").partition_broadcast(P))
-        basis_raw = {}
-        basis_rows = basis_bytes.rearrange("(b p) k -> p b k", p=P)
-        for h in (1, 0):
-            braw = keep.tile([P, RANK // P, K // 2], U8, name="braw%d" % h)
-            nc.sync.dma_start(out=braw[:], in_=basis_rows[:, :, h * (K // 2) : (h + 1) * (K // 2)])
-            basis_raw[h] = braw
-        grad_sc = keep.tile([P, TILES * SCALES], F32, name="grad_sc")
-        nc.sync.dma_start(out=grad_sc[:], in_=grad_scale.rearrange("(p i) c -> p (i c)", p=P))
+        grad_raw = {}
+        mom_raw = {}
 
-        graw = {}
-        momt = {}
+        def load_grad(first, count, pool, name):
+            g = pool.tile([P, count, K], U8, name=name)
+            nc.sync.dma_start(out=g[:], in_=grad_rows[:, first : first + count, :])
+            for t in range(count):
+                grad_raw[first + t] = g[:, t, :]
 
-        def load_grad(m):
-            if m >= TILES // 2:
-                return
-            g = load.tile([P, 2, K], U8, name="g")
-            nc.sync.dma_start(out=g[:], in_=grad_rows[:, 2 * m : 2 * m + 2, :])
-            graw[m] = g
+        def load_pair(m):
+            if m < TILES // 2:
+                load_grad(2 * m, 2, load, "g")
 
         def load_mom(m):
-            if m >= TILES // 4:
-                return
-            mo = keep.tile([P, 4, RANK], BF16, name="mo%d" % m)
-            nc.sync.dma_start(out=mo[:], in_=mom_rows[:, 4 * m : 4 * m + 4, :])
-            momt[m] = mo
+            if m < TILES // 4:
+                mo = keep.tile([P, 4, RANK], BF16, name="mo%d" % m)
+                nc.sync.dma_start(out=mo[:], in_=mom_rows[:, 4 * m : 4 * m + 4, :])
+                for t in range(4):
+                    mom_raw[4 * m + t] = mo[:, t, :]
 
-        load_grad(0)
+        sc_first = keep.tile([P, FIRST_SCALES * SCALES], F32, name="sc_first")
+        nc.sync.dma_start(out=sc_first[:], in_=scale_rows[:, 0 : FIRST_SCALES * SCALES])
+        load_grad(0, 1, keep, "g0")
+        nc.sync.dma_start(out=basis_col[0:64, :], in_=basis_scale.rearrange("b (c o) -> (b c) o", o=1))
+        load_grad(1, 1, keep, "g1")
+        basis_raw = {}
+        for h in range(2):
+            braw = keep.tile([P, ROW_TILES, K // 2], U8, name="braw%d" % h)
+            nc.sync.dma_start(out=braw[:], in_=basis_rows[:, :, h * (K // 2) : (h + 1) * (K // 2)])
+            basis_raw[h] = braw
+        load_pair(1)
+        sc_rest = keep.tile([P, (TILES - FIRST_SCALES) * SCALES], F32, name="sc_rest")
+        nc.sync.dma_start(out=sc_rest[:], in_=scale_rows[:, FIRST_SCALES * SCALES :])
+        load_pair(2)
+        load_mom(0)
         lr_raw = keep.tile([P, TILES], BF16, name="lr_raw")
         nc.sync.dma_start(out=lr_raw[:], in_=lr.rearrange("(p i) -> p i", p=P))
-        load_mom(0)
-        for m in range(1, AHEAD):
-            load_grad(m)
+        for m in range(3, LOAD_AHEAD):
+            load_pair(m)
         load_mom(1)
 
         dummy = keep.tile([P, 1], F32, name="dummy")
         nc.scalar.activation(out=dummy[:], in_=ident[:, 0:1], func=COPY)
 
-        def widen_v(dst, src, sc):
-            for q in range(4):
-                nc.vector.tensor_scalar(
-                    out=dst.rearrange("p (u b j) -> p b u j", u=2, j=16)[:, 4 * q : 4 * q + 4],
-                    in0=src[:, 128 * q : 128 * q + 128].bitcast(FP8).rearrange("p (b u j) -> p b u j", u=2, j=16),
-                    scalar1=sc[:, q : q + 1],
-                    scalar2=None,
-                    op0=MULT,
-                )
-
-        def widen_s(dst, src, sc):
-            for q in range(4):
-                nc.scalar.activation(out=dst[:, 128 * q : 128 * q + 128], in_=src[:, 128 * q : 128 * q + 128].bitcast(FP8), func=COPY, scale=sc[:, q : q + 1])
-
-        def words_of(wide, g):
-            w = wide.bitcast(F32)
-            if g < V_PASSES:
-                return w[:, 0:128], w[:, 128:256]
-            return w[:, 0:256:2], w[:, 1:256:2]
-
-        nb = RANK // P
-        bwide = {}
-        for g in range(PASSES):
-            bw = keep.tile([P, nb, 512], BF16, name="bw%d" % g, align_bytes=64)
-            bwide[g] = bw
-        bgroup = {}
-        for g in range(PASSES):
-            bg = keep.tile([P, RANK * 4], BF16, name="bg%d" % g, align_bytes=64)
-            bgroup[g] = bg
+        basis_sc = keep.tile([P, ROW_TILES * SCALES], F32, name="basis_sc")
+        lr_f = keep.tile([P, TILES], F32, name="lr_f")
         bcodes = keep.tile([P, PASSES, RANK], U32, name="bcodes", align_bytes=64)
         bscales = keep.tile([P, PASSES, RANK], U8, name="bscales", align_bytes=64)
 
-        def basis_widen(g):
-            for b in range(nb):
-                src = basis_raw[g // 2][:, b, 512 * (g % 2) : 512 * (g % 2) + 512]
-                sc = basis_sc[:, SCALES * b + 4 * g : SCALES * b + 4 * g + 4]
-                (widen_v if g < V_PASSES else widen_s)(bwide[g][:, b, :], src, sc)
+        def spread_basis_scales():
+            xt = psum_t.tile([P, 2, 2, P], F32, name="xt")
+            nc.tensor.transpose(xt[:, 0, 0, :], basis_col[:, 0:1].to_broadcast([P, P]), ident[:])
+            return xt[:, 0, 0, 0 : ROW_TILES * SCALES]
 
-        bbank = {}
+        units = [("grad", i) for i in range(LEAD)] + [("basis", g) for g in range(PASSES)] + [("grad", i) for i in range(LEAD, TILES)]
+        UNITS = len(units)
 
-        def basis_turn(g):
-            for h in range(2):
-                xt = psum_t.tile([P, 2, 2, P], F32, name="xt")
-                for b in range(2):
-                    for u, w in enumerate(words_of(bwide[g][:, 2 * h + b, :], g)):
-                        nc.tensor.transpose(xt[:, b, u, :], w, ident[:])
-                bbank[g, h] = xt
+        def slab(s, a):
+            kind, n = units[s]
+            if kind == "basis":
+                g = ORDER[n]
+                return basis_raw[g // 2][:, a, 512 * (g % 2) : 512 * (g % 2) + 512], basis_sc[:, SCALES * a + 4 * g : SCALES * a + 4 * g + 4]
+            sc, first = (sc_first, 0) if n < FIRST_SCALES else (sc_rest, FIRST_SCALES)
+            g = ORDER[a]
+            c = SCALES * (n - first) + 4 * g
+            return grad_raw[n][:, 512 * g : 512 * g + 512], sc[:, c : c + 4]
 
-        def basis_out(g, copy):
-            for h in range(2):
-                copy(
-                    out=bgroup[g][:, 1024 * h : 1024 * h + 1024].bitcast(F32).rearrange("p (b r u) -> p b r u", b=2, u=2),
-                    in_=bbank[g, h][:].rearrange("p b u r -> p b r u"),
-                )
-
-        def basis_quant(g):
-            nc.vector.quantize_mx(out=bcodes[:, g, :].bitcast(FP8X4), scales=bscales[:, g, :], in_=bgroup[g][:])
+        slabs = [(s, a) for s in range(UNITS) for a in range(4)]
+        for_scalar = [(s, a) for s, a in slabs if (a if units[s][0] == "grad" else units[s][1]) == PASSES - 1]
+        for_vector = [x for x in slabs if x not in for_scalar]
 
         wide = {}
         bank = {}
@@ -148,131 +132,148 @@ def tile_galore_projected_step_d2_kernel(tc, grad_bytes, grad_scale, basis_bytes
         acc = {}
         new = {}
         step = {}
-        lr_f = keep.tile([P, TILES], F32, name="lr_f")
 
-        def wv(i):
-            if i >= TILES:
-                return
-            wide_v = work.tile([P, V_PASSES, 512], BF16, name="wide_v", align_bytes=64)
-            for g in range(V_PASSES):
-                widen_v(wide_v[:, g, :], graw[i // 2][:, i % 2, 512 * g : 512 * g + 512], grad_sc[:, SCALES * i + 4 * g : SCALES * i + 4 * g + 4])
-            for g in range(V_PASSES):
-                wide[i, g] = wide_v[:, g, :]
+        def widen_v(n):
+            for s, a in for_vector[3 * n : 3 * n + 3]:
+                src, sc = slab(s, a)
+                dst = wides.tile([P, 512], BF16, name="wv", align_bytes=64, bufs=3 * WIDEN_AHEAD + 3)
+                for q in range(4):
+                    nc.vector.tensor_scalar(
+                        out=dst[:].rearrange("p (u b j) -> p b u j", u=2, j=16)[:, 4 * q : 4 * q + 4],
+                        in0=src[:, 128 * q : 128 * q + 128].bitcast(FP8).rearrange("p (b u j) -> p b u j", u=2, j=16),
+                        scalar1=sc[:, q : q + 1],
+                        scalar2=None,
+                        op0=MULT,
+                    )
+                w = dst[:].bitcast(F32)
+                wide[s, a] = (w[:, 0:128], w[:, 128:256])
 
-        def ws(i):
-            if i >= TILES:
-                return
-            wide_s = work.tile([P, 512], BF16, name="wide_s", align_bytes=64)
-            g = V_PASSES
-            widen_s(wide_s[:], graw[i // 2][:, i % 2, 512 * g : 512 * g + 512], grad_sc[:, SCALES * i + 4 * g : SCALES * i + 4 * g + 4])
-            wide[i, g] = wide_s[:]
+        def widen_s(n):
+            s, a = for_scalar[n]
+            src, sc = slab(s, a)
+            dst = wides.tile([P, 512], BF16, name="ws", align_bytes=64, bufs=WIDEN_AHEAD + 3)
+            for q in range(4):
+                nc.scalar.activation(out=dst[:, 128 * q : 128 * q + 128], in_=src[:, 128 * q : 128 * q + 128].bitcast(FP8), func=COPY, scale=sc[:, q : q + 1])
+            w = dst[:].bitcast(F32)
+            wide[s, a] = (w[:, 0:256:2], w[:, 1:256:2])
 
-        def turn(i):
+        def turn(s):
             for h in range(2):
                 xt = psum_t.tile([P, 2, 2, P], F32, name="xt")
-                for gg in range(2):
-                    for u, w in enumerate(words_of(wide[i, 2 * h + gg], 2 * h + gg)):
-                        nc.tensor.transpose(xt[:, gg, u, :], w, ident[:])
-                bank[i, h] = xt
+                for a in range(2):
+                    for u in range(2):
+                        nc.tensor.transpose(xt[:, a, u, :], wide[s, 2 * h + a][u], ident[:])
+                bank[s, h] = xt
 
-        def out_of_psum(i):
-            grp = work.tile([P, K], BF16, name="grp", align_bytes=64)
-            for h in range(2):
-                nc.scalar.copy(
-                    out=grp[:, 1024 * h : 1024 * h + 1024].bitcast(F32).rearrange("p (g r u) -> p g r u", g=2, u=2),
-                    in_=bank[i, h][:].rearrange("p g u r -> p g r u"),
-                )
-            group[i] = grp
+        def out_of_psum(s, h, copy):
+            if h == 0:
+                grp = work.tile([P, K], BF16, name="grp", align_bytes=64)
+                group[s] = grp
+            copy(
+                out=group[s][:, 1024 * h : 1024 * h + 1024].bitcast(F32).rearrange("p (a r u) -> p a r u", a=2, u=2),
+                in_=bank[s, h][:].rearrange("p a u r -> p a r u"),
+            )
 
-        def quant(i):
+        def quant(s):
+            kind, n = units[s]
+            if kind == "basis":
+                nc.vector.quantize_mx(out=bcodes[:, n, :].bitcast(FP8X4), scales=bscales[:, n, :], in_=group[s][:])
+                return
             cod = work.tile([P, PASSES * P], U32, name="cod", align_bytes=64)
             scl = work.tile([P, PASSES * P], U8, name="scl", align_bytes=64)
-            nc.vector.quantize_mx(out=cod[:].bitcast(FP8X4), scales=scl[:], in_=group[i][:])
-            codes[i] = (cod, scl)
+            nc.vector.quantize_mx(out=cod[:].bitcast(FP8X4), scales=scl[:], in_=group[s][:])
+            codes[n] = (cod, scl)
 
-        def mm(i):
-            a = psum_m.tile([P, RANK], F32, name="a")
-            cod, scl = codes[i]
-            for g in range(PASSES):
-                nc.tensor.matmul_mx(
-                    out=a[:],
-                    lhsT=cod[:, P * g : P * g + P].bitcast(FP8X4),
-                    lhsT_scale=scl[:, P * g : P * g + P],
-                    rhs=bcodes[:, g, :].bitcast(FP8X4),
-                    rhs_scale=bscales[:, g, :],
-                    start=(g == 0),
-                    stop=(g == PASSES - 1),
-                )
-            acc[i] = a
-
-        def halves(i):
+        def pieces(i):
             return [slice(0, 256), slice(256, 512)] if i == TILES - 1 else [slice(0, 512)]
 
-        def momentum(i):
-            if i % 2 == 0:
+        def mm(i, g, c):
+            if g == 0:
+                a = psum_m.tile([P, c.stop - c.start], F32, name="a")
+                acc[i, c.start] = a
+            cod, scl = codes[i]
+            nc.tensor.matmul_mx(
+                out=acc[i, c.start][:],
+                lhsT=cod[:, P * g : P * g + P].bitcast(FP8X4),
+                lhsT_scale=scl[:, P * g : P * g + P],
+                rhs=bcodes[:, g, c].bitcast(FP8X4),
+                rhs_scale=bscales[:, g, c],
+                start=(g == 0),
+                stop=(g == PASSES - 1),
+            )
+
+        def multiply(s):
+            kind, n = units[s]
+            if kind == "basis":
+                for i in range(LEAD):
+                    mm(i, n, slice(0, RANK))
+            elif n >= LEAD:
+                for c in pieces(n):
+                    for g in range(PASSES):
+                        mm(n, g, c)
+
+        def store(i, c, pairs, rows):
+            m = i // 2
+            if i >= TILES - SINGLE_STORES:
+                nc.sync.dma_start(out=rows[:, i, c], in_=pairs[m][:, i % 2, c])
+            elif i % 2 == 1:
+                nc.sync.dma_start(out=rows[:, 2 * m : 2 * m + 2, :], in_=pairs[m][:])
+
+        def momentum(i, c):
+            if i // 2 not in new:
                 nw = outs.tile([P, 2, RANK], F32, name="nw")
                 new[i // 2] = nw
-            for c in halves(i):
-                nc.vector.scalar_tensor_tensor(
-                    out=new[i // 2][:, i % 2, c], in0=momt[i // 4][:, i % 4, c], scalar=BETA, in1=acc[i][:, c], op0=MULT, op1=ADD)
+            nc.vector.scalar_tensor_tensor(out=new[i // 2][:, i % 2, c], in0=mom_raw[i][:, c], scalar=BETA, in1=acc[i, c.start][:], op0=MULT, op1=ADD)
+            store(i, c, new, new_rows)
 
-        def stepped(i):
-            if i % 2 == 0:
+        def stepped(i, c=slice(0, RANK)):
+            if i // 2 not in step:
                 sp = outs.tile([P, 2, RANK], F32, name="sp")
                 step[i // 2] = sp
-            for c in halves(i):
-                nc.scalar.activation(out=step[i // 2][:, i % 2, c], in_=new[i // 2][:, i % 2, c], func=COPY, scale=lr_f[:, i : i + 1])
+            nc.scalar.activation(out=step[i // 2][:, i % 2, c], in_=new[i // 2][:, i % 2, c], func=COPY, scale=lr_f[:, i : i + 1])
+            store(i, c, step, step_rows)
 
-        def store(i):
-            m = i // 2
-            if m == TILES // 2 - 1:
-                for c in halves(i):
-                    nc.sync.dma_start(out=new_rows[:, i, c], in_=new[m][:, i % 2, c])
-                    nc.sync.dma_start(out=step_rows[:, i, c], in_=step[m][:, i % 2, c])
-            elif i % 2 == 1:
-                nc.sync.dma_start(out=new_rows[:, 2 * m : 2 * m + 2, :], in_=new[m][:])
-                nc.sync.dma_start(out=step_rows[:, 2 * m : 2 * m + 2, :], in_=step[m][:])
+        def finished(s):
+            if not 0 <= s < UNITS:
+                return []
+            kind, n = units[s]
+            if kind == "basis":
+                return list(range(LEAD)) if n == PASSES - 1 else []
+            return [n] if n >= LEAD else []
 
-        basis_widen(2)
-        basis_widen(3)
-        basis_turn(2)
-        basis_widen(0)
-        basis_turn(0)
-        basis_out(2, nc.scalar.copy)
-        basis_turn(3)
-        basis_widen(1)
-        basis_turn(1)
-        basis_quant(2)
-        basis_out(0, nc.scalar.copy)
-        basis_out(1, nc.vector.tensor_copy)
-        basis_out(3, nc.scalar.copy)
-        ws(0)
-        wv(0)
-        basis_quant(0)
+        spread = spread_basis_scales()
+        for s in range(WIDEN_AHEAD):
+            if s == LEAD:
+                nc.vector.tensor_copy(out=basis_sc[:], in_=spread)
+            widen_v(s)
+            widen_s(s)
         turn(0)
-        basis_quant(1)
-        ws(1)
-        wv(1)
-        basis_quant(3)
-        nc.vector.tensor_copy(out=lr_f[:], in_=lr_raw[:])
 
-        for j in range(TILES + 3):
-            if j % 2 == 0:
-                load_grad(j // 2 + AHEAD)
-            if j % 4 == 2:
+        for s in range(UNITS + 2):
+            j = s - PASSES
+            if j >= 0 and j % 2 == 0:
+                load_pair(j // 2 + LOAD_AHEAD)
+            if j >= 0 and j % 4 == 2:
                 load_mom(j // 4 + 2)
-            if j < TILES:
-                out_of_psum(j)
-            wv(j + 2)
-            ws(j + 2)
-            if j + 1 < TILES:
-                turn(j + 1)
-            if 2 <= j < TILES + 2:
-                momentum(j - 2)
-            if j < TILES:
-                quant(j)
-            if 1 <= j <= TILES:
-                mm(j - 1)
-            if j >= 3:
-                stepped(j - 3)
-                store(j - 3)
+            ahead = s + WIDEN_AHEAD
+            if s < UNITS:
+                out_of_psum(s, 0, nc.scalar.copy)
+                out_of_psum(s, 1, nc.scalar.copy if ahead < UNITS else nc.vector.tensor_copy)
+            if ahead < UNITS:
+                widen_v(ahead)
+                widen_s(ahead)
+            if s + 1 < UNITS:
+                turn(s + 1)
+            if s == LEAD + PASSES:
+                nc.vector.tensor_copy(out=lr_f[:], in_=lr_raw[:])
+            for i in finished(s - 3):
+                stepped(i)
+            for i in finished(s - 2):
+                for c in pieces(i):
+                    momentum(i, c)
+                    if i == TILES - 1:
+                        stepped(i, c)
+            if s < UNITS:
+                quant(s)
+            if 1 <= s <= UNITS:
+                multiply(s - 1)

@@ -26,6 +26,7 @@ LEAD = 2
 WIDEN_AHEAD = 3
 LOAD_AHEAD = 8
 FIRST_SCALES = 4
+HELP_EVERY = 3
 ORDER = (0, 2, 3, 1)
 SINGLE_STORES = 6
 
@@ -153,7 +154,11 @@ def tile_galore_projected_step_d2_kernel(tc, grad_bytes, grad_scale, basis_bytes
             src, sc = slab(s, a)
             dst = wides.tile([P, 512], BF16, name="ws", align_bytes=64, bufs=WIDEN_AHEAD + 3)
             for q in range(4):
-                nc.scalar.activation(out=dst[:, 128 * q : 128 * q + 128], in_=src[:, 128 * q : 128 * q + 128].bitcast(FP8), func=COPY, scale=sc[:, q : q + 1])
+                out, codes_in = dst[:, 128 * q : 128 * q + 128], src[:, 128 * q : 128 * q + 128].bitcast(FP8)
+                if q == 0 and n % HELP_EVERY == HELP_EVERY - 1:
+                    nc.vector.tensor_scalar(out=out, in0=codes_in, scalar1=sc[:, q : q + 1], scalar2=None, op0=MULT)
+                else:
+                    nc.scalar.activation(out=out, in_=codes_in, func=COPY, scale=sc[:, q : q + 1])
             w = dst[:].bitcast(F32)
             wide[s, a] = (w[:, 0:256:2], w[:, 1:256:2])
 
@@ -243,10 +248,10 @@ def tile_galore_projected_step_d2_kernel(tc, grad_bytes, grad_scale, basis_bytes
 
         spread = spread_basis_scales()
         for s in range(WIDEN_AHEAD):
-            if s == LEAD:
-                nc.vector.tensor_copy(out=basis_sc[:], in_=spread)
             widen_v(s)
             widen_s(s)
+            if s == 0:
+                nc.scalar.copy(out=basis_sc[:], in_=spread)
         turn(0)
 
         for s in range(UNITS + 2):

@@ -26,7 +26,8 @@ LEAD = 2
 WIDEN_AHEAD = 3
 LOAD_AHEAD = 8
 FIRST_SCALES = 4
-HELP_EVERY = 3
+GPSIMD_PAIRS = 12
+SHIFT = 2
 ORDER = (0, 2, 3, 1)
 SINGLE_STORES = 6
 
@@ -42,7 +43,6 @@ def tile_galore_projected_step_d2_kernel(tc, grad_bytes, grad_scale, basis_bytes
 
     with ExitStack() as ctx:
         keep = ctx.enter_context(tc.tile_pool(name="keep", bufs=1))
-        load = ctx.enter_context(tc.tile_pool(name="load", bufs=LOAD_AHEAD + 3))
         wides = ctx.enter_context(tc.tile_pool(name="wides", bufs=WIDEN_AHEAD + 1))
         work = ctx.enter_context(tc.tile_pool(name="work", bufs=3))
         outs = ctx.enter_context(tc.tile_pool(name="outs", bufs=5))
@@ -58,15 +58,15 @@ def tile_galore_projected_step_d2_kernel(tc, grad_bytes, grad_scale, basis_bytes
         grad_raw = {}
         mom_raw = {}
 
-        def load_grad(first, count, pool, name):
-            g = pool.tile([P, count, K], U8, name=name)
+        def load_grad(first, count):
+            g = keep.tile([P, count, K], U8, name="g%d" % first, tag="slot%d" % first)
             nc.sync.dma_start(out=g[:], in_=grad_rows[:, first : first + count, :])
             for t in range(count):
                 grad_raw[first + t] = g[:, t, :]
 
         def load_pair(m):
-            if m < TILES // 2:
-                load_grad(2 * m, 2, load, "g")
+            if 2 * m + 1 < TILES:
+                load_grad(2 * m + 1, min(2, TILES - 2 * m - 1))
 
         def load_mom(m):
             if m < TILES // 4:
@@ -77,14 +77,15 @@ def tile_galore_projected_step_d2_kernel(tc, grad_bytes, grad_scale, basis_bytes
 
         sc_first = keep.tile([P, FIRST_SCALES * SCALES], F32, name="sc_first")
         nc.sync.dma_start(out=sc_first[:], in_=scale_rows[:, 0 : FIRST_SCALES * SCALES])
-        load_grad(0, 1, keep, "g0")
+        load_grad(0, 1)
         nc.sync.dma_start(out=basis_col[0:64, :], in_=basis_scale.rearrange("b (c o) -> (b c) o", o=1))
-        load_grad(1, 1, keep, "g1")
+        load_grad(1, 1)
         basis_raw = {}
         for h in range(2):
             braw = keep.tile([P, ROW_TILES, K // 2], U8, name="braw%d" % h)
             nc.sync.dma_start(out=braw[:], in_=basis_rows[:, :, h * (K // 2) : (h + 1) * (K // 2)])
             basis_raw[h] = braw
+        load_grad(2, 1)
         load_pair(1)
         sc_rest = keep.tile([P, (TILES - FIRST_SCALES) * SCALES], F32, name="sc_rest")
         nc.sync.dma_start(out=sc_rest[:], in_=scale_rows[:, FIRST_SCALES * SCALES :])
@@ -127,6 +128,8 @@ def tile_galore_projected_step_d2_kernel(tc, grad_bytes, grad_scale, basis_bytes
         for_vector = [x for x in slabs if x not in for_scalar]
 
         wide = {}
+        casts = {}
+        scaled = {}
         bank = {}
         group = {}
         codes = {}
@@ -134,31 +137,37 @@ def tile_galore_projected_step_d2_kernel(tc, grad_bytes, grad_scale, basis_bytes
         new = {}
         step = {}
 
+        blocks = [(s, a, q) for s, a in for_vector for q in range(4)]
+
+        def cast(s):
+            plain = wides.tile([P, 512], BF16, name="plain", align_bytes=64, bufs=3)
+            nc.scalar.copy(out=plain[:], in_=slab(s, 0)[0].bitcast(FP8))
+            casts[s] = plain
+
         def widen_v(n):
-            for s, a in for_vector[3 * n : 3 * n + 3]:
+            for s, a, q in blocks[12 * n + SHIFT if n else 0 : 12 * n + 12 + SHIFT]:
                 src, sc = slab(s, a)
-                dst = wides.tile([P, 512], BF16, name="wv", align_bytes=64, bufs=3 * WIDEN_AHEAD + 3)
-                for q in range(4):
-                    nc.vector.tensor_scalar(
-                        out=dst[:].rearrange("p (u b j) -> p b u j", u=2, j=16)[:, 4 * q : 4 * q + 4],
-                        in0=src[:, 128 * q : 128 * q + 128].bitcast(FP8).rearrange("p (b u j) -> p b u j", u=2, j=16),
-                        scalar1=sc[:, q : q + 1],
-                        scalar2=None,
-                        op0=MULT,
-                    )
-                w = dst[:].bitcast(F32)
-                wide[s, a] = (w[:, 0:128], w[:, 128:256])
+                values = casts[s][:] if a == 0 and s in casts else src.bitcast(FP8)
+                if q == 0:
+                    dst = wides.tile([P, 512], BF16, name="wv", align_bytes=64, bufs=3 * WIDEN_AHEAD + 4)
+                    w = dst[:].bitcast(F32)
+                    wide[s, a] = (w[:, 0:128], w[:, 128:256])
+                    scaled[s, a] = dst
+                nc.vector.tensor_scalar(
+                    out=scaled[s, a][:].rearrange("p (u b j) -> p b u j", u=2, j=16)[:, 4 * q : 4 * q + 4],
+                    in0=values[:, 128 * q : 128 * q + 128].rearrange("p (b u j) -> p b u j", u=2, j=16),
+                    scalar1=sc[:, q : q + 1],
+                    scalar2=None,
+                    op0=MULT,
+                )
 
         def widen_s(n):
             s, a = for_scalar[n]
             src, sc = slab(s, a)
-            dst = wides.tile([P, 512], BF16, name="ws", align_bytes=64, bufs=WIDEN_AHEAD + 3)
+            dst = wides.tile([P, 512], BF16, name="ws", align_bytes=64, bufs=WIDEN_AHEAD + 4)
             for q in range(4):
                 out, codes_in = dst[:, 128 * q : 128 * q + 128], src[:, 128 * q : 128 * q + 128].bitcast(FP8)
-                if q == 0 and n % HELP_EVERY == HELP_EVERY - 1:
-                    nc.vector.tensor_scalar(out=out, in0=codes_in, scalar1=sc[:, q : q + 1], scalar2=None, op0=MULT)
-                else:
-                    nc.scalar.activation(out=out, in_=codes_in, func=COPY, scale=sc[:, q : q + 1])
+                nc.scalar.activation(out=out, in_=codes_in, func=COPY, scale=sc[:, q : q + 1])
             w = dst[:].bitcast(F32)
             wide[s, a] = (w[:, 0:256:2], w[:, 1:256:2])
 
@@ -232,19 +241,25 @@ def tile_galore_projected_step_d2_kernel(tc, grad_bytes, grad_scale, basis_bytes
             store(i, c, new, new_rows)
 
         def stepped(i, c=slice(0, RANK)):
-            if i // 2 not in step:
-                sp = outs.tile([P, 2, RANK], F32, name="sp")
-                step[i // 2] = sp
-            nc.scalar.activation(out=step[i // 2][:, i % 2, c], in_=new[i // 2][:, i % 2, c], func=COPY, scale=lr_f[:, i : i + 1])
+            m = i // 2
+            if m not in step:
+                if m < GPSIMD_PAIRS:
+                    sp = keep.tile([P, 2, RANK], F32, name="sp%d" % m, tag="slot%d" % (2 * m + 7))
+                else:
+                    sp = outs.tile([P, 2, RANK], F32, name="sp")
+                step[m] = sp
+            if m < GPSIMD_PAIRS and i % 2 == 0:
+                nc.gpsimd.tensor_scalar(out=step[m][:, 0, c], in0=new[m][:, 0, c], scalar1=lr_f[:, i : i + 1], scalar2=0.0, op0=MULT, op1=ADD)
+            else:
+                nc.scalar.activation(out=step[m][:, i % 2, c], in_=new[m][:, i % 2, c], func=COPY, scale=lr_f[:, i : i + 1])
             store(i, c, step, step_rows)
 
-        def finished(s):
-            if not 0 <= s < UNITS:
-                return []
-            kind, n = units[s]
-            if kind == "basis":
-                return list(range(LEAD)) if n == PASSES - 1 else []
-            return [n] if n >= LEAD else []
+        PAIRED = 2 * GPSIMD_PAIRS + 2
+        momentum_at = {}
+        step_at = {}
+        for i in range(TILES):
+            momentum_at.setdefault(i + 7 - i % 2 if i < PAIRED else i + 6, []).append(i)
+            step_at.setdefault(i + 9 if i < 2 * GPSIMD_PAIRS else i + 8 - i % 2 if i < PAIRED else i + 7, []).append(i)
 
         spread = spread_basis_scales()
         for s in range(WIDEN_AHEAD):
@@ -253,6 +268,7 @@ def tile_galore_projected_step_d2_kernel(tc, grad_bytes, grad_scale, basis_bytes
             if s == 0:
                 nc.scalar.copy(out=basis_sc[:], in_=spread)
         turn(0)
+        widen_s(WIDEN_AHEAD)
 
         for s in range(UNITS + 2):
             j = s - PASSES
@@ -266,14 +282,17 @@ def tile_galore_projected_step_d2_kernel(tc, grad_bytes, grad_scale, basis_bytes
                 out_of_psum(s, 1, nc.scalar.copy if ahead < UNITS else nc.vector.tensor_copy)
             if ahead < UNITS:
                 widen_v(ahead)
-                widen_s(ahead)
+            if ahead + 1 < UNITS:
+                widen_s(ahead + 1)
+            if s >= 9 and s % 2 == 1 and ahead + 2 < UNITS:
+                cast(ahead + 2)
             if s + 1 < UNITS:
                 turn(s + 1)
             if s == LEAD + PASSES:
                 nc.vector.tensor_copy(out=lr_f[:], in_=lr_raw[:])
-            for i in finished(s - 3):
+            for i in step_at.get(s, []):
                 stepped(i)
-            for i in finished(s - 2):
+            for i in momentum_at.get(s, []):
                 for c in pieces(i):
                     momentum(i, c)
                     if i == TILES - 1:

@@ -23,13 +23,15 @@ ADD = mybir.AluOpType.add
 COPY = mybir.ActivationFunctionType.Copy
 
 LEAD = 2
-WIDEN_AHEAD = 3
+WIDEN_AHEAD = 2
 LOAD_AHEAD = 8
 FIRST_SCALES = 4
 GPSIMD_PAIRS = 12
 SHIFT = 2
-ORDER = (0, 2, 3, 1)
+ORDER = (0, 1, 2, 3)
 SINGLE_STORES = 6
+LAST_PIECES = (slice(0, 512),)
+CAST_FROM = 9
 
 
 def tile_galore_projected_step_d2_kernel(tc, grad_bytes, grad_scale, basis_bytes, basis_scale, mom, lr, out_0, out_1):
@@ -65,8 +67,8 @@ def tile_galore_projected_step_d2_kernel(tc, grad_bytes, grad_scale, basis_bytes
                 grad_raw[first + t] = g[:, t, :]
 
         def load_pair(m):
-            if 2 * m + 1 < TILES:
-                load_grad(2 * m + 1, min(2, TILES - 2 * m - 1))
+            if m < TILES // 2:
+                load_grad(2 * m, 2)
 
         def load_mom(m):
             if m < TILES // 4:
@@ -77,15 +79,18 @@ def tile_galore_projected_step_d2_kernel(tc, grad_bytes, grad_scale, basis_bytes
 
         sc_first = keep.tile([P, FIRST_SCALES * SCALES], F32, name="sc_first")
         nc.sync.dma_start(out=sc_first[:], in_=scale_rows[:, 0 : FIRST_SCALES * SCALES])
-        load_grad(0, 1)
+        first_halves = []
+        for h in range(2):
+            half = keep.tile([P, K // 2], U8, name="g0_%d" % h)
+            nc.sync.dma_start(out=half[:], in_=grad_rows[:, 0, h * (K // 2) : (h + 1) * (K // 2)])
+            first_halves.append(half)
         nc.sync.dma_start(out=basis_col[0:64, :], in_=basis_scale.rearrange("b (c o) -> (b c) o", o=1))
         load_grad(1, 1)
         basis_raw = {}
-        for h in range(2):
-            braw = keep.tile([P, ROW_TILES, K // 2], U8, name="braw%d" % h)
-            nc.sync.dma_start(out=braw[:], in_=basis_rows[:, :, h * (K // 2) : (h + 1) * (K // 2)])
-            basis_raw[h] = braw
-        load_grad(2, 1)
+        for b in range(ROW_TILES):
+            braw = keep.tile([P, K], U8, name="braw%d" % b)
+            nc.sync.dma_start(out=braw[:], in_=basis_rows[:, b, :])
+            basis_raw[b] = braw
         load_pair(1)
         sc_rest = keep.tile([P, (TILES - FIRST_SCALES) * SCALES], F32, name="sc_rest")
         nc.sync.dma_start(out=sc_rest[:], in_=scale_rows[:, FIRST_SCALES * SCALES :])
@@ -110,22 +115,19 @@ def tile_galore_projected_step_d2_kernel(tc, grad_bytes, grad_scale, basis_bytes
             nc.tensor.transpose(xt[:, 0, 0, :], basis_col[:, 0:1].to_broadcast([P, P]), ident[:])
             return xt[:, 0, 0, 0 : ROW_TILES * SCALES]
 
-        units = [("grad", i) for i in range(LEAD)] + [("basis", g) for g in range(PASSES)] + [("grad", i) for i in range(LEAD, TILES)]
+        units = [("grad", i) for i in range(LEAD)] + [("basis", b) for b in range(ROW_TILES)] + [("grad", i) for i in range(LEAD, TILES)]
         UNITS = len(units)
 
         def slab(s, a):
             kind, n = units[s]
-            if kind == "basis":
-                g = ORDER[n]
-                return basis_raw[g // 2][:, a, 512 * (g % 2) : 512 * (g % 2) + 512], basis_sc[:, SCALES * a + 4 * g : SCALES * a + 4 * g + 4]
-            sc, first = (sc_first, 0) if n < FIRST_SCALES else (sc_rest, FIRST_SCALES)
             g = ORDER[a]
+            if kind == "basis":
+                return basis_raw[n][:, 512 * g : 512 * g + 512], basis_sc[:, SCALES * n + 4 * g : SCALES * n + 4 * g + 4]
+            sc, first = (sc_first, 0) if n < FIRST_SCALES else (sc_rest, FIRST_SCALES)
             c = SCALES * (n - first) + 4 * g
+            if n == 0:
+                return first_halves[g // 2][:, 512 * (g % 2) : 512 * (g % 2) + 512], sc[:, c : c + 4]
             return grad_raw[n][:, 512 * g : 512 * g + 512], sc[:, c : c + 4]
-
-        slabs = [(s, a) for s in range(UNITS) for a in range(4)]
-        for_scalar = [(s, a) for s, a in slabs if (a if units[s][0] == "grad" else units[s][1]) == PASSES - 1]
-        for_vector = [x for x in slabs if x not in for_scalar]
 
         wide = {}
         casts = {}
@@ -137,7 +139,7 @@ def tile_galore_projected_step_d2_kernel(tc, grad_bytes, grad_scale, basis_bytes
         new = {}
         step = {}
 
-        blocks = [(s, a, q) for s, a in for_vector for q in range(4)]
+        blocks = [(s, a, q) for s in range(UNITS) for a in range(PASSES - 1) for q in range(4)]
 
         def cast(s):
             plain = wides.tile([P, 512], BF16, name="plain", align_bytes=64, bufs=3)
@@ -161,8 +163,8 @@ def tile_galore_projected_step_d2_kernel(tc, grad_bytes, grad_scale, basis_bytes
                     op0=MULT,
                 )
 
-        def widen_s(n):
-            s, a = for_scalar[n]
+        def widen_s(s):
+            a = PASSES - 1
             src, sc = slab(s, a)
             dst = wides.tile([P, 512], BF16, name="ws", align_bytes=64, bufs=WIDEN_AHEAD + 4)
             for q in range(4):
@@ -188,26 +190,29 @@ def tile_galore_projected_step_d2_kernel(tc, grad_bytes, grad_scale, basis_bytes
                 in_=bank[s, h][:].rearrange("p a u r -> p a r u"),
             )
 
-        def quant(s):
+        def quant(s, words=slice(0, PASSES * P)):
             kind, n = units[s]
             if kind == "basis":
-                nc.vector.quantize_mx(out=bcodes[:, n, :].bitcast(FP8X4), scales=bscales[:, n, :], in_=group[s][:])
+                for a in range(PASSES):
+                    nc.vector.quantize_mx(out=bcodes[:, a, P * n : P * n + P].bitcast(FP8X4), scales=bscales[:, a, P * n : P * n + P], in_=group[s][:, 512 * a : 512 * a + 512])
                 return
-            cod = work.tile([P, PASSES * P], U32, name="cod", align_bytes=64)
-            scl = work.tile([P, PASSES * P], U8, name="scl", align_bytes=64)
-            nc.vector.quantize_mx(out=cod[:].bitcast(FP8X4), scales=scl[:], in_=group[s][:])
-            codes[n] = (cod, scl)
+            if n not in codes:
+                cod = work.tile([P, PASSES * P], U32, name="cod", align_bytes=64)
+                scl = work.tile([P, PASSES * P], U8, name="scl", align_bytes=64)
+                codes[n] = (cod, scl)
+            cod, scl = codes[n]
+            nc.vector.quantize_mx(out=cod[:, words].bitcast(FP8X4), scales=scl[:, words], in_=group[s][:, 4 * words.start : 4 * words.stop])
 
         def pieces(i):
-            return [slice(0, 256), slice(256, 512)] if i == TILES - 1 else [slice(0, 512)]
+            return LAST_PIECES if i == TILES - 1 else [slice(0, RANK)]
 
         def mm(i, g, c):
-            if g == 0:
-                a = psum_m.tile([P, c.stop - c.start], F32, name="a")
-                acc[i, c.start] = a
+            if i not in acc:
+                a = psum_m.tile([P, RANK], F32, name="a")
+                acc[i] = a
             cod, scl = codes[i]
             nc.tensor.matmul_mx(
-                out=acc[i, c.start][:],
+                out=acc[i][:, c],
                 lhsT=cod[:, P * g : P * g + P].bitcast(FP8X4),
                 lhsT_scale=scl[:, P * g : P * g + P],
                 rhs=bcodes[:, g, c].bitcast(FP8X4),
@@ -220,11 +225,11 @@ def tile_galore_projected_step_d2_kernel(tc, grad_bytes, grad_scale, basis_bytes
             kind, n = units[s]
             if kind == "basis":
                 for i in range(LEAD):
-                    mm(i, n, slice(0, RANK))
-            elif n >= LEAD:
-                for c in pieces(n):
                     for g in range(PASSES):
-                        mm(n, g, c)
+                        mm(i, g, slice(P * n, P * n + P))
+            elif n >= LEAD:
+                for g in range(PASSES):
+                    mm(n, g, slice(0, RANK))
 
         def store(i, c, pairs, rows):
             m = i // 2
@@ -237,14 +242,14 @@ def tile_galore_projected_step_d2_kernel(tc, grad_bytes, grad_scale, basis_bytes
             if i // 2 not in new:
                 nw = outs.tile([P, 2, RANK], F32, name="nw")
                 new[i // 2] = nw
-            nc.vector.scalar_tensor_tensor(out=new[i // 2][:, i % 2, c], in0=mom_raw[i][:, c], scalar=BETA, in1=acc[i, c.start][:], op0=MULT, op1=ADD)
+            nc.vector.scalar_tensor_tensor(out=new[i // 2][:, i % 2, c], in0=mom_raw[i][:, c], scalar=BETA, in1=acc[i][:, c], op0=MULT, op1=ADD)
             store(i, c, new, new_rows)
 
         def stepped(i, c=slice(0, RANK)):
             m = i // 2
             if m not in step:
                 if m < GPSIMD_PAIRS:
-                    sp = keep.tile([P, 2, RANK], F32, name="sp%d" % m, tag="slot%d" % (2 * m + 7))
+                    sp = keep.tile([P, 2, RANK], F32, name="sp%d" % m, tag="slot%d" % (2 * m + 6))
                 else:
                     sp = outs.tile([P, 2, RANK], F32, name="sp")
                 step[m] = sp
@@ -262,13 +267,15 @@ def tile_galore_projected_step_d2_kernel(tc, grad_bytes, grad_scale, basis_bytes
             step_at.setdefault(i + 9 if i < 2 * GPSIMD_PAIRS else i + 8 - i % 2 if i < PAIRED else i + 7, []).append(i)
 
         spread = spread_basis_scales()
-        for s in range(WIDEN_AHEAD):
-            widen_v(s)
-            widen_s(s)
-            if s == 0:
-                nc.scalar.copy(out=basis_sc[:], in_=spread)
+        widen_v(0)
+        widen_s(0)
+        nc.scalar.copy(out=basis_sc[:], in_=spread)
         turn(0)
-        widen_s(WIDEN_AHEAD)
+        widen_v(1)
+        widen_s(1)
+        out_of_psum(0, 0, nc.scalar.copy)
+        widen_s(2)
+        out_of_psum(0, 1, nc.scalar.copy)
 
         for s in range(UNITS + 2):
             j = s - PASSES
@@ -277,19 +284,21 @@ def tile_galore_projected_step_d2_kernel(tc, grad_bytes, grad_scale, basis_bytes
             if j >= 0 and j % 4 == 2:
                 load_mom(j // 4 + 2)
             ahead = s + WIDEN_AHEAD
-            if s < UNITS:
+            if 0 < s < UNITS:
                 out_of_psum(s, 0, nc.scalar.copy)
-                out_of_psum(s, 1, nc.scalar.copy if ahead < UNITS else nc.vector.tensor_copy)
+                out_of_psum(s, 1, nc.scalar.copy)
             if ahead < UNITS:
                 widen_v(ahead)
             if ahead + 1 < UNITS:
                 widen_s(ahead + 1)
-            if s >= 9 and s % 2 == 1 and ahead + 2 < UNITS:
+            if s >= CAST_FROM and s % 2 == 1 and ahead + 2 < UNITS:
                 cast(ahead + 2)
             if s + 1 < UNITS:
                 turn(s + 1)
             if s == LEAD + PASSES:
                 nc.vector.tensor_copy(out=lr_f[:], in_=lr_raw[:])
+            if s == UNITS - 1:
+                quant(s, slice(0, 2 * P))
             for i in step_at.get(s, []):
                 stepped(i)
             for i in momentum_at.get(s, []):
@@ -298,6 +307,6 @@ def tile_galore_projected_step_d2_kernel(tc, grad_bytes, grad_scale, basis_bytes
                     if i == TILES - 1:
                         stepped(i, c)
             if s < UNITS:
-                quant(s)
+                quant(s, slice(2 * P if s == UNITS - 1 else 0, PASSES * P))
             if 1 <= s <= UNITS:
                 multiply(s - 1)

@@ -7,7 +7,7 @@ TOKENS, K, RANK = 4096, 2048, 512
 P = 128
 TILES = TOKENS // P
 PASSES = K // 512
-SCALES = K // 128
+BLOCKS = K // 128
 ROW_TILES = RANK // P
 BETA = 0.9
 FLOPS = 2 * TOKENS * K * RANK
@@ -23,15 +23,17 @@ ADD = mybir.AluOpType.add
 COPY = mybir.ActivationFunctionType.Copy
 
 LEAD = 2
-WIDEN_AHEAD = 2
+AHEAD = 2
 LOAD_AHEAD = 8
 FIRST_SCALES = 4
 GPSIMD_PAIRS = 12
-SHIFT = 2
-ORDER = (0, 1, 2, 3)
 SINGLE_STORES = 6
-LAST_PIECES = (slice(0, 512),)
-CAST_FROM = 9
+CAST_FIRST = 7
+CAST_HEAD = 9
+CAST_EVEN = 12
+CAST_ODD = 11
+CAST_TAIL = 9
+TRAILING = 3
 
 
 def tile_galore_projected_step_d2_kernel(tc, grad_bytes, grad_scale, basis_bytes, basis_scale, mom, lr, out_0, out_1):
@@ -43,9 +45,20 @@ def tile_galore_projected_step_d2_kernel(tc, grad_bytes, grad_scale, basis_bytes
     step_rows = out_0.rearrange("(p i) n -> p i n", p=P)
     new_rows = out_1.rearrange("(p i) n -> p i n", p=P)
 
+    units = [("grad", i) for i in range(LEAD)] + [("basis", b) for b in range(ROW_TILES)] + [("grad", i) for i in range(LEAD, TILES)]
+    last_unit = len(units) - 1
+
+    def cast_blocks(s):
+        if s < LEAD:
+            return CAST_FIRST
+        if s < LEAD + ROW_TILES + 4:
+            return CAST_HEAD
+        if s >= 2 * GPSIMD_PAIRS + 10:
+            return CAST_TAIL
+        return CAST_ODD if s % 2 else CAST_EVEN
+
     with ExitStack() as ctx:
         keep = ctx.enter_context(tc.tile_pool(name="keep", bufs=1))
-        wides = ctx.enter_context(tc.tile_pool(name="wides", bufs=WIDEN_AHEAD + 1))
         work = ctx.enter_context(tc.tile_pool(name="work", bufs=3))
         outs = ctx.enter_context(tc.tile_pool(name="outs", bufs=5))
         psum_t = ctx.enter_context(tc.psum_pool(name="psum_t", bufs=5))
@@ -57,14 +70,14 @@ def tile_galore_projected_step_d2_kernel(tc, grad_bytes, grad_scale, basis_bytes
         ident = keep.tile([P, P], F32, name="ident")
         make_identity(nc, ident[:])
 
-        grad_raw = {}
+        raw = {}
         mom_raw = {}
 
         def load_grad(first, count):
             g = keep.tile([P, count, K], U8, name="g%d" % first, tag="slot%d" % first)
             nc.sync.dma_start(out=g[:], in_=grad_rows[:, first : first + count, :])
             for t in range(count):
-                grad_raw[first + t] = g[:, t, :]
+                raw["grad", first + t] = g[:, t, :]
 
         def load_pair(m):
             if m < TILES // 2:
@@ -77,23 +90,18 @@ def tile_galore_projected_step_d2_kernel(tc, grad_bytes, grad_scale, basis_bytes
                 for t in range(4):
                     mom_raw[4 * m + t] = mo[:, t, :]
 
-        sc_first = keep.tile([P, FIRST_SCALES * SCALES], F32, name="sc_first")
-        nc.sync.dma_start(out=sc_first[:], in_=scale_rows[:, 0 : FIRST_SCALES * SCALES])
-        first_halves = []
-        for h in range(2):
-            half = keep.tile([P, K // 2], U8, name="g0_%d" % h)
-            nc.sync.dma_start(out=half[:], in_=grad_rows[:, 0, h * (K // 2) : (h + 1) * (K // 2)])
-            first_halves.append(half)
+        sc_first = keep.tile([P, FIRST_SCALES * BLOCKS], F32, name="sc_first")
+        nc.sync.dma_start(out=sc_first[:], in_=scale_rows[:, 0 : FIRST_SCALES * BLOCKS])
+        load_grad(0, 1)
         nc.sync.dma_start(out=basis_col[0:64, :], in_=basis_scale.rearrange("b (c o) -> (b c) o", o=1))
         load_grad(1, 1)
-        basis_raw = {}
         for b in range(ROW_TILES):
             braw = keep.tile([P, K], U8, name="braw%d" % b)
             nc.sync.dma_start(out=braw[:], in_=basis_rows[:, b, :])
-            basis_raw[b] = braw
+            raw["basis", b] = braw[:]
         load_pair(1)
-        sc_rest = keep.tile([P, (TILES - FIRST_SCALES) * SCALES], F32, name="sc_rest")
-        nc.sync.dma_start(out=sc_rest[:], in_=scale_rows[:, FIRST_SCALES * SCALES :])
+        sc_rest = keep.tile([P, (TILES - FIRST_SCALES) * BLOCKS], F32, name="sc_rest")
+        nc.sync.dma_start(out=sc_rest[:], in_=scale_rows[:, FIRST_SCALES * BLOCKS :])
         load_pair(2)
         load_mom(0)
         lr_raw = keep.tile([P, TILES], BF16, name="lr_raw")
@@ -105,33 +113,13 @@ def tile_galore_projected_step_d2_kernel(tc, grad_bytes, grad_scale, basis_bytes
         dummy = keep.tile([P, 1], F32, name="dummy")
         nc.scalar.activation(out=dummy[:], in_=ident[:, 0:1], func=COPY)
 
-        basis_sc = keep.tile([P, ROW_TILES * SCALES], F32, name="basis_sc")
+        basis_sc = keep.tile([P, ROW_TILES * BLOCKS], F32, name="basis_sc")
         lr_f = keep.tile([P, TILES], F32, name="lr_f")
         bcodes = keep.tile([P, PASSES, RANK], U32, name="bcodes", align_bytes=64)
         bscales = keep.tile([P, PASSES, RANK], U8, name="bscales", align_bytes=64)
 
-        def spread_basis_scales():
-            xt = psum_t.tile([P, 2, 2, P], F32, name="xt")
-            nc.tensor.transpose(xt[:, 0, 0, :], basis_col[:, 0:1].to_broadcast([P, P]), ident[:])
-            return xt[:, 0, 0, 0 : ROW_TILES * SCALES]
-
-        units = [("grad", i) for i in range(LEAD)] + [("basis", b) for b in range(ROW_TILES)] + [("grad", i) for i in range(LEAD, TILES)]
-        UNITS = len(units)
-
-        def slab(s, a):
-            kind, n = units[s]
-            g = ORDER[a]
-            if kind == "basis":
-                return basis_raw[n][:, 512 * g : 512 * g + 512], basis_sc[:, SCALES * n + 4 * g : SCALES * n + 4 * g + 4]
-            sc, first = (sc_first, 0) if n < FIRST_SCALES else (sc_rest, FIRST_SCALES)
-            c = SCALES * (n - first) + 4 * g
-            if n == 0:
-                return first_halves[g // 2][:, 512 * (g % 2) : 512 * (g % 2) + 512], sc[:, c : c + 4]
-            return grad_raw[n][:, 512 * g : 512 * g + 512], sc[:, c : c + 4]
-
+        plain = {}
         wide = {}
-        casts = {}
-        scaled = {}
         bank = {}
         group = {}
         codes = {}
@@ -139,62 +127,61 @@ def tile_galore_projected_step_d2_kernel(tc, grad_bytes, grad_scale, basis_bytes
         new = {}
         step = {}
 
-        blocks = [(s, a, q) for s in range(UNITS) for a in range(PASSES - 1) for q in range(4)]
+        def scale_of(s, c):
+            kind, n = units[s]
+            if kind == "basis":
+                return basis_sc[:, BLOCKS * n + c : BLOCKS * n + c + 1]
+            sc, first = (sc_first, 0) if n < FIRST_SCALES else (sc_rest, FIRST_SCALES)
+            return sc[:, BLOCKS * (n - first) + c : BLOCKS * (n - first) + c + 1]
 
         def cast(s):
-            plain = wides.tile([P, 512], BF16, name="plain", align_bytes=64, bufs=3)
-            nc.scalar.copy(out=plain[:], in_=slab(s, 0)[0].bitcast(FP8))
-            casts[s] = plain
+            width = 128 * cast_blocks(s)
+            values = work.tile([P, width], BF16, name="values", align_bytes=64)
+            nc.scalar.copy(out=values[:], in_=raw[units[s]][:, 0:width].bitcast(FP8))
+            plain[s] = values
 
-        def widen_v(n):
-            for s, a, q in blocks[12 * n + SHIFT if n else 0 : 12 * n + 12 + SHIFT]:
-                src, sc = slab(s, a)
-                values = casts[s][:] if a == 0 and s in casts else src.bitcast(FP8)
-                if q == 0:
-                    dst = wides.tile([P, 512], BF16, name="wv", align_bytes=64, bufs=3 * WIDEN_AHEAD + 4)
-                    w = dst[:].bitcast(F32)
-                    wide[s, a] = (w[:, 0:128], w[:, 128:256])
-                    scaled[s, a] = dst
+        def widen(s):
+            count = cast_blocks(s)
+            if s < LEAD:
+                order = list(range(count, BLOCKS)) + list(range(count))
+            else:
+                order = list(range(count - TRAILING)) + list(range(count, BLOCKS)) + list(range(count - TRAILING, count))
+            for g in range(PASSES):
+                dst = work.tile([P, 512], BF16, name="wide%d" % g, align_bytes=64, bufs=AHEAD + 2)
+                wide[s, g] = dst
+            for c in order:
+                src = plain[s][:, 128 * c : 128 * c + 128] if c < count else raw[units[s]][:, 128 * c : 128 * c + 128].bitcast(FP8)
                 nc.vector.tensor_scalar(
-                    out=scaled[s, a][:].rearrange("p (u b j) -> p b u j", u=2, j=16)[:, 4 * q : 4 * q + 4],
-                    in0=values[:, 128 * q : 128 * q + 128].rearrange("p (b u j) -> p b u j", u=2, j=16),
-                    scalar1=sc[:, q : q + 1],
+                    out=wide[s, c // 4][:].rearrange("p (u b j) -> p b u j", u=2, j=16)[:, 4 * (c % 4) : 4 * (c % 4) + 4],
+                    in0=src.rearrange("p (b u j) -> p b u j", u=2, j=16),
+                    scalar1=scale_of(s, c),
                     scalar2=None,
                     op0=MULT,
                 )
 
-        def widen_s(s):
-            a = PASSES - 1
-            src, sc = slab(s, a)
-            dst = wides.tile([P, 512], BF16, name="ws", align_bytes=64, bufs=WIDEN_AHEAD + 4)
-            for q in range(4):
-                out, codes_in = dst[:, 128 * q : 128 * q + 128], src[:, 128 * q : 128 * q + 128].bitcast(FP8)
-                nc.scalar.activation(out=out, in_=codes_in, func=COPY, scale=sc[:, q : q + 1])
-            w = dst[:].bitcast(F32)
-            wide[s, a] = (w[:, 0:256:2], w[:, 1:256:2])
-
         def turn(s):
-            for h in range(2):
+            for h in (1, 0) if s < LEAD else (0, 1):
                 xt = psum_t.tile([P, 2, 2, P], F32, name="xt")
                 for a in range(2):
+                    words = wide[s, 2 * h + a][:].bitcast(F32)
                     for u in range(2):
-                        nc.tensor.transpose(xt[:, a, u, :], wide[s, 2 * h + a][u], ident[:])
+                        nc.tensor.transpose(xt[:, a, u, :], words[:, P * u : P * u + P], ident[:])
                 bank[s, h] = xt
 
-        def out_of_psum(s, h, copy):
-            if h == 0:
+        def out_of_psum(s, h):
+            if s not in group:
                 grp = work.tile([P, K], BF16, name="grp", align_bytes=64)
                 group[s] = grp
-            copy(
+            nc.scalar.copy(
                 out=group[s][:, 1024 * h : 1024 * h + 1024].bitcast(F32).rearrange("p (a r u) -> p a r u", a=2, u=2),
                 in_=bank[s, h][:].rearrange("p a u r -> p a r u"),
             )
 
-        def quant(s, words=slice(0, PASSES * P)):
+        def quant(s, words):
             kind, n = units[s]
             if kind == "basis":
-                for a in range(PASSES):
-                    nc.vector.quantize_mx(out=bcodes[:, a, P * n : P * n + P].bitcast(FP8X4), scales=bscales[:, a, P * n : P * n + P], in_=group[s][:, 512 * a : 512 * a + 512])
+                for g in range(PASSES):
+                    nc.vector.quantize_mx(out=bcodes[:, g, P * n : P * n + P].bitcast(FP8X4), scales=bscales[:, g, P * n : P * n + P], in_=group[s][:, 512 * g : 512 * g + 512])
                 return
             if n not in codes:
                 cod = work.tile([P, PASSES * P], U32, name="cod", align_bytes=64)
@@ -203,110 +190,99 @@ def tile_galore_projected_step_d2_kernel(tc, grad_bytes, grad_scale, basis_bytes
             cod, scl = codes[n]
             nc.vector.quantize_mx(out=cod[:, words].bitcast(FP8X4), scales=scl[:, words], in_=group[s][:, 4 * words.start : 4 * words.stop])
 
-        def pieces(i):
-            return LAST_PIECES if i == TILES - 1 else [slice(0, RANK)]
-
-        def mm(i, g, c):
+        def product(i, cols):
             if i not in acc:
                 a = psum_m.tile([P, RANK], F32, name="a")
                 acc[i] = a
             cod, scl = codes[i]
-            nc.tensor.matmul_mx(
-                out=acc[i][:, c],
-                lhsT=cod[:, P * g : P * g + P].bitcast(FP8X4),
-                lhsT_scale=scl[:, P * g : P * g + P],
-                rhs=bcodes[:, g, c].bitcast(FP8X4),
-                rhs_scale=bscales[:, g, c],
-                start=(g == 0),
-                stop=(g == PASSES - 1),
-            )
+            for g in range(PASSES):
+                nc.tensor.matmul_mx(
+                    out=acc[i][:, cols],
+                    lhsT=cod[:, P * g : P * g + P].bitcast(FP8X4),
+                    lhsT_scale=scl[:, P * g : P * g + P],
+                    rhs=bcodes[:, g, cols].bitcast(FP8X4),
+                    rhs_scale=bscales[:, g, cols],
+                    start=(g == 0),
+                    stop=(g == PASSES - 1),
+                )
 
         def multiply(s):
             kind, n = units[s]
             if kind == "basis":
                 for i in range(LEAD):
-                    for g in range(PASSES):
-                        mm(i, g, slice(P * n, P * n + P))
+                    product(i, slice(P * n, P * n + P))
             elif n >= LEAD:
-                for g in range(PASSES):
-                    mm(n, g, slice(0, RANK))
+                product(n, slice(0, RANK))
 
-        def store(i, c, pairs, rows):
+        def store(i, pairs, rows):
             m = i // 2
             if i >= TILES - SINGLE_STORES:
-                nc.sync.dma_start(out=rows[:, i, c], in_=pairs[m][:, i % 2, c])
+                nc.sync.dma_start(out=rows[:, i, :], in_=pairs[m][:, i % 2, :])
             elif i % 2 == 1:
                 nc.sync.dma_start(out=rows[:, 2 * m : 2 * m + 2, :], in_=pairs[m][:])
 
-        def momentum(i, c):
-            if i // 2 not in new:
+        def momentum(i):
+            if i % 2 == 0:
                 nw = outs.tile([P, 2, RANK], F32, name="nw")
                 new[i // 2] = nw
-            nc.vector.scalar_tensor_tensor(out=new[i // 2][:, i % 2, c], in0=mom_raw[i][:, c], scalar=BETA, in1=acc[i][:, c], op0=MULT, op1=ADD)
-            store(i, c, new, new_rows)
+            nc.vector.scalar_tensor_tensor(out=new[i // 2][:, i % 2, :], in0=mom_raw[i], scalar=BETA, in1=acc[i][:], op0=MULT, op1=ADD)
+            store(i, new, new_rows)
 
-        def stepped(i, c=slice(0, RANK)):
+        def stepped(i):
             m = i // 2
-            if m not in step:
+            if i % 2 == 0:
                 if m < GPSIMD_PAIRS:
                     sp = keep.tile([P, 2, RANK], F32, name="sp%d" % m, tag="slot%d" % (2 * m + 6))
                 else:
                     sp = outs.tile([P, 2, RANK], F32, name="sp")
                 step[m] = sp
             if m < GPSIMD_PAIRS and i % 2 == 0:
-                nc.gpsimd.tensor_scalar(out=step[m][:, 0, c], in0=new[m][:, 0, c], scalar1=lr_f[:, i : i + 1], scalar2=0.0, op0=MULT, op1=ADD)
+                nc.gpsimd.tensor_scalar(out=step[m][:, 0, :], in0=new[m][:, 0, :], scalar1=lr_f[:, i : i + 1], scalar2=0.0, op0=MULT, op1=ADD)
             else:
-                nc.scalar.activation(out=step[m][:, i % 2, c], in_=new[m][:, i % 2, c], func=COPY, scale=lr_f[:, i : i + 1])
-            store(i, c, step, step_rows)
+                nc.scalar.activation(out=step[m][:, i % 2, :], in_=new[m][:, i % 2, :], func=COPY, scale=lr_f[:, i : i + 1])
+            store(i, step, step_rows)
 
-        PAIRED = 2 * GPSIMD_PAIRS + 2
+        paired = 2 * GPSIMD_PAIRS + 2
         momentum_at = {}
         step_at = {}
         for i in range(TILES):
-            momentum_at.setdefault(i + 7 - i % 2 if i < PAIRED else i + 6, []).append(i)
-            step_at.setdefault(i + 9 if i < 2 * GPSIMD_PAIRS else i + 8 - i % 2 if i < PAIRED else i + 7, []).append(i)
+            momentum_at.setdefault(i + 7 - i % 2 if i < paired else i + 6, []).append(i)
+            step_at.setdefault(i + 9 if i < 2 * GPSIMD_PAIRS else i + 8 - i % 2 if i < paired else i + 7, []).append(i)
 
-        spread = spread_basis_scales()
-        widen_v(0)
-        widen_s(0)
-        nc.scalar.copy(out=basis_sc[:], in_=spread)
+        spread = psum_t.tile([P, 2, 2, P], F32, name="xt")
+        nc.tensor.transpose(spread[:, 0, 0, :], basis_col[:, 0:1].to_broadcast([P, P]), ident[:])
+        cast(0)
+        widen(0)
+        cast(1)
+        nc.scalar.copy(out=basis_sc[:], in_=spread[:, 0, 0, 0 : ROW_TILES * BLOCKS])
         turn(0)
-        widen_v(1)
-        widen_s(1)
-        out_of_psum(0, 0, nc.scalar.copy)
-        widen_s(2)
-        out_of_psum(0, 1, nc.scalar.copy)
+        widen(1)
+        cast(2)
 
-        for s in range(UNITS + 2):
+        for s in range(last_unit + 4):
             j = s - PASSES
             if j >= 0 and j % 2 == 0:
                 load_pair(j // 2 + LOAD_AHEAD)
             if j >= 0 and j % 4 == 2:
                 load_mom(j // 4 + 2)
-            ahead = s + WIDEN_AHEAD
-            if 0 < s < UNITS:
-                out_of_psum(s, 0, nc.scalar.copy)
-                out_of_psum(s, 1, nc.scalar.copy)
-            if ahead < UNITS:
-                widen_v(ahead)
-            if ahead + 1 < UNITS:
-                widen_s(ahead + 1)
-            if s >= CAST_FROM and s % 2 == 1 and ahead + 2 < UNITS:
-                cast(ahead + 2)
-            if s + 1 < UNITS:
+            if s <= last_unit:
+                for h in (1, 0) if s < LEAD else (0, 1):
+                    out_of_psum(s, h)
+            if s + AHEAD <= last_unit:
+                widen(s + AHEAD)
+            if s + AHEAD + 1 <= last_unit:
+                cast(s + AHEAD + 1)
+            if s + 1 <= last_unit:
                 turn(s + 1)
-            if s == LEAD + PASSES:
+            if s == LEAD + ROW_TILES:
                 nc.vector.tensor_copy(out=lr_f[:], in_=lr_raw[:])
-            if s == UNITS - 1:
+            if s == last_unit:
                 quant(s, slice(0, 2 * P))
             for i in step_at.get(s, []):
                 stepped(i)
             for i in momentum_at.get(s, []):
-                for c in pieces(i):
-                    momentum(i, c)
-                    if i == TILES - 1:
-                        stepped(i, c)
-            if s < UNITS:
-                quant(s, slice(2 * P if s == UNITS - 1 else 0, PASSES * P))
-            if 1 <= s <= UNITS:
+                momentum(i)
+            if s <= last_unit:
+                quant(s, slice(2 * P if s == last_unit else 0, PASSES * P))
+            if 1 <= s <= last_unit + 1:
                 multiply(s - 1)

@@ -34,6 +34,8 @@ CAST_EVEN = 12
 CAST_ODD = 11
 CAST_TAIL = 9
 TRAILING = 3
+LAST_PIECES = (slice(0, 256), slice(256, 512))
+PIECE_STORES = False
 
 
 def tile_galore_projected_step_d2_kernel(tc, grad_bytes, grad_scale, basis_bytes, basis_scale, mom, lr, out_0, out_1):
@@ -66,7 +68,7 @@ def tile_galore_projected_step_d2_kernel(tc, grad_bytes, grad_scale, basis_bytes
         ctx.enter_context(tc.manual_schedule())
 
         basis_col = keep.tile([P, 1], F32, name="basis_col")
-        nc.gpsimd.memset(basis_col[64:128, :], 0.0)
+        nc.vector.memset(basis_col[64:128, :], 0.0)
         ident = keep.tile([P, P], F32, name="ident")
         make_identity(nc, ident[:])
 
@@ -146,13 +148,13 @@ def tile_galore_projected_step_d2_kernel(tc, grad_bytes, grad_scale, basis_bytes
                 order = list(range(count, BLOCKS)) + list(range(count))
             else:
                 order = list(range(count - TRAILING)) + list(range(count, BLOCKS)) + list(range(count - TRAILING, count))
+            dst = work.tile([P, K], BF16, name="wide", align_bytes=64, bufs=AHEAD + 2)
             for g in range(PASSES):
-                dst = work.tile([P, 512], BF16, name="wide%d" % g, align_bytes=64, bufs=AHEAD + 2)
-                wide[s, g] = dst
+                wide[s, g] = dst[:, 512 * g : 512 * g + 512]
             for c in order:
                 src = plain[s][:, 128 * c : 128 * c + 128] if c < count else raw[units[s]][:, 128 * c : 128 * c + 128].bitcast(FP8)
                 nc.vector.tensor_scalar(
-                    out=wide[s, c // 4][:].rearrange("p (u b j) -> p b u j", u=2, j=16)[:, 4 * (c % 4) : 4 * (c % 4) + 4],
+                    out=wide[s, c // 4].rearrange("p (u b j) -> p b u j", u=2, j=16)[:, 4 * (c % 4) : 4 * (c % 4) + 4],
                     in0=src.rearrange("p (b u j) -> p b u j", u=2, j=16),
                     scalar1=scale_of(s, c),
                     scalar2=None,
@@ -163,7 +165,7 @@ def tile_galore_projected_step_d2_kernel(tc, grad_bytes, grad_scale, basis_bytes
             for h in (1, 0) if s < LEAD else (0, 1):
                 xt = psum_t.tile([P, 2, 2, P], F32, name="xt")
                 for a in range(2):
-                    words = wide[s, 2 * h + a][:].bitcast(F32)
+                    words = wide[s, 2 * h + a].bitcast(F32)
                     for u in range(2):
                         nc.tensor.transpose(xt[:, a, u, :], words[:, P * u : P * u + P], ident[:])
                 bank[s, h] = xt
@@ -190,14 +192,15 @@ def tile_galore_projected_step_d2_kernel(tc, grad_bytes, grad_scale, basis_bytes
             cod, scl = codes[n]
             nc.vector.quantize_mx(out=cod[:, words].bitcast(FP8X4), scales=scl[:, words], in_=group[s][:, 4 * words.start : 4 * words.stop])
 
-        def product(i, cols):
-            if i not in acc:
+        def product(i, cols, own=False, passes=range(PASSES)):
+            key = (i, cols.start if own else 0)
+            if key not in acc:
                 a = psum_m.tile([P, RANK], F32, name="a")
-                acc[i] = a
+                acc[key] = a
             cod, scl = codes[i]
-            for g in range(PASSES):
+            for g in passes:
                 nc.tensor.matmul_mx(
-                    out=acc[i][:, cols],
+                    out=acc[key][:, cols],
                     lhsT=cod[:, P * g : P * g + P].bitcast(FP8X4),
                     lhsT_scale=scl[:, P * g : P * g + P],
                     rhs=bcodes[:, g, cols].bitcast(FP8X4),
@@ -211,24 +214,29 @@ def tile_galore_projected_step_d2_kernel(tc, grad_bytes, grad_scale, basis_bytes
             if kind == "basis":
                 for i in range(LEAD):
                     product(i, slice(P * n, P * n + P))
+            elif n == TILES - 1:
+                for passes in ((0, 1), (2, 3)):
+                    for c in LAST_PIECES:
+                        product(n, c, True, passes)
             elif n >= LEAD:
                 product(n, slice(0, RANK))
 
-        def store(i, pairs, rows):
+        def store(i, pairs, rows, c):
             m = i // 2
             if i >= TILES - SINGLE_STORES:
-                nc.sync.dma_start(out=rows[:, i, :], in_=pairs[m][:, i % 2, :])
+                nc.sync.dma_start(out=rows[:, i, c], in_=pairs[m][:, i % 2, c])
             elif i % 2 == 1:
                 nc.sync.dma_start(out=rows[:, 2 * m : 2 * m + 2, :], in_=pairs[m][:])
 
-        def momentum(i):
+        def momentum(i, c=slice(0, RANK), then_store=True):
             if i % 2 == 0:
                 nw = outs.tile([P, 2, RANK], F32, name="nw")
                 new[i // 2] = nw
-            nc.vector.scalar_tensor_tensor(out=new[i // 2][:, i % 2, :], in0=mom_raw[i], scalar=BETA, in1=acc[i][:], op0=MULT, op1=ADD)
-            store(i, new, new_rows)
+            nc.vector.scalar_tensor_tensor(out=new[i // 2][:, i % 2, c], in0=mom_raw[i][:, c], scalar=BETA, in1=acc[i, c.start][:, c], op0=MULT, op1=ADD)
+            if then_store:
+                store(i, new, new_rows, c)
 
-        def stepped(i):
+        def stepped(i, c=slice(0, RANK), then_store=True):
             m = i // 2
             if i % 2 == 0:
                 if m < GPSIMD_PAIRS:
@@ -239,13 +247,14 @@ def tile_galore_projected_step_d2_kernel(tc, grad_bytes, grad_scale, basis_bytes
             if m < GPSIMD_PAIRS and i % 2 == 0:
                 nc.gpsimd.tensor_scalar(out=step[m][:, 0, :], in0=new[m][:, 0, :], scalar1=lr_f[:, i : i + 1], scalar2=0.0, op0=MULT, op1=ADD)
             else:
-                nc.scalar.activation(out=step[m][:, i % 2, :], in_=new[m][:, i % 2, :], func=COPY, scale=lr_f[:, i : i + 1])
-            store(i, step, step_rows)
+                nc.scalar.activation(out=step[m][:, i % 2, c], in_=new[m][:, i % 2, c], func=COPY, scale=lr_f[:, i : i + 1])
+            if then_store:
+                store(i, step, step_rows, c)
 
         paired = 2 * GPSIMD_PAIRS + 2
         momentum_at = {}
         step_at = {}
-        for i in range(TILES):
+        for i in range(TILES - 1):
             momentum_at.setdefault(i + 7 - i % 2 if i < paired else i + 6, []).append(i)
             step_at.setdefault(i + 9 if i < 2 * GPSIMD_PAIRS else i + 8 - i % 2 if i < paired else i + 7, []).append(i)
 
@@ -259,15 +268,17 @@ def tile_galore_projected_step_d2_kernel(tc, grad_bytes, grad_scale, basis_bytes
         widen(1)
         cast(2)
 
-        for s in range(last_unit + 4):
+        for s in range(last_unit + 3):
             j = s - PASSES
             if j >= 0 and j % 2 == 0:
                 load_pair(j // 2 + LOAD_AHEAD)
             if j >= 0 and j % 4 == 2:
                 load_mom(j // 4 + 2)
-            if s <= last_unit:
+            if s < last_unit:
                 for h in (1, 0) if s < LEAD else (0, 1):
                     out_of_psum(s, h)
+            if s == last_unit:
+                out_of_psum(s, 0)
             if s + AHEAD <= last_unit:
                 widen(s + AHEAD)
             if s + AHEAD + 1 <= last_unit:
@@ -275,14 +286,24 @@ def tile_galore_projected_step_d2_kernel(tc, grad_bytes, grad_scale, basis_bytes
             if s + 1 <= last_unit:
                 turn(s + 1)
             if s == LEAD + ROW_TILES:
-                nc.vector.tensor_copy(out=lr_f[:], in_=lr_raw[:])
+                nc.scalar.copy(out=lr_f[:], in_=lr_raw[:])
             if s == last_unit:
                 quant(s, slice(0, 2 * P))
             for i in step_at.get(s, []):
                 stepped(i)
+            if s == last_unit:
+                out_of_psum(s, 1)
             for i in momentum_at.get(s, []):
                 momentum(i)
             if s <= last_unit:
                 quant(s, slice(2 * P if s == last_unit else 0, PASSES * P))
             if 1 <= s <= last_unit + 1:
                 multiply(s - 1)
+
+        last = TILES - 1
+        for c in LAST_PIECES:
+            momentum(last, c, PIECE_STORES)
+            stepped(last, c, PIECE_STORES)
+        if not PIECE_STORES:
+            store(last, new, new_rows, slice(0, RANK))
+            store(last, step, step_rows, slice(0, RANK))

@@ -30,10 +30,11 @@ GPSIMD_PAIRS = 12
 SINGLE_STORES = 6
 CAST_FIRST = 7
 CAST_HEAD = 9
-CAST_EVEN = 12
-CAST_ODD = 11
+CAST_EVEN = 13
+CAST_ODD = 13
 CAST_TAIL = 9
-TRAILING = 3
+TRAILING = 8
+GPSIMD_COLUMNS = 256
 LAST_PIECES = (slice(0, 256), slice(256, 512))
 PIECE_STORES = False
 
@@ -245,8 +246,11 @@ def tile_galore_projected_step_d2_kernel(tc, grad_bytes, grad_scale, basis_bytes
                     sp = outs.tile([P, 2, RANK], F32, name="sp")
                 step[m] = sp
             if m < GPSIMD_PAIRS and i % 2 == 0:
-                nc.gpsimd.tensor_scalar(out=step[m][:, 0, :], in0=new[m][:, 0, :], scalar1=lr_f[:, i : i + 1], scalar2=0.0, op0=MULT, op1=ADD)
+                for t, cols in ((0, slice(0, RANK)), (1, slice(0, GPSIMD_COLUMNS))):
+                    nc.gpsimd.tensor_scalar(out=step[m][:, t, cols], in0=new[m][:, t, cols], scalar1=lr_f[:, i + t : i + t + 1], scalar2=0.0, op0=MULT, op1=ADD)
             else:
+                if m < GPSIMD_PAIRS:
+                    c = slice(GPSIMD_COLUMNS, RANK)
                 nc.scalar.activation(out=step[m][:, i % 2, c], in_=new[m][:, i % 2, c], func=COPY, scale=lr_f[:, i : i + 1])
             if then_store:
                 store(i, step, step_rows, c)

@@ -23,20 +23,20 @@ ADD = mybir.AluOpType.add
 COPY = mybir.ActivationFunctionType.Copy
 
 LEAD = 2
-AHEAD = 2
-LOAD_AHEAD = 8
+RUN = 3
+RUNS = 8
+LOAD_AHEAD = 16
 FIRST_SCALES = 4
-GPSIMD_PAIRS = 12
-SINGLE_STORES = 6
 CAST_FIRST = 7
 CAST_HEAD = 9
-CAST_EVEN = 13
-CAST_ODD = 13
-CAST_TAIL = 9
-TRAILING = 8
-GPSIMD_COLUMNS = 256
-LAST_PIECES = (slice(0, 256), slice(256, 512))
-PIECE_STORES = False
+CAST_RUN = (12,13,12)
+CAST_TAIL = 8
+HEAD_UNITS = 11
+TAIL_FROM = 33
+PAD = 64
+CATCH_UP = 33
+HALVES = (slice(0, 256), slice(256, 512))
+ALL = slice(0, RANK)
 
 
 def tile_galore_projected_step_d2_kernel(tc, grad_bytes, grad_scale, basis_bytes, basis_scale, mom, lr, out_0, out_1):
@@ -50,22 +50,33 @@ def tile_galore_projected_step_d2_kernel(tc, grad_bytes, grad_scale, basis_bytes
 
     units = [("grad", i) for i in range(LEAD)] + [("basis", b) for b in range(ROW_TILES)] + [("grad", i) for i in range(LEAD, TILES)]
     last_unit = len(units) - 1
+    in_runs = RUN * RUNS
+    run_step = {RUN * r + 8: RUN * r for r in range(RUNS)}
+    last_run_step = max(run_step)
 
     def cast_blocks(s):
         if s < LEAD:
             return CAST_FIRST
-        if s < LEAD + ROW_TILES + 4:
+        if s < HEAD_UNITS:
             return CAST_HEAD
-        if s >= 2 * GPSIMD_PAIRS + 10:
+        if s >= TAIL_FROM:
             return CAST_TAIL
-        return CAST_ODD if s % 2 else CAST_EVEN
+        return CAST_RUN[s % len(CAST_RUN)]
+
+    def widened_by(s):
+        ahead = 0
+        if min(run_step) <= s < last_run_step:
+            ahead = 8 * ((s - min(run_step)) % RUN)
+        return min(BLOCKS * (s + 3) + ahead, BLOCKS * len(units))
+
+    loads = [(0, 1), (1, 1), (2, 2)] + [(i, RUN) for i in range(4, TILES - 1, RUN)] + [(TILES - 1, 1)]
 
     with ExitStack() as ctx:
         keep = ctx.enter_context(tc.tile_pool(name="keep", bufs=1))
         work = ctx.enter_context(tc.tile_pool(name="work", bufs=3))
-        outs = ctx.enter_context(tc.tile_pool(name="outs", bufs=5))
-        psum_t = ctx.enter_context(tc.psum_pool(name="psum_t", bufs=5))
-        psum_m = ctx.enter_context(tc.psum_pool(name="psum_m", bufs=3))
+        outs = ctx.enter_context(tc.tile_pool(name="outs", bufs=3))
+        psum_t = ctx.enter_context(tc.psum_pool(name="psum_t", bufs=4))
+        psum_m = ctx.enter_context(tc.psum_pool(name="psum_m", bufs=4))
         ctx.enter_context(tc.manual_schedule())
 
         basis_col = keep.tile([P, 1], F32, name="basis_col")
@@ -77,14 +88,14 @@ def tile_galore_projected_step_d2_kernel(tc, grad_bytes, grad_scale, basis_bytes
         mom_raw = {}
 
         def load_grad(first, count):
-            g = keep.tile([P, count, K], U8, name="g%d" % first, tag="slot%d" % first)
-            nc.sync.dma_start(out=g[:], in_=grad_rows[:, first : first + count, :])
+            g = keep.tile([P, count, K + PAD], U8, name="g%d" % first, tag="slot%d" % (first + count - 1))
+            nc.sync.dma_start(out=g[:, :, 0:K], in_=grad_rows[:, first : first + count, :])
             for t in range(count):
-                raw["grad", first + t] = g[:, t, :]
+                raw["grad", first + t] = g[:, t, 0:K]
 
-        def load_pair(m):
-            if m < TILES // 2:
-                load_grad(2 * m, 2)
+        def load_until(tile):
+            while loads and loads[0][0] <= tile:
+                load_grad(*loads.pop(0))
 
         def load_mom(m):
             if m < TILES // 4:
@@ -95,22 +106,21 @@ def tile_galore_projected_step_d2_kernel(tc, grad_bytes, grad_scale, basis_bytes
 
         sc_first = keep.tile([P, FIRST_SCALES * BLOCKS], F32, name="sc_first")
         nc.sync.dma_start(out=sc_first[:], in_=scale_rows[:, 0 : FIRST_SCALES * BLOCKS])
-        load_grad(0, 1)
+        load_until(0)
         nc.sync.dma_start(out=basis_col[0:64, :], in_=basis_scale.rearrange("b (c o) -> (b c) o", o=1))
-        load_grad(1, 1)
+        load_until(1)
         for b in range(ROW_TILES):
             braw = keep.tile([P, K], U8, name="braw%d" % b)
             nc.sync.dma_start(out=braw[:], in_=basis_rows[:, b, :])
             raw["basis", b] = braw[:]
-        load_pair(1)
+        load_until(2)
         sc_rest = keep.tile([P, (TILES - FIRST_SCALES) * BLOCKS], F32, name="sc_rest")
         nc.sync.dma_start(out=sc_rest[:], in_=scale_rows[:, FIRST_SCALES * BLOCKS :])
-        load_pair(2)
+        load_until(4)
         load_mom(0)
         lr_raw = keep.tile([P, TILES], BF16, name="lr_raw")
         nc.sync.dma_start(out=lr_raw[:], in_=lr.rearrange("(p i) -> p i", p=P))
-        for m in range(3, LOAD_AHEAD):
-            load_pair(m)
+        load_until(LOAD_AHEAD)
         load_mom(1)
 
         dummy = keep.tile([P, 1], F32, name="dummy")
@@ -138,35 +148,35 @@ def tile_galore_projected_step_d2_kernel(tc, grad_bytes, grad_scale, basis_bytes
             return sc[:, BLOCKS * (n - first) + c : BLOCKS * (n - first) + c + 1]
 
         def cast(s):
-            width = 128 * cast_blocks(s)
-            values = work.tile([P, width], BF16, name="values", align_bytes=64)
-            nc.scalar.copy(out=values[:], in_=raw[units[s]][:, 0:width].bitcast(FP8))
-            plain[s] = values
+            if s <= last_unit and s not in plain:
+                width = 128 * cast_blocks(s)
+                values = work.tile([P, width], BF16, name="values", align_bytes=64, bufs=4)
+                nc.scalar.copy(out=values[:], in_=raw[units[s]][:, 0:width].bitcast(FP8))
+                plain[s] = values
 
-        def widen(s):
-            count = cast_blocks(s)
-            if s < LEAD:
-                order = list(range(count, BLOCKS)) + list(range(count))
-            else:
-                order = list(range(count - TRAILING)) + list(range(count, BLOCKS)) + list(range(count - TRAILING, count))
-            dst = work.tile([P, K], BF16, name="wide", align_bytes=64, bufs=AHEAD + 2)
-            for g in range(PASSES):
-                wide[s, g] = dst[:, 512 * g : 512 * g + 512]
-            for c in order:
+        def widen(first, stop):
+            for n in range(first, stop):
+                s, place = divmod(n, BLOCKS)
+                count = cast_blocks(s)
+                c = (place + count) % BLOCKS if s < LEAD else place
+                if place == 0:
+                    dst = work.tile([P, K], BF16, name="wide", align_bytes=64, bufs=5)
+                    wide[s] = dst
                 src = plain[s][:, 128 * c : 128 * c + 128] if c < count else raw[units[s]][:, 128 * c : 128 * c + 128].bitcast(FP8)
+                halves = wide[s][:, 512 * (c // 4) : 512 * (c // 4) + 512].rearrange("p (u b j) -> p b u j", u=2, j=16)
                 nc.vector.tensor_scalar(
-                    out=wide[s, c // 4].rearrange("p (u b j) -> p b u j", u=2, j=16)[:, 4 * (c % 4) : 4 * (c % 4) + 4],
+                    out=halves[:, 4 * (c % 4) : 4 * (c % 4) + 4],
                     in0=src.rearrange("p (b u j) -> p b u j", u=2, j=16),
                     scalar1=scale_of(s, c),
                     scalar2=None,
                     op0=MULT,
                 )
 
-        def turn(s):
-            for h in (1, 0) if s < LEAD else (0, 1):
+        def turn(s, sides=(0, 1)):
+            for h in sides:
                 xt = psum_t.tile([P, 2, 2, P], F32, name="xt")
                 for a in range(2):
-                    words = wide[s, 2 * h + a].bitcast(F32)
+                    words = wide[s][:, 512 * (2 * h + a) : 512 * (2 * h + a) + 512].bitcast(F32)
                     for u in range(2):
                         nc.tensor.transpose(xt[:, a, u, :], words[:, P * u : P * u + P], ident[:])
                 bank[s, h] = xt
@@ -180,7 +190,7 @@ def tile_galore_projected_step_d2_kernel(tc, grad_bytes, grad_scale, basis_bytes
                 in_=bank[s, h][:].rearrange("p a u r -> p a r u"),
             )
 
-        def quant(s, words):
+        def quant(s, words=slice(0, PASSES * P)):
             kind, n = units[s]
             if kind == "basis":
                 for g in range(PASSES):
@@ -215,99 +225,115 @@ def tile_galore_projected_step_d2_kernel(tc, grad_bytes, grad_scale, basis_bytes
             if kind == "basis":
                 for i in range(LEAD):
                     product(i, slice(P * n, P * n + P))
-            elif n == TILES - 1:
-                for passes in ((0, 1), (2, 3)):
-                    for c in LAST_PIECES:
-                        product(n, c, True, passes)
             elif n >= LEAD:
-                product(n, slice(0, RANK))
+                product(n, ALL)
 
-        def store(i, pairs, rows, c):
-            m = i // 2
-            if i >= TILES - SINGLE_STORES:
-                nc.sync.dma_start(out=rows[:, i, c], in_=pairs[m][:, i % 2, c])
-            elif i % 2 == 1:
-                nc.sync.dma_start(out=rows[:, 2 * m : 2 * m + 2, :], in_=pairs[m][:])
+        def open_rows(table, first, count, tile):
+            for t in range(count):
+                table[first + t] = (tile, first, count)
 
-        def momentum(i, c=slice(0, RANK), then_store=True):
-            if i % 2 == 0:
-                nw = outs.tile([P, 2, RANK], F32, name="nw")
-                new[i // 2] = nw
-            nc.vector.scalar_tensor_tensor(out=new[i // 2][:, i % 2, c], in0=mom_raw[i][:, c], scalar=BETA, in1=acc[i, c.start][:, c], op0=MULT, op1=ADD)
-            if then_store:
-                store(i, new, new_rows, c)
+        def store(table, rows, i, c=ALL):
+            tile, first, count = table[i]
+            if i == first + count - 1:
+                nc.sync.dma_start(out=rows[:, first : first + count, c], in_=tile[:, 0:count, c])
 
-        def stepped(i, c=slice(0, RANK), then_store=True):
-            m = i // 2
-            if i % 2 == 0:
-                if m < GPSIMD_PAIRS:
-                    sp = keep.tile([P, 2, RANK], F32, name="sp%d" % m, tag="slot%d" % (2 * m + 6))
+        def momentum(i, c=ALL):
+            if i not in new:
+                nw = outs.tile([P, RUN, RANK], F32, name="nw")
+                open_rows(new, i, RUN if i < in_runs else 1, nw)
+            tile, first, count = new[i]
+            nc.vector.scalar_tensor_tensor(out=tile[:, i - first, c], in0=mom_raw[i][:, c], scalar=BETA, in1=acc[i, c.start][:, c], op0=MULT, op1=ADD)
+
+        def stepped(i, engine, c=ALL):
+            if i not in step:
+                if i == 0:
+                    sp = outs.tile([P, RUN, RANK], F32, name="sp")
+                    open_rows(step, i, RUN - 1, sp)
+                elif i < in_runs - 1:
+                    sp = keep.tile([P, RUN, RANK], F32, name="sp%d" % i, tag="slot%d" % (i + 7))
+                    open_rows(step, i, RUN, sp)
                 else:
-                    sp = outs.tile([P, 2, RANK], F32, name="sp")
-                step[m] = sp
-            if m < GPSIMD_PAIRS and i % 2 == 0:
-                for t, cols in ((0, slice(0, RANK)), (1, slice(0, GPSIMD_COLUMNS))):
-                    nc.gpsimd.tensor_scalar(out=step[m][:, t, cols], in0=new[m][:, t, cols], scalar1=lr_f[:, i + t : i + t + 1], scalar2=0.0, op0=MULT, op1=ADD)
+                    sp = outs.tile([P, RUN, RANK], F32, name="sp")
+                    open_rows(step, i, 1, sp)
+            dst = step[i][0][:, i - step[i][1], c]
+            src = new[i][0][:, i - new[i][1], c]
+            if engine == "gpsimd":
+                nc.gpsimd.tensor_scalar(out=dst, in0=src, scalar1=lr_f[:, i : i + 1], scalar2=0.0, op0=MULT, op1=ADD)
+            elif engine == "vector":
+                nc.vector.tensor_scalar(out=dst, in0=src, scalar1=lr_f[:, i : i + 1], scalar2=None, op0=MULT)
             else:
-                if m < GPSIMD_PAIRS:
-                    c = slice(GPSIMD_COLUMNS, RANK)
-                nc.scalar.activation(out=step[m][:, i % 2, c], in_=new[m][:, i % 2, c], func=COPY, scale=lr_f[:, i : i + 1])
-            if then_store:
-                store(i, step, step_rows, c)
+                nc.scalar.activation(out=dst, in_=src, func=COPY, scale=lr_f[:, i : i + 1])
 
-        paired = 2 * GPSIMD_PAIRS + 2
-        momentum_at = {}
-        step_at = {}
-        for i in range(TILES - 1):
-            momentum_at.setdefault(i + 7 - i % 2 if i < paired else i + 6, []).append(i)
-            step_at.setdefault(i + 9 if i < 2 * GPSIMD_PAIRS else i + 8 - i % 2 if i < paired else i + 7, []).append(i)
+        def step_and_store(i, engine="scalar"):
+            stepped(i, engine)
+            store(step, step_rows, i)
+
+        def momentum_and_store(i):
+            momentum(i)
+            store(new, new_rows, i)
 
         spread = psum_t.tile([P, 2, 2, P], F32, name="xt")
         nc.tensor.transpose(spread[:, 0, 0, :], basis_col[:, 0:1].to_broadcast([P, P]), ident[:])
         cast(0)
-        widen(0)
+        widen(0, BLOCKS)
         cast(1)
         nc.scalar.copy(out=basis_sc[:], in_=spread[:, 0, 0, 0 : ROW_TILES * BLOCKS])
-        turn(0)
-        widen(1)
+        turn(0, (1, 0))
+        widen(BLOCKS, 2 * BLOCKS)
         cast(2)
 
-        for s in range(last_unit + 3):
+        for s in range(last_unit):
             j = s - PASSES
-            if j >= 0 and j % 2 == 0:
-                load_pair(j // 2 + LOAD_AHEAD)
-            if j >= 0 and j % 4 == 2:
-                load_mom(j // 4 + 2)
-            if s < last_unit:
-                for h in (1, 0) if s < LEAD else (0, 1):
-                    out_of_psum(s, h)
-            if s == last_unit:
-                out_of_psum(s, 0)
-            if s + AHEAD <= last_unit:
-                widen(s + AHEAD)
-            if s + AHEAD + 1 <= last_unit:
-                cast(s + AHEAD + 1)
-            if s + 1 <= last_unit:
-                turn(s + 1)
+            load_until(j + LOAD_AHEAD)
+            if j >= 0 and j % 3 == 2:
+                load_mom(j // 3 + 2)
+            for h in (1, 0) if s < LEAD else (0, 1):
+                out_of_psum(s, h)
+            if s > last_run_step:
+                momentum_and_store(s - 6)
+            widen(widened_by(s - 1), widened_by(s))
+            cast(s + 3)
+            if min(run_step) <= s < last_run_step - 1:
+                cast(s + 4)
+            turn(s + 1, (1, 0) if s + 1 < LEAD else (0, 1))
             if s == LEAD + ROW_TILES:
                 nc.scalar.copy(out=lr_f[:], in_=lr_raw[:])
-            if s == last_unit:
-                quant(s, slice(0, 2 * P))
-            for i in step_at.get(s, []):
-                stepped(i)
-            if s == last_unit:
-                out_of_psum(s, 1)
-            for i in momentum_at.get(s, []):
+            if s - 1 in run_step:
+                step_and_store(run_step[s - 1] + 1)
+            if s - 1 == last_run_step:
+                step_and_store(in_runs - 1)
+            if s - 7 >= in_runs and s - 7 not in step:
+                step_and_store(s - 7)
+            if s >= CATCH_UP:
+                step_and_store(s - 6)
+            if s in run_step:
+                i = run_step[s]
+                if i > 0:
+                    stepped(i - 1, "gpsimd")
                 momentum(i)
-            if s <= last_unit:
-                quant(s, slice(2 * P if s == last_unit else 0, PASSES * P))
-            if 1 <= s <= last_unit + 1:
+                stepped(i, "gpsimd")
+                momentum(i + 1)
+                momentum_and_store(i + 2)
+            quant(s)
+            if s >= 1:
                 multiply(s - 1)
 
+        s = last_unit
         last = TILES - 1
-        for c in LAST_PIECES:
-            momentum(last, c, PIECE_STORES)
-            stepped(last, c, PIECE_STORES)
-        if not PIECE_STORES:
-            store(last, new, new_rows, slice(0, RANK))
-            store(last, step, step_rows, slice(0, RANK))
+        out_of_psum(s, 0)
+        momentum_and_store(last - 2)
+        quant(s, slice(0, 2 * P))
+        out_of_psum(s, 1)
+        step_and_store(last - 2)
+        quant(s, slice(2 * P, PASSES * P))
+        multiply(s - 1)
+        momentum_and_store(last - 1)
+        for passes in ((0, 1), (2, 3)):
+            for c in HALVES:
+                product(last, c, True, passes)
+        step_and_store(last - 1)
+        for c in HALVES:
+            momentum(last, c)
+            stepped(last, "scalar", c)
+        store(new, new_rows, last)
+        store(step, step_rows, last)

@@ -27,10 +27,9 @@ RUN = 3
 RUNS = 8
 LOAD_AHEAD = 16
 FIRST_SCALES = 4
-CAST_FIRST = 7
-CAST_HEAD = 9
+CAST_HEAD = {0: 8, 1: 0, 2: 16, 3: 16, 4: 16, 5: 16, 6: 0, 7: 0, 8: 0, 9: 6, 10: 12}
 CAST_RUN = (12,13,12)
-CAST_TAIL = 8
+CAST_TAIL = 12
 HEAD_UNITS = 11
 TAIL_FROM = 33
 PAD = 64
@@ -43,7 +42,7 @@ def tile_galore_projected_step_d2_kernel(tc, grad_bytes, grad_scale, basis_bytes
     nc = tc.nc
     grad_rows = grad_bytes.rearrange("(p i) k -> p i k", p=P)
     scale_rows = grad_scale.rearrange("(p i) c -> p (i c)", p=P)
-    basis_rows = basis_bytes.rearrange("(b p) k -> p b k", p=P)
+    basis_rows = basis_bytes.rearrange("(p j) k -> p j k", p=P)
     mom_rows = mom.rearrange("(p i) n -> p i n", p=P)
     step_rows = out_0.rearrange("(p i) n -> p i n", p=P)
     new_rows = out_1.rearrange("(p i) n -> p i n", p=P)
@@ -55,10 +54,8 @@ def tile_galore_projected_step_d2_kernel(tc, grad_bytes, grad_scale, basis_bytes
     last_run_step = max(run_step)
 
     def cast_blocks(s):
-        if s < LEAD:
-            return CAST_FIRST
-        if s < HEAD_UNITS:
-            return CAST_HEAD
+        if s in CAST_HEAD:
+            return CAST_HEAD[s]
         if s >= TAIL_FROM:
             return CAST_TAIL
         return CAST_RUN[s % len(CAST_RUN)]
@@ -69,7 +66,7 @@ def tile_galore_projected_step_d2_kernel(tc, grad_bytes, grad_scale, basis_bytes
             ahead = 8 * ((s - min(run_step)) % RUN)
         return min(BLOCKS * (s + 3) + ahead, BLOCKS * len(units))
 
-    loads = [(0, 1), (1, 1), (2, 2)] + [(i, RUN) for i in range(4, TILES - 1, RUN)] + [(TILES - 1, 1)]
+    loads = [(0, 1), (1, 1), (2, 1), (3, 1)] + [(i, RUN) for i in range(4, TILES - 4, RUN)] + [(TILES - 4, 2), (TILES - 2, 2)]
 
     with ExitStack() as ctx:
         keep = ctx.enter_context(tc.tile_pool(name="keep", bufs=1))
@@ -79,8 +76,8 @@ def tile_galore_projected_step_d2_kernel(tc, grad_bytes, grad_scale, basis_bytes
         psum_m = ctx.enter_context(tc.psum_pool(name="psum_m", bufs=4))
         ctx.enter_context(tc.manual_schedule())
 
-        basis_col = keep.tile([P, 1], F32, name="basis_col")
-        nc.vector.memset(basis_col[64:128, :], 0.0)
+        by_column = keep.tile([P, ROW_TILES], F32, name="by_column")
+        nc.vector.memset(by_column[:], 0.0)
         ident = keep.tile([P, P], F32, name="ident")
         make_identity(nc, ident[:])
 
@@ -106,14 +103,21 @@ def tile_galore_projected_step_d2_kernel(tc, grad_bytes, grad_scale, basis_bytes
 
         sc_first = keep.tile([P, FIRST_SCALES * BLOCKS], F32, name="sc_first")
         nc.sync.dma_start(out=sc_first[:], in_=scale_rows[:, 0 : FIRST_SCALES * BLOCKS])
+        def load_basis(g):
+            braw = keep.tile([P, ROW_TILES, 512], U8, name="braw%d" % g)
+            nc.sync.dma_start(out=braw[:], in_=basis_rows[:, :, 512 * g : 512 * g + 512])
+            raw["basis", g] = braw[:].rearrange("p j k -> p (j k)")
+
         load_until(0)
-        nc.sync.dma_start(out=basis_col[0:64, :], in_=basis_scale.rearrange("b (c o) -> (b c) o", o=1))
+        with nc.allow_non_contiguous_dma(reason="64 scales, once"):
+            nc.sync.dma_start(out=by_column[0:BLOCKS, :], in_=basis_scale.rearrange("b c -> c b"))
+        load_basis(0)
         load_until(1)
-        for b in range(ROW_TILES):
-            braw = keep.tile([P, K], U8, name="braw%d" % b)
-            nc.sync.dma_start(out=braw[:], in_=basis_rows[:, b, :])
-            raw["basis", b] = braw[:]
+        load_basis(1)
         load_until(2)
+        load_basis(2)
+        load_until(3)
+        load_basis(3)
         sc_rest = keep.tile([P, (TILES - FIRST_SCALES) * BLOCKS], F32, name="sc_rest")
         nc.sync.dma_start(out=sc_rest[:], in_=scale_rows[:, FIRST_SCALES * BLOCKS :])
         load_until(4)
@@ -126,7 +130,8 @@ def tile_galore_projected_step_d2_kernel(tc, grad_bytes, grad_scale, basis_bytes
         dummy = keep.tile([P, 1], F32, name="dummy")
         nc.scalar.activation(out=dummy[:], in_=ident[:, 0:1], func=COPY)
 
-        basis_sc = keep.tile([P, ROW_TILES * BLOCKS], F32, name="basis_sc")
+        basis_sc = keep.tile([P, BLOCKS], F32, name="basis_sc")
+        by_partition = keep.tile([P, ROW_TILES, P // ROW_TILES], F32, name="by_partition")
         lr_f = keep.tile([P, TILES], F32, name="lr_f")
         bcodes = keep.tile([P, PASSES, RANK], U32, name="bcodes", align_bytes=64)
         bscales = keep.tile([P, PASSES, RANK], U8, name="bscales", align_bytes=64)
@@ -142,13 +147,11 @@ def tile_galore_projected_step_d2_kernel(tc, grad_bytes, grad_scale, basis_bytes
 
         def scale_of(s, c):
             kind, n = units[s]
-            if kind == "basis":
-                return basis_sc[:, BLOCKS * n + c : BLOCKS * n + c + 1]
             sc, first = (sc_first, 0) if n < FIRST_SCALES else (sc_rest, FIRST_SCALES)
             return sc[:, BLOCKS * (n - first) + c : BLOCKS * (n - first) + c + 1]
 
         def cast(s):
-            if s <= last_unit and s not in plain:
+            if s <= last_unit and s not in plain and cast_blocks(s):
                 width = 128 * cast_blocks(s)
                 values = work.tile([P, width], BF16, name="values", align_bytes=64, bufs=4)
                 nc.scalar.copy(out=values[:], in_=raw[units[s]][:, 0:width].bitcast(FP8))
@@ -158,9 +161,9 @@ def tile_galore_projected_step_d2_kernel(tc, grad_bytes, grad_scale, basis_bytes
             for n in range(first, stop):
                 s, place = divmod(n, BLOCKS)
                 count = cast_blocks(s)
-                c = (place + count) % BLOCKS if s < LEAD else place
+                c = (place + count) % BLOCKS if s in (0, 8, 9) else place
                 if place == 0:
-                    dst = work.tile([P, K], BF16, name="wide", align_bytes=64, bufs=5)
+                    dst = work.tile([P, K], BF16, name="wide", align_bytes=64, bufs=6)
                     wide[s] = dst
                 src = plain[s][:, 128 * c : 128 * c + 128] if c < count else raw[units[s]][:, 128 * c : 128 * c + 128].bitcast(FP8)
                 halves = wide[s][:, 512 * (c // 4) : 512 * (c // 4) + 512].rearrange("p (u b j) -> p b u j", u=2, j=16)
@@ -171,6 +174,22 @@ def tile_galore_projected_step_d2_kernel(tc, grad_bytes, grad_scale, basis_bytes
                     scalar2=None,
                     op0=MULT,
                 )
+
+        def widen_basis(s):
+            g = units[s][1]
+            dst = work.tile([P, K], BF16, name="wide", align_bytes=64, bufs=6)
+            wide[s] = dst
+            src = plain[s][:].rearrange("p (j b u x) -> p j b u x", j=ROW_TILES, u=2, x=16)
+            halves = dst[:].rearrange("p (j u b x) -> p j b u x", j=ROW_TILES, u=2, x=16)
+            for c in range(4):
+                for u in range(2):
+                    nc.vector.tensor_scalar(
+                        out=halves[:, :, 4 * c : 4 * c + 4, u, :],
+                        in0=src[:, :, 4 * c : 4 * c + 4, u, :],
+                        scalar1=basis_sc[:, 4 * g + c : 4 * g + c + 1],
+                        scalar2=None,
+                        op0=MULT,
+                    )
 
         def turn(s, sides=(0, 1)):
             for h in sides:
@@ -185,6 +204,12 @@ def tile_galore_projected_step_d2_kernel(tc, grad_bytes, grad_scale, basis_bytes
             if s not in group:
                 grp = work.tile([P, K], BF16, name="grp", align_bytes=64)
                 group[s] = grp
+            if units[s][0] == "basis":
+                nc.scalar.copy(
+                    out=group[s][:].bitcast(F32).rearrange("p (r j u) -> p r j u", j=ROW_TILES, u=2)[:, :, 2 * h : 2 * h + 2, :],
+                    in_=bank[s, h][:].rearrange("p a u r -> p r a u"),
+                )
+                return
             nc.scalar.copy(
                 out=group[s][:, 1024 * h : 1024 * h + 1024].bitcast(F32).rearrange("p (a r u) -> p a r u", a=2, u=2),
                 in_=bank[s, h][:].rearrange("p a u r -> p a r u"),
@@ -193,8 +218,7 @@ def tile_galore_projected_step_d2_kernel(tc, grad_bytes, grad_scale, basis_bytes
         def quant(s, words=slice(0, PASSES * P)):
             kind, n = units[s]
             if kind == "basis":
-                for g in range(PASSES):
-                    nc.vector.quantize_mx(out=bcodes[:, g, P * n : P * n + P].bitcast(FP8X4), scales=bscales[:, g, P * n : P * n + P], in_=group[s][:, 512 * g : 512 * g + 512])
+                nc.vector.quantize_mx(out=bcodes[:, n, :].bitcast(FP8X4), scales=bscales[:, n, :], in_=group[s][:])
                 return
             if n not in codes:
                 cod = work.tile([P, PASSES * P], U32, name="cod", align_bytes=64)
@@ -224,7 +248,7 @@ def tile_galore_projected_step_d2_kernel(tc, grad_bytes, grad_scale, basis_bytes
             kind, n = units[s]
             if kind == "basis":
                 for i in range(LEAD):
-                    product(i, slice(P * n, P * n + P))
+                    product(i, ALL, passes=(n,))
             elif n >= LEAD:
                 product(n, ALL)
 
@@ -239,7 +263,10 @@ def tile_galore_projected_step_d2_kernel(tc, grad_bytes, grad_scale, basis_bytes
 
         def momentum(i, c=ALL):
             if i not in new:
-                nw = outs.tile([P, RUN, RANK], F32, name="nw")
+                if i < in_runs:
+                    nw = outs.tile([P, RUN, RANK], F32, name="nw")
+                else:
+                    nw = outs.tile([P, 1, RANK], F32, name="nw_one", bufs=4)
                 open_rows(new, i, RUN if i < in_runs else 1, nw)
             tile, first, count = new[i]
             nc.vector.scalar_tensor_tensor(out=tile[:, i - first, c], in0=mom_raw[i][:, c], scalar=BETA, in1=acc[i, c.start][:, c], op0=MULT, op1=ADD)
@@ -247,13 +274,16 @@ def tile_galore_projected_step_d2_kernel(tc, grad_bytes, grad_scale, basis_bytes
         def stepped(i, engine, c=ALL):
             if i not in step:
                 if i == 0:
-                    sp = outs.tile([P, RUN, RANK], F32, name="sp")
+                    sp = keep.tile([P, RUN - 1, RANK], F32, name="sp0")
                     open_rows(step, i, RUN - 1, sp)
-                elif i < in_runs - 1:
+                elif i < in_runs - 2:
                     sp = keep.tile([P, RUN, RANK], F32, name="sp%d" % i, tag="slot%d" % (i + 7))
-                    open_rows(step, i, RUN, sp)
+                    open_rows(step, i, RUN if i < in_runs - 4 else RUN - 1, sp)
+                elif i == in_runs - 1:
+                    sp = keep.tile([P, 1, RANK], F32, name="sp%d" % i, tag="slot%d" % (i + 6))
+                    open_rows(step, i, 1, sp)
                 else:
-                    sp = outs.tile([P, RUN, RANK], F32, name="sp")
+                    sp = outs.tile([P, 1, RANK], F32, name="sp_one", bufs=4)
                     open_rows(step, i, 1, sp)
             dst = step[i][0][:, i - step[i][1], c]
             src = new[i][0][:, i - new[i][1], c]
@@ -272,17 +302,61 @@ def tile_galore_projected_step_d2_kernel(tc, grad_bytes, grad_scale, basis_bytes
             momentum(i)
             store(new, new_rows, i)
 
-        spread = psum_t.tile([P, 2, 2, P], F32, name="xt")
-        nc.tensor.transpose(spread[:, 0, 0, :], basis_col[:, 0:1].to_broadcast([P, P]), ident[:])
-        cast(0)
-        widen(0, BLOCKS)
-        cast(1)
-        nc.scalar.copy(out=basis_sc[:], in_=spread[:, 0, 0, 0 : ROW_TILES * BLOCKS])
-        turn(0, (1, 0))
-        widen(BLOCKS, 2 * BLOCKS)
-        cast(2)
+        def empty(s):
+            out_of_psum(s, 0)
+            out_of_psum(s, 1)
 
-        for s in range(last_unit):
+        def whole(s):
+            widen(BLOCKS * s, BLOCKS * s + BLOCKS)
+
+        cast(0)
+        widen(0, 8)
+        nc.vector.tensor_copy(out=by_partition[:], in_=by_column[:].unsqueeze(2).to_broadcast([P, ROW_TILES, P // ROW_TILES]))
+        spread = psum_t.tile([P, 2, 2, P], F32, name="xt")
+        nc.tensor.transpose(spread[:, 0, 0, :], by_partition[:].rearrange("p b r -> p (b r)"), ident[:])
+        widen(8, BLOCKS)
+        nc.vector.tensor_copy(out=basis_sc[:], in_=spread[:, 0, 0, 0:BLOCKS])
+        cast(2)
+        turn(0, (1, 0))
+        whole(1)
+        out_of_psum(0, 1)
+        out_of_psum(0, 0)
+        turn(1)
+        cast(3)
+        widen_basis(2)
+        quant(0)
+        empty(1)
+        turn(2)
+        whole(6)
+        cast(4)
+        widen_basis(3)
+        quant(1)
+        empty(2)
+        turn(3)
+        cast(5)
+        widen_basis(4)
+        widen(BLOCKS * 7, BLOCKS * 7 + 3)
+        quant(2)
+        widen(BLOCKS * 7 + 3, BLOCKS * 7 + 9)
+        widen_basis(5)
+        widen(BLOCKS * 7 + 9, BLOCKS * 8)
+        empty(3)
+        turn(4)
+        multiply(2)
+        quant(3)
+        empty(4)
+        turn(5)
+        widen(BLOCKS * 8, BLOCKS * 8 + 4)
+        quant(4)
+        widen(BLOCKS * 8 + 4, BLOCKS * 8 + 8)
+        empty(5)
+        turn(6)
+        multiply(3)
+        multiply(4)
+        quant(5)
+        done = BLOCKS * 8 + 8
+
+        for s in range(LEAD + ROW_TILES, last_run_step + 1):
             j = s - PASSES
             load_until(j + LOAD_AHEAD)
             if j >= 0 and j % 3 == 2:
@@ -291,15 +365,18 @@ def tile_galore_projected_step_d2_kernel(tc, grad_bytes, grad_scale, basis_bytes
                 out_of_psum(s, h)
             if s > last_run_step:
                 momentum_and_store(s - 6)
-            widen(widened_by(s - 1), widened_by(s))
+            if s == LEAD + ROW_TILES:
+                cast(s + 3)
+            widen(done, widened_by(s))
+            done = widened_by(s)
             cast(s + 3)
             if min(run_step) <= s < last_run_step - 1:
                 cast(s + 4)
             turn(s + 1, (1, 0) if s + 1 < LEAD else (0, 1))
             if s == LEAD + ROW_TILES:
                 nc.scalar.copy(out=lr_f[:], in_=lr_raw[:])
-            if s - 1 in run_step:
-                step_and_store(run_step[s - 1] + 1)
+            if s - 2 in run_step:
+                step_and_store(run_step[s - 2] + 1)
             if s - 1 == last_run_step:
                 step_and_store(in_runs - 1)
             if s - 7 >= in_runs and s - 7 not in step:
@@ -312,26 +389,64 @@ def tile_galore_projected_step_d2_kernel(tc, grad_bytes, grad_scale, basis_bytes
                     stepped(i - 1, "gpsimd")
                 momentum(i)
                 stepped(i, "gpsimd")
+                store(step, step_rows, i)
                 momentum(i + 1)
                 momentum_and_store(i + 2)
             quant(s)
             if s >= 1:
                 multiply(s - 1)
 
-        s = last_unit
         last = TILES - 1
-        out_of_psum(s, 0)
-        momentum_and_store(last - 2)
-        quant(s, slice(0, 2 * P))
-        out_of_psum(s, 1)
-        step_and_store(last - 2)
-        quant(s, slice(2 * P, PASSES * P))
-        multiply(s - 1)
-        momentum_and_store(last - 1)
-        for passes in ((0, 1), (2, 3)):
-            for c in HALVES:
-                product(last, c, True, passes)
-        step_and_store(last - 1)
+        empty(30)
+        whole(32)
+        cast(33)
+        turn(31)
+        multiply(29)
+        quant(30)
+        empty(31)
+        step_and_store(22)
+        whole(33)
+        cast(34)
+        turn(32)
+        multiply(30)
+        quant(31)
+        multiply(31)
+        step_and_store(23, "gpsimd")
+        momentum_and_store(24)
+        step_and_store(24, "gpsimd")
+        momentum_and_store(25)
+        momentum_and_store(26)
+        empty(32)
+        cast(35)
+        turn(33)
+        whole(34)
+        step_and_store(25)
+        quant(32)
+        empty(33)
+        momentum_and_store(27)
+        step_and_store(26)
+        turn(34)
+        multiply(32)
+        whole(35)
+        quant(33)
+        empty(34)
+        momentum_and_store(28)
+        step_and_store(27)
+        turn(35)
+        multiply(33)
+        quant(34)
+        out_of_psum(35, 0)
+        step_and_store(28)
+        out_of_psum(35, 1)
+        quant(35, slice(0, 2 * P))
+        momentum_and_store(29)
+        step_and_store(29)
+        quant(35, slice(2 * P, PASSES * P))
+        multiply(34)
+        momentum_and_store(30)
+        for c in HALVES:
+            product(last, c, True)
+        step_and_store(30)
         for c in HALVES:
             momentum(last, c)
             stepped(last, "scalar", c)

@@ -27,12 +27,15 @@ RUN = 3
 RUNS = 8
 LOAD_AHEAD = 16
 FIRST_SCALES = 4
-CAST_HEAD = {0: 8, 1: 0, 2: 16, 3: 16, 4: 16, 5: 16, 6: 0, 7: 0, 8: 0, 9: 6, 10: 12}
-CAST_RUN = (12,13,12)
-CAST_TAIL = 12
+CAST_HEAD = {0: 8, 1: 0, 2: 16, 3: 16, 4: 16, 5: 16, 6: 0, 7: 0, 8: 0, 9: 6, 10: 8}
+CAST_RUN = (8, 7)
+CAST_TAIL = {33: 4, 34: 0, 35: 0}
 HEAD_UNITS = 11
 TAIL_FROM = 33
 PAD = 64
+BASIS_ORDER = (3, 0, 1, 2)
+GATED = (26,)
+NATURAL = 12
 CATCH_UP = 33
 HALVES = (slice(0, 256), slice(256, 512))
 ALL = slice(0, RANK)
@@ -47,7 +50,7 @@ def tile_galore_projected_step_d2_kernel(tc, grad_bytes, grad_scale, basis_bytes
     step_rows = out_0.rearrange("(p i) n -> p i n", p=P)
     new_rows = out_1.rearrange("(p i) n -> p i n", p=P)
 
-    units = [("grad", i) for i in range(LEAD)] + [("basis", b) for b in range(ROW_TILES)] + [("grad", i) for i in range(LEAD, TILES)]
+    units = [("grad", i) for i in range(LEAD)] + [("basis", g) for g in BASIS_ORDER] + [("grad", i) for i in range(LEAD, TILES)]
     last_unit = len(units) - 1
     in_runs = RUN * RUNS
     run_step = {RUN * r + 8: RUN * r for r in range(RUNS)}
@@ -56,17 +59,11 @@ def tile_galore_projected_step_d2_kernel(tc, grad_bytes, grad_scale, basis_bytes
     def cast_blocks(s):
         if s in CAST_HEAD:
             return CAST_HEAD[s]
-        if s >= TAIL_FROM:
-            return CAST_TAIL
-        return CAST_RUN[s % len(CAST_RUN)]
+        if s in CAST_TAIL:
+            return CAST_TAIL[s]
+        return CAST_RUN[s // RUN % len(CAST_RUN)] if s % RUN == 0 else 0
 
-    def widened_by(s):
-        ahead = 0
-        if min(run_step) <= s < last_run_step:
-            ahead = 8 * ((s - min(run_step)) % RUN)
-        return min(BLOCKS * (s + 3) + ahead, BLOCKS * len(units))
-
-    loads = [(0, 1), (1, 1), (2, 1), (3, 1)] + [(i, RUN) for i in range(4, TILES - 4, RUN)] + [(TILES - 4, 2), (TILES - 2, 2)]
+    loads = [(0, 1), (1, 1), (2, 1), (3, 1)] + [(i, RUN) for i in range(4, TILES - 4, RUN)] + [(TILES - 4, 2), (TILES - 2, 1), (TILES - 1, 1)]
 
     with ExitStack() as ctx:
         keep = ctx.enter_context(tc.tile_pool(name="keep", bufs=1))
@@ -76,8 +73,9 @@ def tile_galore_projected_step_d2_kernel(tc, grad_bytes, grad_scale, basis_bytes
         psum_m = ctx.enter_context(tc.psum_pool(name="psum_m", bufs=4))
         ctx.enter_context(tc.manual_schedule())
 
-        by_column = keep.tile([P, ROW_TILES], F32, name="by_column")
-        nc.vector.memset(by_column[:], 0.0)
+        by_column = keep.tile([BLOCKS, ROW_TILES], F32, name="by_column")
+        by_partition = keep.tile([P, ROW_TILES, P // ROW_TILES], F32, name="by_partition")
+        nc.vector.memset(by_partition[:], 0.0)
         ident = keep.tile([P, P], F32, name="ident")
         make_identity(nc, ident[:])
 
@@ -102,7 +100,7 @@ def tile_galore_projected_step_d2_kernel(tc, grad_bytes, grad_scale, basis_bytes
                     mom_raw[4 * m + t] = mo[:, t, :]
 
         sc_first = keep.tile([P, FIRST_SCALES * BLOCKS], F32, name="sc_first")
-        nc.sync.dma_start(out=sc_first[:], in_=scale_rows[:, 0 : FIRST_SCALES * BLOCKS])
+        nc.scalar.dma_start(out=sc_first[:], in_=scale_rows[:, 0 : FIRST_SCALES * BLOCKS])
         def load_basis(g):
             braw = keep.tile([P, ROW_TILES, 512], U8, name="braw%d" % g)
             nc.sync.dma_start(out=braw[:], in_=basis_rows[:, :, 512 * g : 512 * g + 512])
@@ -110,14 +108,14 @@ def tile_galore_projected_step_d2_kernel(tc, grad_bytes, grad_scale, basis_bytes
 
         load_until(0)
         with nc.allow_non_contiguous_dma(reason="64 scales, once"):
-            nc.sync.dma_start(out=by_column[0:BLOCKS, :], in_=basis_scale.rearrange("b c -> c b"))
-        load_basis(0)
+            nc.scalar.dma_start(out=by_column[:], in_=basis_scale.rearrange("b c -> c b"))
+        load_basis(BASIS_ORDER[0])
         load_until(1)
-        load_basis(1)
+        load_basis(BASIS_ORDER[1])
         load_until(2)
-        load_basis(2)
+        load_basis(BASIS_ORDER[2])
         load_until(3)
-        load_basis(3)
+        load_basis(BASIS_ORDER[3])
         sc_rest = keep.tile([P, (TILES - FIRST_SCALES) * BLOCKS], F32, name="sc_rest")
         nc.sync.dma_start(out=sc_rest[:], in_=scale_rows[:, FIRST_SCALES * BLOCKS :])
         load_until(4)
@@ -131,7 +129,6 @@ def tile_galore_projected_step_d2_kernel(tc, grad_bytes, grad_scale, basis_bytes
         nc.scalar.activation(out=dummy[:], in_=ident[:, 0:1], func=COPY)
 
         basis_sc = keep.tile([P, BLOCKS], F32, name="basis_sc")
-        by_partition = keep.tile([P, ROW_TILES, P // ROW_TILES], F32, name="by_partition")
         lr_f = keep.tile([P, TILES], F32, name="lr_f")
         bcodes = keep.tile([P, PASSES, RANK], U32, name="bcodes", align_bytes=64)
         bscales = keep.tile([P, PASSES, RANK], U8, name="bscales", align_bytes=64)
@@ -157,28 +154,40 @@ def tile_galore_projected_step_d2_kernel(tc, grad_bytes, grad_scale, basis_bytes
                 nc.scalar.copy(out=values[:], in_=raw[units[s]][:, 0:width].bitcast(FP8))
                 plain[s] = values
 
-        def widen(first, stop):
-            for n in range(first, stop):
-                s, place = divmod(n, BLOCKS)
-                count = cast_blocks(s)
-                c = (place + count) % BLOCKS if s in (0, 8, 9) else place
-                if place == 0:
-                    dst = work.tile([P, K], BF16, name="wide", align_bytes=64, bufs=6)
-                    wide[s] = dst
+        def wide_tile(s):
+            if s not in wide:
+                dst = work.tile([P, K], BF16, name="wide", align_bytes=64, bufs=6)
+                wide[s] = dst
+            return wide[s]
+
+        def widen(s, blocks):
+            count = cast_blocks(s)
+            for c in blocks:
                 src = plain[s][:, 128 * c : 128 * c + 128] if c < count else raw[units[s]][:, 128 * c : 128 * c + 128].bitcast(FP8)
-                halves = wide[s][:, 512 * (c // 4) : 512 * (c // 4) + 512].rearrange("p (u b j) -> p b u j", u=2, j=16)
-                nc.vector.tensor_scalar(
-                    out=halves[:, 4 * (c % 4) : 4 * (c % 4) + 4],
-                    in0=src.rearrange("p (b u j) -> p b u j", u=2, j=16),
-                    scalar1=scale_of(s, c),
-                    scalar2=None,
-                    op0=MULT,
-                )
+                dst = wide_tile(s)[:, 128 * c : 128 * c + 128]
+                if c < NATURAL:
+                    halves = wide[s][:, 512 * (c // 4) : 512 * (c // 4) + 512].rearrange("p (u b j) -> p b u j", u=2, j=16)
+                    dst = halves[:, 4 * (c % 4) : 4 * (c % 4) + 4]
+                    src = src.rearrange("p (b u j) -> p b u j", u=2, j=16)
+                nc.vector.tensor_scalar(out=dst, in0=src, scalar1=scale_of(s, c), scalar2=None, op0=MULT)
+
+        def direct(s, blocks=range(NATURAL, BLOCKS)):
+            for c in blocks:
+                nc.scalar.activation(out=wide_tile(s)[:, 128 * c : 128 * c + 128], in_=raw[units[s]][:, 128 * c : 128 * c + 128].bitcast(FP8), func=COPY, scale=scale_of(s, c))
 
         def widen_basis(s):
             g = units[s][1]
-            dst = work.tile([P, K], BF16, name="wide", align_bytes=64, bufs=6)
-            wide[s] = dst
+            dst = wide_tile(s)
+            if 4 * g == NATURAL:
+                for c in range(4):
+                    nc.vector.tensor_scalar(
+                        out=dst[:].rearrange("p (j k) -> p j k", j=ROW_TILES)[:, :, 128 * c : 128 * c + 128],
+                        in0=plain[s][:].rearrange("p (j k) -> p j k", j=ROW_TILES)[:, :, 128 * c : 128 * c + 128],
+                        scalar1=basis_sc[:, 4 * g + c : 4 * g + c + 1],
+                        scalar2=None,
+                        op0=MULT,
+                    )
+                return
             src = plain[s][:].rearrange("p (j b u x) -> p j b u x", j=ROW_TILES, u=2, x=16)
             halves = dst[:].rearrange("p (j u b x) -> p j b u x", j=ROW_TILES, u=2, x=16)
             for c in range(4):
@@ -196,8 +205,9 @@ def tile_galore_projected_step_d2_kernel(tc, grad_bytes, grad_scale, basis_bytes
                 xt = psum_t.tile([P, 2, 2, P], F32, name="xt")
                 for a in range(2):
                     words = wide[s][:, 512 * (2 * h + a) : 512 * (2 * h + a) + 512].bitcast(F32)
+                    natural = 4 * (units[s][1] if units[s][0] == "basis" else 2 * h + a) == NATURAL
                     for u in range(2):
-                        nc.tensor.transpose(xt[:, a, u, :], words[:, P * u : P * u + P], ident[:])
+                        nc.tensor.transpose(xt[:, a, u, :], words[:, u : 2 * P : 2] if natural else words[:, P * u : P * u + P], ident[:])
                 bank[s, h] = xt
 
         def out_of_psum(s, h):
@@ -233,6 +243,7 @@ def tile_galore_projected_step_d2_kernel(tc, grad_bytes, grad_scale, basis_bytes
                 a = psum_m.tile([P, RANK], F32, name="a")
                 acc[key] = a
             cod, scl = codes[i]
+            order = BASIS_ORDER if i < LEAD else range(PASSES)
             for g in passes:
                 nc.tensor.matmul_mx(
                     out=acc[key][:, cols],
@@ -240,8 +251,8 @@ def tile_galore_projected_step_d2_kernel(tc, grad_bytes, grad_scale, basis_bytes
                     lhsT_scale=scl[:, P * g : P * g + P],
                     rhs=bcodes[:, g, cols].bitcast(FP8X4),
                     rhs_scale=bscales[:, g, cols],
-                    start=(g == 0),
-                    stop=(g == PASSES - 1),
+                    start=(g == order[0]),
+                    stop=(g == order[-1]),
                 )
 
         def multiply(s):
@@ -282,6 +293,9 @@ def tile_galore_projected_step_d2_kernel(tc, grad_bytes, grad_scale, basis_bytes
                 elif i == in_runs - 1:
                     sp = keep.tile([P, 1, RANK], F32, name="sp%d" % i, tag="slot%d" % (i + 6))
                     open_rows(step, i, 1, sp)
+                elif i in GATED:
+                    sp = keep.tile([P, 1, RANK], F32, name="sp%d" % i, tag="slot%d" % (i + 4))
+                    open_rows(step, i, 1, sp)
                 else:
                     sp = outs.tile([P, 1, RANK], F32, name="sp_one", bufs=4)
                     open_rows(step, i, 1, sp)
@@ -307,15 +321,15 @@ def tile_galore_projected_step_d2_kernel(tc, grad_bytes, grad_scale, basis_bytes
             out_of_psum(s, 1)
 
         def whole(s):
-            widen(BLOCKS * s, BLOCKS * s + BLOCKS)
+            widen(s, range(BLOCKS))
 
+        nc.vector.tensor_copy(out=by_partition[0:BLOCKS], in_=by_column[:].unsqueeze(2).to_broadcast([BLOCKS, ROW_TILES, P // ROW_TILES]))
+        spread = psum_m.tile([P, RANK], F32, name="a")
+        nc.tensor.transpose(spread[:, 0:P], by_partition[:].rearrange("p b r -> p (b r)"), ident[:])
         cast(0)
-        widen(0, 8)
-        nc.vector.tensor_copy(out=by_partition[:], in_=by_column[:].unsqueeze(2).to_broadcast([P, ROW_TILES, P // ROW_TILES]))
-        spread = psum_t.tile([P, 2, 2, P], F32, name="xt")
-        nc.tensor.transpose(spread[:, 0, 0, :], by_partition[:].rearrange("p b r -> p (b r)"), ident[:])
-        widen(8, BLOCKS)
-        nc.vector.tensor_copy(out=basis_sc[:], in_=spread[:, 0, 0, 0:BLOCKS])
+        widen(0, range(8, BLOCKS))
+        nc.vector.tensor_copy(out=basis_sc[:], in_=spread[:, 0:BLOCKS])
+        widen(0, range(8))
         cast(2)
         turn(0, (1, 0))
         whole(1)
@@ -335,103 +349,120 @@ def tile_galore_projected_step_d2_kernel(tc, grad_bytes, grad_scale, basis_bytes
         turn(3)
         cast(5)
         widen_basis(4)
-        widen(BLOCKS * 7, BLOCKS * 7 + 3)
+        widen(7, range(0, 3))
         quant(2)
-        widen(BLOCKS * 7 + 3, BLOCKS * 7 + 9)
+        widen(7, range(3, 9))
         widen_basis(5)
-        widen(BLOCKS * 7 + 9, BLOCKS * 8)
+        widen(7, range(9, 16))
         empty(3)
         turn(4)
         multiply(2)
         quant(3)
         empty(4)
         turn(5)
-        widen(BLOCKS * 8, BLOCKS * 8 + 4)
+        widen(8, range(0, 4))
         quant(4)
-        widen(BLOCKS * 8 + 4, BLOCKS * 8 + 8)
+        widen(8, range(4, 8))
         empty(5)
         turn(6)
         multiply(3)
+        turn(7)
         multiply(4)
         quant(5)
-        done = BLOCKS * 8 + 8
+        def product_of(s, passes):
+            product(units[s][1], ALL, passes=passes)
 
-        for s in range(LEAD + ROW_TILES, last_run_step + 1):
-            j = s - PASSES
-            load_until(j + LOAD_AHEAD)
-            if j >= 0 and j % 3 == 2:
-                load_mom(j // 3 + 2)
-            for h in (1, 0) if s < LEAD else (0, 1):
-                out_of_psum(s, h)
-            if s > last_run_step:
-                momentum_and_store(s - 6)
-            if s == LEAD + ROW_TILES:
-                cast(s + 3)
-            widen(done, widened_by(s))
-            done = widened_by(s)
-            cast(s + 3)
-            if min(run_step) <= s < last_run_step - 1:
-                cast(s + 4)
-            turn(s + 1, (1, 0) if s + 1 < LEAD else (0, 1))
-            if s == LEAD + ROW_TILES:
-                nc.scalar.copy(out=lr_f[:], in_=lr_raw[:])
-            if s - 2 in run_step:
-                step_and_store(run_step[s - 2] + 1)
-            if s - 1 == last_run_step:
-                step_and_store(in_runs - 1)
-            if s - 7 >= in_runs and s - 7 not in step:
-                step_and_store(s - 7)
-            if s >= CATCH_UP:
-                step_and_store(s - 6)
-            if s in run_step:
-                i = run_step[s]
-                if i > 0:
-                    stepped(i - 1, "gpsimd")
-                momentum(i)
-                stepped(i, "gpsimd")
-                store(step, step_rows, i)
-                momentum(i + 1)
-                momentum_and_store(i + 2)
-            quant(s)
-            if s >= 1:
-                multiply(s - 1)
+        def run_of_momentum(i):
+            if i > 0:
+                stepped(i - 1, "gpsimd")
+            momentum(i)
+            stepped(i, "gpsimd")
+            store(step, step_rows, i)
+            momentum(i + 1)
+            momentum_and_store(i + 2)
+
+        empty(6)
+        cast(9)
+        widen(8, range(8, BLOCKS))
+        multiply(5)
+        turn(8)
+        quant(6)
+        empty(7)
+        widen(9, list(range(6, NATURAL)) + list(range(6)))
+        turn(9, (0,))
+        cast(10)
+        direct(9)
+        quant(7)
+        multiply(6)
+        nc.scalar.copy(out=lr_f[:], in_=lr_raw[:])
+        out_of_psum(8, 0)
+        direct(10)
+        widen(10, list(range(8, NATURAL)) + list(range(8)))
+        product_of(7, (0, 1))
+
+        for w in sorted(run_step):
+            load_until(w - PASSES + LOAD_AHEAD + 2)
+            load_mom((w - 2) // 3)
+            turn(w + 1, (1,))
+            out_of_psum(w, 1)
+            turn(w + 2, (0,))
+            out_of_psum(w + 1, 0)
+            turn(w + 2, (1,))
+            cast(w + 4)
+            run_of_momentum(run_step[w])
+            quant(w)
+            product_of(w - 1, (2, 3))
+            product_of(w, range(PASSES))
+            out_of_psum(w + 1, 1)
+            direct(w + 3)
+            widen(w + 3, range(NATURAL))
+            widen(w + 4, range(8))
+            turn(w + 3)
+            out_of_psum(w + 2, 0)
+            if w < last_run_step:
+                turn(w + 4, (0,))
+            out_of_psum(w + 2, 1)
+            quant(w + 1)
+            direct(w + 4)
+            widen(w + 4, range(8, NATURAL))
+            if w < last_run_step:
+                direct(w + 5)
+                widen(w + 5, range(NATURAL))
+            quant(w + 2)
+            product_of(w + 1, range(PASSES))
+            if w < last_run_step:
+                product_of(w + 2, (0, 1))
+            step_and_store(run_step[w] + 1)
+            out_of_psum(w + 3, 0)
 
         last = TILES - 1
-        empty(30)
-        whole(32)
-        cast(33)
-        turn(31)
-        multiply(29)
-        quant(30)
-        empty(31)
-        step_and_store(22)
-        whole(33)
-        cast(34)
-        turn(32)
-        multiply(30)
-        quant(31)
+        turn(33)
         multiply(31)
+        out_of_psum(32, 1)
+        cast(34)
+        direct(34)
         step_and_store(23, "gpsimd")
         momentum_and_store(24)
         step_and_store(24, "gpsimd")
         momentum_and_store(25)
         momentum_and_store(26)
-        empty(32)
+        out_of_psum(33, 0)
         cast(35)
-        turn(33)
-        whole(34)
+        widen(34, range(NATURAL))
+        turn(34, (0,))
         step_and_store(25)
         quant(32)
-        empty(33)
+        out_of_psum(33, 1)
+        turn(34, (1,))
+        direct(35)
+        step_and_store(26, "gpsimd")
         momentum_and_store(27)
-        step_and_store(26)
-        turn(34)
+        step_and_store(27)
         multiply(32)
-        whole(35)
+        widen(35, range(NATURAL))
         quant(33)
         empty(34)
         momentum_and_store(28)
-        step_and_store(27)
         turn(35)
         multiply(33)
         quant(34)
@@ -440,15 +471,16 @@ def tile_galore_projected_step_d2_kernel(tc, grad_bytes, grad_scale, basis_bytes
         out_of_psum(35, 1)
         quant(35, slice(0, 2 * P))
         momentum_and_store(29)
-        step_and_store(29)
         quant(35, slice(2 * P, PASSES * P))
+        step_and_store(29, "vector")
         multiply(34)
         momentum_and_store(30)
         for c in HALVES:
             product(last, c, True)
-        step_and_store(30)
         for c in HALVES:
             momentum(last, c)
+            if c.start == 0:
+                step_and_store(30, "vector")
             stepped(last, "scalar", c)
         store(new, new_rows, last)
         store(step, step_rows, last)

@@ -100,7 +100,7 @@ def tile_galore_projected_step_d2_kernel(tc, grad_bytes, grad_scale, basis_bytes
                     mom_raw[4 * m + t] = mo[:, t, :]
 
         sc_first = keep.tile([P, FIRST_SCALES * BLOCKS], F32, name="sc_first")
-        nc.scalar.dma_start(out=sc_first[:], in_=scale_rows[:, 0 : FIRST_SCALES * BLOCKS])
+        nc.sync.dma_start(out=sc_first[:], in_=scale_rows[:, 0 : FIRST_SCALES * BLOCKS])
         def load_basis(g):
             braw = keep.tile([P, ROW_TILES, 512], U8, name="braw%d" % g)
             nc.sync.dma_start(out=braw[:], in_=basis_rows[:, :, 512 * g : 512 * g + 512])
@@ -108,7 +108,7 @@ def tile_galore_projected_step_d2_kernel(tc, grad_bytes, grad_scale, basis_bytes
 
         load_until(0)
         with nc.allow_non_contiguous_dma(reason="64 scales, once"):
-            nc.scalar.dma_start(out=by_column[:], in_=basis_scale.rearrange("b c -> c b"))
+            nc.sync.dma_start(out=by_column[:], in_=basis_scale.rearrange("b c -> c b"))
         load_basis(BASIS_ORDER[0])
         load_until(1)
         load_basis(BASIS_ORDER[1])
@@ -212,7 +212,7 @@ def tile_galore_projected_step_d2_kernel(tc, grad_bytes, grad_scale, basis_bytes
 
         def out_of_psum(s, h):
             if s not in group:
-                grp = work.tile([P, K], BF16, name="grp", align_bytes=64)
+                grp = work.tile([P, K], BF16, name="grp", align_bytes=64, bufs=4)
                 group[s] = grp
             if units[s][0] == "basis":
                 nc.scalar.copy(
@@ -231,8 +231,8 @@ def tile_galore_projected_step_d2_kernel(tc, grad_bytes, grad_scale, basis_bytes
                 nc.vector.quantize_mx(out=bcodes[:, n, :].bitcast(FP8X4), scales=bscales[:, n, :], in_=group[s][:])
                 return
             if n not in codes:
-                cod = work.tile([P, PASSES * P], U32, name="cod", align_bytes=64)
-                scl = work.tile([P, PASSES * P], U8, name="scl", align_bytes=64)
+                cod = work.tile([P, PASSES * P], U32, name="cod", align_bytes=64, bufs=5)
+                scl = work.tile([P, PASSES * P], U8, name="scl", align_bytes=64, bufs=5)
                 codes[n] = (cod, scl)
             cod, scl = codes[n]
             nc.vector.quantize_mx(out=cod[:, words].bitcast(FP8X4), scales=scl[:, words], in_=group[s][:, 4 * words.start : 4 * words.stop])
@@ -323,16 +323,18 @@ def tile_galore_projected_step_d2_kernel(tc, grad_bytes, grad_scale, basis_bytes
         def whole(s):
             widen(s, range(BLOCKS))
 
-        nc.vector.tensor_copy(out=by_partition[0:BLOCKS], in_=by_column[:].unsqueeze(2).to_broadcast([BLOCKS, ROW_TILES, P // ROW_TILES]))
-        spread = psum_m.tile([P, RANK], F32, name="a")
-        nc.tensor.transpose(spread[:, 0:P], by_partition[:].rearrange("p b r -> p (b r)"), ident[:])
         cast(0)
         widen(0, range(8, BLOCKS))
-        nc.vector.tensor_copy(out=basis_sc[:], in_=spread[:, 0:BLOCKS])
+        turn(0, (1,))
         widen(0, range(8))
+        nc.vector.tensor_copy(out=by_partition[0:BLOCKS], in_=by_column[:].unsqueeze(2).to_broadcast([BLOCKS, ROW_TILES, P // ROW_TILES]))
+        turn(0, (0,))
+        spread = psum_m.tile([P, RANK], F32, name="a")
+        nc.tensor.transpose(spread[:, 0:P], by_partition[:].rearrange("p b r -> p (b r)"), ident[:])
         cast(2)
-        turn(0, (1, 0))
-        whole(1)
+        widen(1, range(12))
+        nc.vector.tensor_copy(out=basis_sc[:], in_=spread[:, 0:BLOCKS])
+        widen(1, range(12, BLOCKS))
         out_of_psum(0, 1)
         out_of_psum(0, 0)
         turn(1)

@@ -34,7 +34,7 @@ HEAD_UNITS = 11
 TAIL_FROM = 33
 PAD = 64
 BASIS_ORDER = (3, 0, 1, 2)
-GATED = (26,)
+GATED = {23: 28, 24: 29, 26: 30}
 NATURAL = 12
 CATCH_UP = 33
 HALVES = (slice(0, 256), slice(256, 512))
@@ -63,7 +63,7 @@ def tile_galore_projected_step_d2_kernel(tc, grad_bytes, grad_scale, basis_bytes
             return CAST_TAIL[s]
         return CAST_RUN[s // RUN % len(CAST_RUN)] if s % RUN == 0 else 0
 
-    loads = [(0, 1), (1, 1), (2, 1), (3, 1)] + [(i, RUN) for i in range(4, TILES - 4, RUN)] + [(TILES - 4, 2), (TILES - 2, 1), (TILES - 1, 1)]
+    loads = [(0, 1), (1, 1), (2, 1), (3, 1)] + [(i, RUN) for i in range(4, TILES - 4, RUN)] + [(i, 1) for i in range(TILES - 4, TILES)]
 
     with ExitStack() as ctx:
         keep = ctx.enter_context(tc.tile_pool(name="keep", bufs=1))
@@ -290,11 +290,8 @@ def tile_galore_projected_step_d2_kernel(tc, grad_bytes, grad_scale, basis_bytes
                 elif i < in_runs - 2:
                     sp = keep.tile([P, RUN, RANK], F32, name="sp%d" % i, tag="slot%d" % (i + 7))
                     open_rows(step, i, RUN if i < in_runs - 4 else RUN - 1, sp)
-                elif i == in_runs - 1:
-                    sp = keep.tile([P, 1, RANK], F32, name="sp%d" % i, tag="slot%d" % (i + 6))
-                    open_rows(step, i, 1, sp)
                 elif i in GATED:
-                    sp = keep.tile([P, 1, RANK], F32, name="sp%d" % i, tag="slot%d" % (i + 4))
+                    sp = keep.tile([P, 1, RANK], F32, name="sp%d" % i, tag="slot%d" % GATED[i])
                     open_rows(step, i, 1, sp)
                 else:
                     sp = outs.tile([P, 1, RANK], F32, name="sp_one", bufs=4)
@@ -425,6 +422,8 @@ def tile_galore_projected_step_d2_kernel(tc, grad_bytes, grad_scale, basis_bytes
                 turn(w + 4, (0,))
             out_of_psum(w + 2, 1)
             quant(w + 1)
+            if w == last_run_step:
+                break
             direct(w + 4)
             widen(w + 4, range(8, NATURAL))
             if w < last_run_step:
@@ -438,21 +437,27 @@ def tile_galore_projected_step_d2_kernel(tc, grad_bytes, grad_scale, basis_bytes
             out_of_psum(w + 3, 0)
 
         last = TILES - 1
+        multiply(30)
+        direct(33)
+        stepped(22, "scalar")
+        step_and_store(23, "gpsimd")
+        momentum_and_store(24)
+        momentum_and_store(25)
+        store(step, step_rows, 22)
+        out_of_psum(32, 0)
+        widen(33, range(8, NATURAL))
+        quant(31)
         turn(33)
         multiply(31)
         out_of_psum(32, 1)
-        cast(34)
         direct(34)
-        step_and_store(23, "gpsimd")
-        momentum_and_store(24)
         step_and_store(24, "gpsimd")
-        momentum_and_store(25)
         momentum_and_store(26)
+        step_and_store(25)
         out_of_psum(33, 0)
         cast(35)
         widen(34, range(NATURAL))
         turn(34, (0,))
-        step_and_store(25)
         quant(32)
         out_of_psum(33, 1)
         turn(34, (1,))
@@ -466,23 +471,34 @@ def tile_galore_projected_step_d2_kernel(tc, grad_bytes, grad_scale, basis_bytes
         empty(34)
         momentum_and_store(28)
         turn(35)
-        multiply(33)
+        product(29, HALVES[0], True)
+        product(29, HALVES[1], True)
         quant(34)
         out_of_psum(35, 0)
-        step_and_store(28)
+        stepped(28, "scalar", ALL)
+        store(step, step_rows, 28, ALL)
         out_of_psum(35, 1)
+        momentum(29, HALVES[0])
         quant(35, slice(0, 2 * P))
-        momentum_and_store(29)
+        momentum(29, HALVES[1])
+        store(new, new_rows, 29, ALL)
+        stepped(29, "scalar", HALVES[0])
+        stepped(29, "scalar", HALVES[1])
+        store(step, step_rows, 29, ALL)
         quant(35, slice(2 * P, PASSES * P))
-        step_and_store(29, "vector")
-        multiply(34)
-        momentum_and_store(30)
-        for c in HALVES:
-            product(last, c, True)
-        for c in HALVES:
-            momentum(last, c)
-            if c.start == 0:
-                step_and_store(30, "vector")
-            stepped(last, "scalar", c)
-        store(new, new_rows, last)
-        store(step, step_rows, last)
+        product(30, HALVES[0], True)
+        product(30, HALVES[1], True)
+        product(31, HALVES[0], True)
+        product(31, HALVES[1], True)
+        momentum(30, HALVES[0])
+        momentum(30, HALVES[1])
+        store(new, new_rows, 30, ALL)
+        stepped(30, "scalar", HALVES[0])
+        stepped(30, "scalar", HALVES[1])
+        store(step, step_rows, 30, ALL)
+        momentum(31, HALVES[0])
+        stepped(31, "scalar", HALVES[0])
+        momentum(31, HALVES[1])
+        store(new, new_rows, 31, ALL)
+        stepped(31, "scalar", HALVES[1])
+        store(step, step_rows, 31, ALL)

@@ -6,9 +6,12 @@ from concourse.masks import make_identity
 TOKENS, K, RANK = 4096, 2048, 512
 P = 128
 TILES = TOKENS // P
-PASSES = K // 512
-BLOCKS = K // 128
-ROW_TILES = RANK // P
+PASS = 512
+PASSES = K // PASS
+BLOCK = 128
+BLOCKS = K // BLOCK
+PASS_BLOCKS = PASS // BLOCK
+ROWS = RANK // P
 BETA = 0.9
 FLOPS = 2 * TOKENS * K * RANK
 
@@ -22,22 +25,19 @@ MULT = mybir.AluOpType.mult
 ADD = mybir.AluOpType.add
 COPY = mybir.ActivationFunctionType.Copy
 
+IN_ORDER = PASSES - 1
+BASIS_ORDER = (IN_ORDER, 0, 1, 2)
 LEAD = 2
 RUN = 3
-RUNS = 8
-LOAD_AHEAD = 16
-FIRST_SCALES = 4
-CAST_HEAD = {0: 8, 1: 0, 2: 16, 3: 16, 4: 16, 5: 16, 6: 0, 7: 0, 8: 0, 9: 6, 10: 8}
-CAST_RUN = (8, 7)
-CAST_TAIL = {33: 4, 34: 0, 35: 0}
-HEAD_UNITS = 11
-TAIL_FROM = 33
+IN_RUNS = 24
+IN_HALVES = 3
+SINGLE_LOADS = 4
+PRELOAD = 16
+MOM_TILES = 4
 PAD = 64
-BASIS_ORDER = (3, 0, 1, 2)
-GATED = {23: 28, 24: 29, 26: 30}
-NATURAL = 12
-CATCH_UP = 33
-HALVES = (slice(0, 256), slice(256, 512))
+CAST_PASSES = {0: 2, 5: 1, 6: 2, TILES - 3: 1}
+CAST_PASSES_IN_RUNS = 2
+HALVES = (slice(0, RANK // 2), slice(RANK // 2, RANK))
 ALL = slice(0, RANK)
 
 
@@ -50,455 +50,407 @@ def tile_galore_projected_step_d2_kernel(tc, grad_bytes, grad_scale, basis_bytes
     step_rows = out_0.rearrange("(p i) n -> p i n", p=P)
     new_rows = out_1.rearrange("(p i) n -> p i n", p=P)
 
-    units = [("grad", i) for i in range(LEAD)] + [("basis", g) for g in BASIS_ORDER] + [("grad", i) for i in range(LEAD, TILES)]
-    last_unit = len(units) - 1
-    in_runs = RUN * RUNS
-    run_step = {RUN * r + 8: RUN * r for r in range(RUNS)}
-    last_run_step = max(run_step)
-
-    def cast_blocks(s):
-        if s in CAST_HEAD:
-            return CAST_HEAD[s]
-        if s in CAST_TAIL:
-            return CAST_TAIL[s]
-        return CAST_RUN[s // RUN % len(CAST_RUN)] if s % RUN == 0 else 0
-
-    loads = [(0, 1), (1, 1), (2, 1), (3, 1)] + [(i, RUN) for i in range(4, TILES - 4, RUN)] + [(i, 1) for i in range(TILES - 4, TILES)]
+    loads = [(i, 1) for i in range(SINGLE_LOADS)]
+    loads.extend((i, RUN) for i in range(SINGLE_LOADS, TILES - SINGLE_LOADS, RUN))
+    loads.extend((i, 1) for i in range(TILES - SINGLE_LOADS, TILES))
 
     with ExitStack() as ctx:
         keep = ctx.enter_context(tc.tile_pool(name="keep", bufs=1))
-        work = ctx.enter_context(tc.tile_pool(name="work", bufs=3))
-        outs = ctx.enter_context(tc.tile_pool(name="outs", bufs=3))
+        work = ctx.enter_context(tc.tile_pool(name="work", bufs=4))
         psum_t = ctx.enter_context(tc.psum_pool(name="psum_t", bufs=4))
         psum_m = ctx.enter_context(tc.psum_pool(name="psum_m", bufs=4))
         ctx.enter_context(tc.manual_schedule())
 
-        by_column = keep.tile([BLOCKS, ROW_TILES], F32, name="by_column")
-        by_partition = keep.tile([P, ROW_TILES, P // ROW_TILES], F32, name="by_partition")
+        raw = {}
+        cast_values = {}
+        scaled = {}
+        banks = {}
+        turned = {}
+        codes = {}
+        sums = {}
+        mom_raw = {}
+        new = {}
+        step = {}
+
+        by_column = keep.tile([BLOCKS, ROWS], F32, name="by_column")
+        by_partition = keep.tile([P, ROWS, P // ROWS], F32, name="by_partition")
         nc.vector.memset(by_partition[:], 0.0)
         ident = keep.tile([P, P], F32, name="ident")
         make_identity(nc, ident[:])
 
-        raw = {}
-        mom_raw = {}
+        def load_grad(upto):
+            while loads and loads[0][0] <= upto:
+                first, count = loads.pop(0)
+                g = keep.tile([P, count, K + PAD], U8, name="g%d" % first, tag="bytes%d" % (first + count - 1))
+                nc.sync.dma_start(out=g[:, :, 0:K], in_=grad_rows[:, first : first + count, :])
+                for t in range(count):
+                    raw[first + t] = g[:, t, 0:K]
 
-        def load_grad(first, count):
-            g = keep.tile([P, count, K + PAD], U8, name="g%d" % first, tag="slot%d" % (first + count - 1))
-            nc.sync.dma_start(out=g[:, :, 0:K], in_=grad_rows[:, first : first + count, :])
-            for t in range(count):
-                raw["grad", first + t] = g[:, t, 0:K]
-
-        def load_until(tile):
-            while loads and loads[0][0] <= tile:
-                load_grad(*loads.pop(0))
+        def load_basis(g):
+            b = keep.tile([P, ROWS, PASS], U8, name="basis%d" % g)
+            nc.sync.dma_start(out=b[:], in_=basis_rows[:, :, PASS * g : PASS * g + PASS])
+            raw["basis", g] = b[:].rearrange("p j k -> p (j k)")
 
         def load_mom(m):
-            if m < TILES // 4:
-                mo = keep.tile([P, 4, RANK], BF16, name="mo%d" % m)
-                nc.sync.dma_start(out=mo[:], in_=mom_rows[:, 4 * m : 4 * m + 4, :])
-                for t in range(4):
-                    mom_raw[4 * m + t] = mo[:, t, :]
+            if m < TILES // MOM_TILES:
+                mo = keep.tile([P, MOM_TILES, RANK], BF16, name="mom%d" % m)
+                nc.sync.dma_start(out=mo[:], in_=mom_rows[:, MOM_TILES * m : MOM_TILES * m + MOM_TILES, :])
+                for t in range(MOM_TILES):
+                    mom_raw[MOM_TILES * m + t] = mo[:, t, :]
 
-        sc_first = keep.tile([P, FIRST_SCALES * BLOCKS], F32, name="sc_first")
-        nc.sync.dma_start(out=sc_first[:], in_=scale_rows[:, 0 : FIRST_SCALES * BLOCKS])
-        def load_basis(g):
-            braw = keep.tile([P, ROW_TILES, 512], U8, name="braw%d" % g)
-            nc.sync.dma_start(out=braw[:], in_=basis_rows[:, :, 512 * g : 512 * g + 512])
-            raw["basis", g] = braw[:].rearrange("p j k -> p (j k)")
-
-        load_until(0)
-        with nc.allow_non_contiguous_dma(reason="64 scales, once"):
+        first_scales = keep.tile([P, SINGLE_LOADS * BLOCKS], F32, name="first_scales")
+        nc.sync.dma_start(out=first_scales[:], in_=scale_rows[:, 0 : SINGLE_LOADS * BLOCKS])
+        load_grad(0)
+        with nc.allow_non_contiguous_dma(reason="the 64 basis scales, a column block to a partition"):
             nc.sync.dma_start(out=by_column[:], in_=basis_scale.rearrange("b c -> c b"))
-        load_basis(BASIS_ORDER[0])
-        load_until(1)
-        load_basis(BASIS_ORDER[1])
-        load_until(2)
-        load_basis(BASIS_ORDER[2])
-        load_until(3)
-        load_basis(BASIS_ORDER[3])
-        sc_rest = keep.tile([P, (TILES - FIRST_SCALES) * BLOCKS], F32, name="sc_rest")
-        nc.sync.dma_start(out=sc_rest[:], in_=scale_rows[:, FIRST_SCALES * BLOCKS :])
-        load_until(4)
+        for n, g in enumerate(BASIS_ORDER):
+            load_grad(n)
+            load_basis(g)
+        other_scales = keep.tile([P, (TILES - SINGLE_LOADS) * BLOCKS], F32, name="other_scales")
+        nc.sync.dma_start(out=other_scales[:], in_=scale_rows[:, SINGLE_LOADS * BLOCKS :])
+        load_grad(SINGLE_LOADS)
         load_mom(0)
         lr_raw = keep.tile([P, TILES], BF16, name="lr_raw")
         nc.sync.dma_start(out=lr_raw[:], in_=lr.rearrange("(p i) -> p i", p=P))
-        load_until(LOAD_AHEAD)
+        load_grad(PRELOAD)
         load_mom(1)
 
-        dummy = keep.tile([P, 1], F32, name="dummy")
-        nc.scalar.activation(out=dummy[:], in_=ident[:, 0:1], func=COPY)
+        warm_up = keep.tile([P, 1], F32, name="warm_up")
+        nc.scalar.activation(out=warm_up[:], in_=ident[:, 0:1], func=COPY)
 
         basis_sc = keep.tile([P, BLOCKS], F32, name="basis_sc")
         lr_f = keep.tile([P, TILES], F32, name="lr_f")
-        bcodes = keep.tile([P, PASSES, RANK], U32, name="bcodes", align_bytes=64)
-        bscales = keep.tile([P, PASSES, RANK], U8, name="bscales", align_bytes=64)
+        basis_codes = keep.tile([P, PASSES, RANK], U32, name="basis_codes", align_bytes=64)
+        basis_mx_scales = keep.tile([P, PASSES, RANK], U8, name="basis_mx_scales", align_bytes=64)
 
-        plain = {}
-        wide = {}
-        bank = {}
-        group = {}
-        codes = {}
-        acc = {}
-        new = {}
-        step = {}
+        def columns(c):
+            return slice(BLOCK * c, BLOCK * c + BLOCK)
 
-        def scale_of(s, c):
-            kind, n = units[s]
-            sc, first = (sc_first, 0) if n < FIRST_SCALES else (sc_rest, FIRST_SCALES)
-            return sc[:, BLOCKS * (n - first) + c : BLOCKS * (n - first) + c + 1]
+        def scale_of(i, c):
+            tile, first = (first_scales, 0) if i < SINGLE_LOADS else (other_scales, SINGLE_LOADS)
+            return tile[:, BLOCKS * (i - first) + c : BLOCKS * (i - first) + c + 1]
 
-        def cast(s):
-            if s <= last_unit and s not in plain and cast_blocks(s):
-                width = 128 * cast_blocks(s)
-                values = work.tile([P, width], BF16, name="values", align_bytes=64, bufs=4)
-                nc.scalar.copy(out=values[:], in_=raw[units[s]][:, 0:width].bitcast(FP8))
-                plain[s] = values
+        def cast(key, passes):
+            values = work.tile([P, PASS * passes], BF16, name="values", align_bytes=64)
+            nc.scalar.copy(out=values[:], in_=raw[key][:, 0 : PASS * passes].bitcast(FP8))
+            cast_values[key] = (values, PASS_BLOCKS * passes)
 
-        def wide_tile(s):
-            if s not in wide:
-                dst = work.tile([P, K], BF16, name="wide", align_bytes=64, bufs=6)
-                wide[s] = dst
-            return wide[s]
+        def scaled_tile(key):
+            if key not in scaled:
+                dst = work.tile([P, K], BF16, name="scaled", align_bytes=64, bufs=6)
+                scaled[key] = dst
+            return scaled[key]
 
-        def widen(s, blocks):
-            count = cast_blocks(s)
-            for c in blocks:
-                src = plain[s][:, 128 * c : 128 * c + 128] if c < count else raw[units[s]][:, 128 * c : 128 * c + 128].bitcast(FP8)
-                dst = wide_tile(s)[:, 128 * c : 128 * c + 128]
-                if c < NATURAL:
-                    halves = wide[s][:, 512 * (c // 4) : 512 * (c // 4) + 512].rearrange("p (u b j) -> p b u j", u=2, j=16)
-                    dst = halves[:, 4 * (c % 4) : 4 * (c % 4) + 4]
-                    src = src.rearrange("p (b u j) -> p b u j", u=2, j=16)
-                nc.vector.tensor_scalar(out=dst, in0=src, scalar1=scale_of(s, c), scalar2=None, op0=MULT)
+        def scale_on_vector(i, *passes):
+            values, cast_blocks = cast_values.get(i, (None, 0))
+            for g in passes:
+                for c in range(PASS_BLOCKS * g, PASS_BLOCKS * g + PASS_BLOCKS):
+                    src = values[:, columns(c)] if c < cast_blocks else raw[i][:, columns(c)].bitcast(FP8)
+                    dst = scaled_tile(i)[:, columns(c)]
+                    if g != IN_ORDER:
+                        halves = scaled[i][:, PASS * g : PASS * g + PASS].rearrange("p (u b j) -> p b u j", u=2, j=16)
+                        dst = halves[:, 4 * (c % PASS_BLOCKS) : 4 * (c % PASS_BLOCKS) + 4]
+                        src = src.rearrange("p (b u j) -> p b u j", u=2, j=16)
+                    nc.vector.tensor_scalar(out=dst, in0=src, scalar1=scale_of(i, c), scalar2=None, op0=MULT)
 
-        def direct(s, blocks=range(NATURAL, BLOCKS)):
-            for c in blocks:
-                nc.scalar.activation(out=wide_tile(s)[:, 128 * c : 128 * c + 128], in_=raw[units[s]][:, 128 * c : 128 * c + 128].bitcast(FP8), func=COPY, scale=scale_of(s, c))
+        def scale_on_scalar(i):
+            for c in range(PASS_BLOCKS * IN_ORDER, BLOCKS):
+                nc.scalar.activation(out=scaled_tile(i)[:, columns(c)], in_=raw[i][:, columns(c)].bitcast(FP8), func=COPY, scale=scale_of(i, c))
 
-        def widen_basis(s):
-            g = units[s][1]
-            dst = wide_tile(s)
-            if 4 * g == NATURAL:
-                for c in range(4):
-                    nc.vector.tensor_scalar(
-                        out=dst[:].rearrange("p (j k) -> p j k", j=ROW_TILES)[:, :, 128 * c : 128 * c + 128],
-                        in0=plain[s][:].rearrange("p (j k) -> p j k", j=ROW_TILES)[:, :, 128 * c : 128 * c + 128],
-                        scalar1=basis_sc[:, 4 * g + c : 4 * g + c + 1],
-                        scalar2=None,
-                        op0=MULT,
-                    )
-                return
-            src = plain[s][:].rearrange("p (j b u x) -> p j b u x", j=ROW_TILES, u=2, x=16)
-            halves = dst[:].rearrange("p (j u b x) -> p j b u x", j=ROW_TILES, u=2, x=16)
-            for c in range(4):
-                for u in range(2):
-                    nc.vector.tensor_scalar(
-                        out=halves[:, :, 4 * c : 4 * c + 4, u, :],
-                        in0=src[:, :, 4 * c : 4 * c + 4, u, :],
-                        scalar1=basis_sc[:, 4 * g + c : 4 * g + c + 1],
-                        scalar2=None,
-                        op0=MULT,
-                    )
+        def scale_basis(g):
+            src, dst = cast_values["basis", g][0][:], scaled_tile(("basis", g))[:]
+            for c in range(PASS_BLOCKS):
+                scale = basis_sc[:, PASS_BLOCKS * g + c : PASS_BLOCKS * g + c + 1]
+                if g == IN_ORDER:
+                    pieces = [[x.rearrange("p (j k) -> p j k", j=ROWS)[:, :, columns(c)] for x in (dst, src)]]
+                else:
+                    to = dst.rearrange("p (j u b x) -> p j b u x", j=ROWS, u=2, x=16)
+                    of = src.rearrange("p (j b u x) -> p j b u x", j=ROWS, u=2, x=16)
+                    pieces = [[x[:, :, 4 * c : 4 * c + 4, u, :] for x in (to, of)] for u in range(2)]
+                for out, in0 in pieces:
+                    nc.vector.tensor_scalar(out=out, in0=in0, scalar1=scale, scalar2=None, op0=MULT)
 
-        def turn(s, sides=(0, 1)):
+        def turn(key, *sides):
             for h in sides:
-                xt = psum_t.tile([P, 2, 2, P], F32, name="xt")
+                bank = psum_t.tile([P, 2, 2, P], F32, name="bank")
                 for a in range(2):
-                    words = wide[s][:, 512 * (2 * h + a) : 512 * (2 * h + a) + 512].bitcast(F32)
-                    natural = 4 * (units[s][1] if units[s][0] == "basis" else 2 * h + a) == NATURAL
+                    words = scaled[key][:, PASS * (2 * h + a) : PASS * (2 * h + a) + PASS].bitcast(F32)
+                    g = key[1] if isinstance(key, tuple) else 2 * h + a
                     for u in range(2):
-                        nc.tensor.transpose(xt[:, a, u, :], words[:, u : 2 * P : 2] if natural else words[:, P * u : P * u + P], ident[:])
-                bank[s, h] = xt
+                        nc.tensor.transpose(bank[:, a, u, :], words[:, u : 2 * P : 2] if g == IN_ORDER else words[:, P * u : P * u + P], ident[:])
+                banks[key, h] = bank
 
-        def out_of_psum(s, h):
-            if s not in group:
-                grp = work.tile([P, K], BF16, name="grp", align_bytes=64, bufs=4)
-                group[s] = grp
-            if units[s][0] == "basis":
-                nc.scalar.copy(
-                    out=group[s][:].bitcast(F32).rearrange("p (r j u) -> p r j u", j=ROW_TILES, u=2)[:, :, 2 * h : 2 * h + 2, :],
-                    in_=bank[s, h][:].rearrange("p a u r -> p r a u"),
-                )
-                return
-            nc.scalar.copy(
-                out=group[s][:, 1024 * h : 1024 * h + 1024].bitcast(F32).rearrange("p (a r u) -> p a r u", a=2, u=2),
-                in_=bank[s, h][:].rearrange("p a u r -> p a r u"),
-            )
+        def empty(key, *sides):
+            if key not in turned:
+                dst = work.tile([P, K], BF16, name="turned", align_bytes=64)
+                turned[key] = dst
+            for h in sides:
+                words = turned[key][:].bitcast(F32)
+                if isinstance(key, tuple):
+                    out = words.rearrange("p (r j u) -> p r j u", j=ROWS, u=2)[:, :, 2 * h : 2 * h + 2, :]
+                    nc.scalar.copy(out=out, in_=banks[key, h][:].rearrange("p a u r -> p r a u"))
+                else:
+                    out = words[:, PASS * h : PASS * h + PASS].rearrange("p (a r u) -> p a r u", a=2, u=2)
+                    nc.scalar.copy(out=out, in_=banks[key, h][:].rearrange("p a u r -> p a r u"))
 
-        def quant(s, words=slice(0, PASSES * P)):
-            kind, n = units[s]
-            if kind == "basis":
-                nc.vector.quantize_mx(out=bcodes[:, n, :].bitcast(FP8X4), scales=bscales[:, n, :], in_=group[s][:])
-                return
-            if n not in codes:
+        def quantise_basis(g):
+            nc.vector.quantize_mx(out=basis_codes[:, g, :].bitcast(FP8X4), scales=basis_mx_scales[:, g, :], in_=turned["basis", g][:])
+
+        def quantise(i, words=slice(0, PASSES * P)):
+            if i not in codes:
                 cod = work.tile([P, PASSES * P], U32, name="cod", align_bytes=64, bufs=5)
                 scl = work.tile([P, PASSES * P], U8, name="scl", align_bytes=64, bufs=5)
-                codes[n] = (cod, scl)
-            cod, scl = codes[n]
-            nc.vector.quantize_mx(out=cod[:, words].bitcast(FP8X4), scales=scl[:, words], in_=group[s][:, 4 * words.start : 4 * words.stop])
+                codes[i] = (cod, scl)
+            cod, scl = codes[i]
+            nc.vector.quantize_mx(out=cod[:, words].bitcast(FP8X4), scales=scl[:, words], in_=turned[i][:, 4 * words.start : 4 * words.stop])
 
-        def product(i, cols, own=False, passes=range(PASSES)):
-            key = (i, cols.start if own else 0)
-            if key not in acc:
-                a = psum_m.tile([P, RANK], F32, name="a")
-                acc[key] = a
+        def multiply(i, passes=range(PASSES), cols=ALL):
+            if (i, cols.start) not in sums:
+                acc = psum_m.tile([P, RANK], F32, name="acc")
+                sums[i, cols.start] = acc
             cod, scl = codes[i]
             order = BASIS_ORDER if i < LEAD else range(PASSES)
             for g in passes:
                 nc.tensor.matmul_mx(
-                    out=acc[key][:, cols],
+                    out=sums[i, cols.start][:, cols],
                     lhsT=cod[:, P * g : P * g + P].bitcast(FP8X4),
                     lhsT_scale=scl[:, P * g : P * g + P],
-                    rhs=bcodes[:, g, cols].bitcast(FP8X4),
-                    rhs_scale=bscales[:, g, cols],
+                    rhs=basis_codes[:, g, cols].bitcast(FP8X4),
+                    rhs_scale=basis_mx_scales[:, g, cols],
                     start=(g == order[0]),
                     stop=(g == order[-1]),
                 )
 
-        def multiply(s):
-            kind, n = units[s]
-            if kind == "basis":
-                for i in range(LEAD):
-                    product(i, ALL, passes=(n,))
-            elif n >= LEAD:
-                product(n, ALL)
+        def multiply_lead(g):
+            for i in range(LEAD):
+                multiply(i, (g,))
 
-        def open_rows(table, first, count, tile):
-            for t in range(count):
-                table[first + t] = (tile, first, count)
+        def multiply_in_halves(i):
+            for cols in HALVES:
+                multiply(i, cols=cols)
 
-        def store(table, rows, i, c=ALL):
-            tile, first, count = table[i]
-            if i == first + count - 1:
-                nc.sync.dma_start(out=rows[:, first : first + count, c], in_=tile[:, 0:count, c])
+        def assign(table, buffer, first, count):
+            for i in range(first, first + count):
+                table[i] = (buffer, first, count)
 
-        def momentum(i, c=ALL):
+        def store(table, rows, i):
+            buffer, first, count = table[i]
+            nc.sync.dma_start(out=rows[:, first : first + count, :], in_=buffer[:, 0:count, :])
+
+        def momentum(i, cols=ALL):
             if i not in new:
-                if i < in_runs:
-                    nw = outs.tile([P, RUN, RANK], F32, name="nw")
+                if i < IN_RUNS:
+                    buffer = work.tile([P, RUN, RANK], F32, name="new_run", bufs=3)
+                    assign(new, buffer, i, RUN)
                 else:
-                    nw = outs.tile([P, 1, RANK], F32, name="nw_one", bufs=4)
-                open_rows(new, i, RUN if i < in_runs else 1, nw)
-            tile, first, count = new[i]
-            nc.vector.scalar_tensor_tensor(out=tile[:, i - first, c], in0=mom_raw[i][:, c], scalar=BETA, in1=acc[i, c.start][:, c], op0=MULT, op1=ADD)
+                    buffer = work.tile([P, 1, RANK], F32, name="new_one")
+                    assign(new, buffer, i, 1)
+            buffer, first, count = new[i]
+            nc.vector.scalar_tensor_tensor(out=buffer[:, i - first, cols], in0=mom_raw[i][:, cols], scalar=BETA, in1=sums[i, cols.start][:, cols], op0=MULT, op1=ADD)
 
-        def stepped(i, engine, c=ALL):
+        def step_buffer(first, count, after_tile):
+            buffer = keep.tile([P, RUN if count > 1 else 1, RANK], F32, name="step%d" % first, tag="bytes%d" % after_tile)
+            assign(step, buffer, first, count)
+
+        def step_on_gpsimd(i):
+            dst, src = step[i][0][:, i - step[i][1], :], new[i][0][:, i - new[i][1], :]
+            nc.gpsimd.tensor_scalar(out=dst, in0=src, scalar1=lr_f[:, i : i + 1], scalar2=0.0, op0=MULT, op1=ADD)
+
+        def step_on_scalar(i, cols=ALL):
             if i not in step:
-                if i == 0:
-                    sp = keep.tile([P, RUN - 1, RANK], F32, name="sp0")
-                    open_rows(step, i, RUN - 1, sp)
-                elif i < in_runs - 2:
-                    sp = keep.tile([P, RUN, RANK], F32, name="sp%d" % i, tag="slot%d" % (i + 7))
-                    open_rows(step, i, RUN if i < in_runs - 4 else RUN - 1, sp)
-                elif i in GATED:
-                    sp = keep.tile([P, 1, RANK], F32, name="sp%d" % i, tag="slot%d" % GATED[i])
-                    open_rows(step, i, 1, sp)
-                else:
-                    sp = outs.tile([P, 1, RANK], F32, name="sp_one", bufs=4)
-                    open_rows(step, i, 1, sp)
-            dst = step[i][0][:, i - step[i][1], c]
-            src = new[i][0][:, i - new[i][1], c]
-            if engine == "gpsimd":
-                nc.gpsimd.tensor_scalar(out=dst, in0=src, scalar1=lr_f[:, i : i + 1], scalar2=0.0, op0=MULT, op1=ADD)
-            elif engine == "vector":
-                nc.vector.tensor_scalar(out=dst, in0=src, scalar1=lr_f[:, i : i + 1], scalar2=None, op0=MULT)
-            else:
-                nc.scalar.activation(out=dst, in_=src, func=COPY, scale=lr_f[:, i : i + 1])
+                buffer = work.tile([P, 1, RANK], F32, name="step_one")
+                assign(step, buffer, i, 1)
+            dst, src = step[i][0][:, i - step[i][1], cols], new[i][0][:, i - new[i][1], cols]
+            nc.scalar.activation(out=dst, in_=src, func=COPY, scale=lr_f[:, i : i + 1])
 
-        def step_and_store(i, engine="scalar"):
-            stepped(i, engine)
-            store(step, step_rows, i)
+        basis = [("basis", g) for g in BASIS_ORDER]
+        cast(0, CAST_PASSES[0])
+        scale_on_vector(0, 2, 3)
+        turn(0, 1)
+        scale_on_vector(0, 0, 1)
+        nc.vector.tensor_copy(out=by_partition[0:BLOCKS], in_=by_column[:].unsqueeze(2).to_broadcast([BLOCKS, ROWS, P // ROWS]))
+        turn(0, 0)
+        spread = psum_m.tile([P, RANK], F32, name="acc")
+        nc.tensor.transpose(spread[:, 0:P], by_partition[:].rearrange("p b r -> p (b r)"), ident[:])
+        cast(basis[0], ROWS)
+        scale_on_vector(1, 0, 1, 2)
+        nc.vector.tensor_copy(out=basis_sc[:], in_=spread[:, 0:BLOCKS])
+        scale_on_vector(1, 3)
+        empty(0, 1, 0)
+        turn(1, 0, 1)
+        cast(basis[1], ROWS)
+        scale_basis(BASIS_ORDER[0])
+        quantise(0)
+        empty(1, 0, 1)
+        turn(basis[0], 0, 1)
+        scale_on_vector(2, 0, 1, 2, 3)
+        cast(basis[2], ROWS)
+        scale_basis(BASIS_ORDER[1])
+        quantise(1)
+        empty(basis[0], 0, 1)
+        turn(basis[1], 0, 1)
+        cast(basis[3], ROWS)
+        scale_basis(BASIS_ORDER[2])
+        scale_on_vector(3, 0)
+        quantise_basis(BASIS_ORDER[0])
+        scale_on_vector(3, 1)
+        scale_basis(BASIS_ORDER[3])
+        scale_on_vector(3, 2, 3)
+        empty(basis[1], 0, 1)
+        turn(basis[2], 0, 1)
+        multiply_lead(BASIS_ORDER[0])
+        quantise_basis(BASIS_ORDER[1])
+        empty(basis[2], 0, 1)
+        turn(basis[3], 0, 1)
+        scale_on_vector(4, 0)
+        quantise_basis(BASIS_ORDER[2])
+        scale_on_vector(4, 1)
+        empty(basis[3], 0, 1)
+        turn(2, 0, 1)
+        multiply_lead(BASIS_ORDER[1])
+        turn(3, 0, 1)
+        multiply_lead(BASIS_ORDER[2])
+        quantise_basis(BASIS_ORDER[3])
 
-        def momentum_and_store(i):
+        empty(2, 0, 1)
+        cast(5, CAST_PASSES[5])
+        scale_on_vector(4, 2, 3)
+        multiply_lead(BASIS_ORDER[3])
+        turn(4, 0, 1)
+        quantise(2)
+        empty(3, 0, 1)
+        scale_on_vector(5, 1, 2, 0)
+        turn(5, 0)
+        cast(6, CAST_PASSES[6])
+        scale_on_scalar(5)
+        quantise(3)
+        multiply(2)
+        nc.scalar.copy(out=lr_f[:], in_=lr_raw[:])
+        empty(4, 0)
+        scale_on_scalar(6)
+        scale_on_vector(6, 2, 0, 1)
+        multiply(3, (0, 1))
+        first_steps = keep.tile([P, RUN - 1, RANK], F32, name="first_steps")
+        assign(step, first_steps, 0, RUN - 1)
+
+        for first in range(0, IN_RUNS, RUN):
+            q = first + 4
+            last_run = first + RUN == IN_RUNS
+            load_grad(q + PRELOAD + 2)
+            load_mom(first // RUN + 2)
+            turn(q + 1, 1)
+            empty(q, 1)
+            turn(q + 2, 0)
+            empty(q + 1, 0)
+            turn(q + 2, 1)
+            cast(q + 4, CAST_PASSES.get(q + 4, CAST_PASSES_IN_RUNS))
+            if first > 0:
+                step_buffer(first - 1, RUN - 1 if last_run else RUN, q + 2)
+                step_on_gpsimd(first - 1)
+            momentum(first)
+            step_on_gpsimd(first)
+            if last_run:
+                store(step, step_rows, first)
+            momentum(first + 1)
+            momentum(first + 2)
+            store(new, new_rows, first)
+            quantise(q)
+            multiply(q - 1, (2, 3))
+            multiply(q)
+            empty(q + 1, 1)
+            scale_on_scalar(q + 3)
+            scale_on_vector(q + 3, 0, 1, 2)
+            if last_run:
+                break
+            scale_on_vector(q + 4, 0, 1)
+            turn(q + 3, 0, 1)
+            empty(q + 2, 0)
+            turn(q + 4, 0)
+            empty(q + 2, 1)
+            quantise(q + 1)
+            scale_on_scalar(q + 4)
+            scale_on_vector(q + 4, 2)
+            scale_on_scalar(q + 5)
+            scale_on_vector(q + 5, 0, 1, 2)
+            quantise(q + 2)
+            multiply(q + 1)
+            multiply(q + 2, (0, 1))
+            step_on_scalar(first + 1)
+            store(step, step_rows, first + 1)
+            empty(q + 3, 0)
+
+        def finish(i):
             momentum(i)
             store(new, new_rows, i)
 
-        def empty(s):
-            out_of_psum(s, 0)
-            out_of_psum(s, 1)
-
-        def whole(s):
-            widen(s, range(BLOCKS))
-
-        cast(0)
-        widen(0, range(8, BLOCKS))
-        turn(0, (1,))
-        widen(0, range(8))
-        nc.vector.tensor_copy(out=by_partition[0:BLOCKS], in_=by_column[:].unsqueeze(2).to_broadcast([BLOCKS, ROW_TILES, P // ROW_TILES]))
-        turn(0, (0,))
-        spread = psum_m.tile([P, RANK], F32, name="a")
-        nc.tensor.transpose(spread[:, 0:P], by_partition[:].rearrange("p b r -> p (b r)"), ident[:])
-        cast(2)
-        widen(1, range(12))
-        nc.vector.tensor_copy(out=basis_sc[:], in_=spread[:, 0:BLOCKS])
-        widen(1, range(12, BLOCKS))
-        out_of_psum(0, 1)
-        out_of_psum(0, 0)
-        turn(1)
-        cast(3)
-        widen_basis(2)
-        quant(0)
-        empty(1)
-        turn(2)
-        whole(6)
-        cast(4)
-        widen_basis(3)
-        quant(1)
-        empty(2)
-        turn(3)
-        cast(5)
-        widen_basis(4)
-        widen(7, range(0, 3))
-        quant(2)
-        widen(7, range(3, 9))
-        widen_basis(5)
-        widen(7, range(9, 16))
-        empty(3)
-        turn(4)
-        multiply(2)
-        quant(3)
-        empty(4)
-        turn(5)
-        widen(8, range(0, 4))
-        quant(4)
-        widen(8, range(4, 8))
-        empty(5)
-        turn(6)
-        multiply(3)
-        turn(7)
-        multiply(4)
-        quant(5)
-        def product_of(s, passes):
-            product(units[s][1], ALL, passes=passes)
-
-        def run_of_momentum(i):
-            if i > 0:
-                stepped(i - 1, "gpsimd")
-            momentum(i)
-            stepped(i, "gpsimd")
+        def step_beside_momentum(i, after_tile):
+            step_buffer(i, 1, after_tile)
+            step_on_gpsimd(i)
             store(step, step_rows, i)
-            momentum(i + 1)
-            momentum_and_store(i + 2)
 
-        empty(6)
-        cast(9)
-        widen(8, range(8, BLOCKS))
-        multiply(5)
-        turn(8)
-        quant(6)
-        empty(7)
-        widen(9, list(range(6, NATURAL)) + list(range(6)))
-        turn(9, (0,))
-        cast(10)
-        direct(9)
-        quant(7)
-        multiply(6)
-        nc.scalar.copy(out=lr_f[:], in_=lr_raw[:])
-        out_of_psum(8, 0)
-        direct(10)
-        widen(10, list(range(8, NATURAL)) + list(range(8)))
-        product_of(7, (0, 1))
+        def step_and_store(i):
+            step_on_scalar(i)
+            store(step, step_rows, i)
 
-        for w in sorted(run_step):
-            load_until(w - PASSES + LOAD_AHEAD + 2)
-            load_mom((w - 2) // 3)
-            turn(w + 1, (1,))
-            out_of_psum(w, 1)
-            turn(w + 2, (0,))
-            out_of_psum(w + 1, 0)
-            turn(w + 2, (1,))
-            cast(w + 4)
-            run_of_momentum(run_step[w])
-            quant(w)
-            product_of(w - 1, (2, 3))
-            product_of(w, range(PASSES))
-            out_of_psum(w + 1, 1)
-            direct(w + 3)
-            widen(w + 3, range(NATURAL))
-            widen(w + 4, range(8))
-            turn(w + 3)
-            out_of_psum(w + 2, 0)
-            if w < last_run_step:
-                turn(w + 4, (0,))
-            out_of_psum(w + 2, 1)
-            quant(w + 1)
-            if w == last_run_step:
-                break
-            direct(w + 4)
-            widen(w + 4, range(8, NATURAL))
-            if w < last_run_step:
-                direct(w + 5)
-                widen(w + 5, range(NATURAL))
-            quant(w + 2)
-            product_of(w + 1, range(PASSES))
-            if w < last_run_step:
-                product_of(w + 2, (0, 1))
-            step_and_store(run_step[w] + 1)
-            out_of_psum(w + 3, 0)
-
-        last = TILES - 1
-        multiply(30)
-        direct(33)
-        stepped(22, "scalar")
-        step_and_store(23, "gpsimd")
-        momentum_and_store(24)
-        momentum_and_store(25)
+        turn(28, 0, 1)
+        empty(27, 0, 1)
+        quantise(26)
+        multiply(26)
+        scale_on_scalar(29)
+        step_on_scalar(22)
+        step_beside_momentum(23, 28)
+        finish(24)
+        finish(25)
         store(step, step_rows, 22)
-        out_of_psum(32, 0)
-        widen(33, range(8, NATURAL))
-        quant(31)
-        turn(33)
-        multiply(31)
-        out_of_psum(32, 1)
-        direct(34)
-        step_and_store(24, "gpsimd")
-        momentum_and_store(26)
+
+        empty(28, 0)
+        scale_on_vector(29, 0, 1, 2)
+        quantise(27)
+        turn(29, 0, 1)
+        multiply(27)
+        empty(28, 1)
+        scale_on_scalar(30)
+        step_beside_momentum(24, 29)
+        finish(26)
         step_and_store(25)
-        out_of_psum(33, 0)
-        cast(35)
-        widen(34, range(NATURAL))
-        turn(34, (0,))
-        quant(32)
-        out_of_psum(33, 1)
-        turn(34, (1,))
-        direct(35)
-        step_and_store(26, "gpsimd")
-        momentum_and_store(27)
+
+        empty(29, 0)
+        scale_on_vector(30, 0, 1, 2)
+        turn(30, 0)
+        quantise(28)
+        empty(29, 1)
+        turn(30, 1)
+        scale_on_scalar(31)
+        step_beside_momentum(26, 30)
+        finish(27)
         step_and_store(27)
-        multiply(32)
-        widen(35, range(NATURAL))
-        quant(33)
-        empty(34)
-        momentum_and_store(28)
-        turn(35)
-        product(29, HALVES[0], True)
-        product(29, HALVES[1], True)
-        quant(34)
-        out_of_psum(35, 0)
-        stepped(28, "scalar", ALL)
-        store(step, step_rows, 28, ALL)
-        out_of_psum(35, 1)
+        multiply(28)
+
+        scale_on_vector(31, 0, 1, 2)
+        quantise(29)
+        empty(30, 0, 1)
+        finish(28)
+        turn(31, 0, 1)
+        multiply_in_halves(29)
+        quantise(30)
+        empty(31, 0)
+        step_and_store(28)
+        empty(31, 1)
+
         momentum(29, HALVES[0])
-        quant(35, slice(0, 2 * P))
+        quantise(31, slice(0, 2 * P))
         momentum(29, HALVES[1])
-        store(new, new_rows, 29, ALL)
-        stepped(29, "scalar", HALVES[0])
-        stepped(29, "scalar", HALVES[1])
-        store(step, step_rows, 29, ALL)
-        quant(35, slice(2 * P, PASSES * P))
-        product(30, HALVES[0], True)
-        product(30, HALVES[1], True)
-        product(31, HALVES[0], True)
-        product(31, HALVES[1], True)
-        momentum(30, HALVES[0])
-        momentum(30, HALVES[1])
-        store(new, new_rows, 30, ALL)
-        stepped(30, "scalar", HALVES[0])
-        stepped(30, "scalar", HALVES[1])
-        store(step, step_rows, 30, ALL)
-        momentum(31, HALVES[0])
-        stepped(31, "scalar", HALVES[0])
-        momentum(31, HALVES[1])
-        store(new, new_rows, 31, ALL)
-        stepped(31, "scalar", HALVES[1])
-        store(step, step_rows, 31, ALL)
+        store(new, new_rows, 29)
+        for cols in HALVES:
+            step_on_scalar(29, cols)
+        store(step, step_rows, 29)
+        quantise(31, slice(2 * P, PASSES * P))
+        for i in range(TILES - IN_HALVES + 1, TILES):
+            multiply_in_halves(i)
+        for i in range(TILES - IN_HALVES + 1, TILES):
+            for cols in HALVES:
+                momentum(i, cols)
+            store(new, new_rows, i)
+            for cols in HALVES:
+                step_on_scalar(i, cols)
+            store(step, step_rows, i)

@@ -30,12 +30,11 @@ BASIS_ORDER = (IN_ORDER, 0, 1, 2)
 LEAD = 2
 RUN = 3
 IN_RUNS = 24
-IN_HALVES = 3
 SINGLE_LOADS = 4
 PRELOAD = 16
 MOM_TILES = 4
 PAD = 64
-CAST_PASSES = {0: 2, 5: 1, 6: 2, TILES - 3: 1}
+CAST_PASSES = {0: 2, 5: 2, 6: 3, TILES - 3: 1}
 CAST_PASSES_IN_RUNS = 2
 HALVES = (slice(0, RANK // 2), slice(RANK // 2, RANK))
 ALL = slice(0, RANK)
@@ -258,7 +257,7 @@ def tile_galore_projected_step_d2_kernel(tc, grad_bytes, grad_scale, basis_bytes
 
         def step_on_scalar(i, cols=ALL):
             if i not in step:
-                buffer = work.tile([P, 1, RANK], F32, name="step_one")
+                buffer = keep.tile([P, 1, RANK], F32, name="step%d" % i)
                 assign(step, buffer, i, 1)
             dst, src = step[i][0][:, i - step[i][1], cols], new[i][0][:, i - new[i][1], cols]
             nc.scalar.activation(out=dst, in_=src, func=COPY, scale=lr_f[:, i : i + 1])
@@ -319,16 +318,15 @@ def tile_galore_projected_step_d2_kernel(tc, grad_bytes, grad_scale, basis_bytes
         turn(4, 0, 1)
         quantise(2)
         empty(3, 0, 1)
-        scale_on_vector(5, 1, 2, 0)
+        scale_on_vector(5, 2, 3, 0, 1)
         turn(5, 0)
         cast(6, CAST_PASSES[6])
-        scale_on_scalar(5)
         quantise(3)
         multiply(2)
         nc.scalar.copy(out=lr_f[:], in_=lr_raw[:])
         empty(4, 0)
         scale_on_scalar(6)
-        scale_on_vector(6, 2, 0, 1)
+        scale_on_vector(6, 0, 1, 2)
         multiply(3, (0, 1))
         first_steps = keep.tile([P, RUN - 1, RANK], F32, name="first_steps")
         assign(step, first_steps, 0, RUN - 1)
@@ -445,12 +443,14 @@ def tile_galore_projected_step_d2_kernel(tc, grad_bytes, grad_scale, basis_bytes
             step_on_scalar(29, cols)
         store(step, step_rows, 29)
         quantise(31, slice(2 * P, PASSES * P))
-        for i in range(TILES - IN_HALVES + 1, TILES):
-            multiply_in_halves(i)
-        for i in range(TILES - IN_HALVES + 1, TILES):
-            for cols in HALVES:
-                momentum(i, cols)
-            store(new, new_rows, i)
-            for cols in HALVES:
-                step_on_scalar(i, cols)
-            store(step, step_rows, i)
+        multiply_in_halves(30)
+        multiply_in_halves(31)
+        for cols in HALVES:
+            momentum(30, cols)
+        store(new, new_rows, 30)
+        step_and_store(30)
+        for cols in HALVES:
+            momentum(31, cols)
+            step_on_scalar(31, cols)
+        store(new, new_rows, 31)
+        store(step, step_rows, 31)

@@ -32,7 +32,7 @@ RUN = 3
 IN_RUNS = 24
 SINGLE_LOADS = 4
 PRELOAD = 16
-MOM_TILES = 4
+MOM_TILES = 8
 PAD = 64
 CAST_PASSES = {0: 2, 5: 2, 6: 3, TILES - 3: 1}
 CAST_PASSES_IN_RUNS = 2
@@ -112,7 +112,6 @@ def tile_galore_projected_step_d2_kernel(tc, grad_bytes, grad_scale, basis_bytes
         lr_raw = keep.tile([P, TILES], BF16, name="lr_raw")
         nc.sync.dma_start(out=lr_raw[:], in_=lr.rearrange("(p i) -> p i", p=P))
         load_grad(PRELOAD)
-        load_mom(1)
 
         warm_up = keep.tile([P, 1], F32, name="warm_up")
         nc.scalar.activation(out=warm_up[:], in_=ident[:, 0:1], func=COPY)
@@ -335,7 +334,7 @@ def tile_galore_projected_step_d2_kernel(tc, grad_bytes, grad_scale, basis_bytes
             q = first + 4
             last_run = first + RUN == IN_RUNS
             load_grad(q + PRELOAD + 2)
-            load_mom(first // RUN + 2)
+            load_mom(first // RUN + 1)
             turn(q + 1, 1)
             empty(q, 1)
             turn(q + 2, 0)

@@ -34,7 +34,7 @@ SINGLE_LOADS = 4
 PRELOAD = 16
 MOM_TILES = 8
 PAD = 64
-CAST_PASSES = {0: 2, 5: 2, 6: 3, TILES - 3: 1}
+CAST_PASSES = {0: 2, 5: 1, 6: 2, TILES - 3: 1}
 CAST_PASSES_IN_RUNS = 2
 HALVES = (slice(0, RANK // 2), slice(RANK // 2, RANK))
 ALL = slice(0, RANK)
@@ -254,6 +254,12 @@ def tile_galore_projected_step_d2_kernel(tc, grad_bytes, grad_scale, basis_bytes
             dst, src = step[i][0][:, i - step[i][1], :], new[i][0][:, i - new[i][1], :]
             nc.gpsimd.tensor_scalar(out=dst, in0=src, scalar1=lr_f[:, i : i + 1], scalar2=0.0, op0=MULT, op1=ADD)
 
+        def step_on_vector(i):
+            buffer = keep.tile([P, 1, RANK], F32, name="step%d" % i)
+            assign(step, buffer, i, 1)
+            nc.vector.tensor_scalar(out=buffer[:, 0, :], in0=new[i][0][:, 0, :], scalar1=lr_f[:, i : i + 1], scalar2=None, op0=MULT)
+            store(step, step_rows, i)
+
         def step_on_scalar(i, cols=ALL):
             if i not in step:
                 buffer = keep.tile([P, 1, RANK], F32, name="step%d" % i)
@@ -317,15 +323,16 @@ def tile_galore_projected_step_d2_kernel(tc, grad_bytes, grad_scale, basis_bytes
         turn(4, 0, 1)
         quantise(2)
         empty(3, 0, 1)
-        scale_on_vector(5, 2, 3, 0, 1)
+        scale_on_vector(5, 1, 2, 0)
         turn(5, 0)
         cast(6, CAST_PASSES[6])
+        scale_on_scalar(5)
         quantise(3)
         multiply(2)
         nc.scalar.copy(out=lr_f[:], in_=lr_raw[:])
         empty(4, 0)
         scale_on_scalar(6)
-        scale_on_vector(6, 0, 1, 2)
+        scale_on_vector(6, 2, 0, 1)
         multiply(3, (0, 1))
         first_steps = keep.tile([P, RUN - 1, RANK], F32, name="first_steps")
         assign(step, first_steps, 0, RUN - 1)
@@ -428,28 +435,23 @@ def tile_galore_projected_step_d2_kernel(tc, grad_bytes, grad_scale, basis_bytes
         empty(30, 0, 1)
         finish(28)
         turn(31, 0, 1)
-        multiply_in_halves(29)
+        multiply(29)
         quantise(30)
         empty(31, 0)
         step_and_store(28)
         empty(31, 1)
 
-        momentum(29, HALVES[0])
         quantise(31, slice(0, 2 * P))
-        momentum(29, HALVES[1])
-        store(new, new_rows, 29)
-        for cols in HALVES:
-            step_on_scalar(29, cols)
-        store(step, step_rows, 29)
+        finish(29)
         quantise(31, slice(2 * P, PASSES * P))
-        multiply_in_halves(30)
+        step_on_vector(29)
+        multiply(30)
+        finish(30)
         multiply_in_halves(31)
-        for cols in HALVES:
-            momentum(30, cols)
-        store(new, new_rows, 30)
-        step_and_store(30)
-        for cols in HALVES:
-            momentum(31, cols)
-            step_on_scalar(31, cols)
+        momentum(31, HALVES[0])
+        step_on_vector(30)
+        step_on_scalar(31, HALVES[0])
+        momentum(31, HALVES[1])
+        step_on_scalar(31, HALVES[1])
         store(new, new_rows, 31)
         store(step, step_rows, 31)

@@ -260,11 +260,11 @@ def tile_galore_projected_step_d2_kernel(tc, grad_bytes, grad_scale, basis_bytes
             nc.vector.tensor_scalar(out=buffer[:, 0, :], in0=new[i][0][:, 0, :], scalar1=lr_f[:, i : i + 1], scalar2=None, op0=MULT)
             store(step, step_rows, i)
 
-        def step_on_scalar(i, cols=ALL):
+        def step_on_scalar(i):
             if i not in step:
                 buffer = keep.tile([P, 1, RANK], F32, name="step%d" % i)
                 assign(step, buffer, i, 1)
-            dst, src = step[i][0][:, i - step[i][1], cols], new[i][0][:, i - new[i][1], cols]
+            dst, src = step[i][0][:, i - step[i][1], :], new[i][0][:, i - new[i][1], :]
             nc.scalar.activation(out=dst, in_=src, func=COPY, scale=lr_f[:, i : i + 1])
 
         basis = [("basis", g) for g in BASIS_ORDER]
@@ -435,23 +435,21 @@ def tile_galore_projected_step_d2_kernel(tc, grad_bytes, grad_scale, basis_bytes
         empty(30, 0, 1)
         finish(28)
         turn(31, 0, 1)
-        multiply(29)
+        multiply_in_halves(29)
         quantise(30)
         empty(31, 0)
         step_and_store(28)
         empty(31, 1)
 
+        momentum(29, HALVES[0])
         quantise(31, slice(0, 2 * P))
-        finish(29)
+        momentum(29, HALVES[1])
+        store(new, new_rows, 29)
         quantise(31, slice(2 * P, PASSES * P))
         step_on_vector(29)
         multiply(30)
         finish(30)
-        multiply_in_halves(31)
-        momentum(31, HALVES[0])
+        multiply(31)
         step_on_vector(30)
-        step_on_scalar(31, HALVES[0])
-        momentum(31, HALVES[1])
-        step_on_scalar(31, HALVES[1])
-        store(new, new_rows, 31)
-        store(step, step_rows, 31)
+        finish(31)
+        step_on_vector(31)

@@ -33,7 +33,8 @@ IN_RUNS = 24
 SINGLE_LOADS = 4
 PRELOAD = 16
 MOM_TILES = 8
-PAD = 64
+LINE = 256
+PIECE = RUN * K // 2
 CAST_PASSES = {0: 2, 5: 1, 6: 2, TILES - 3: 1}
 CAST_PASSES_IN_RUNS = 2
 HALVES = (slice(0, RANK // 2), slice(RANK // 2, RANK))
@@ -80,19 +81,20 @@ def tile_galore_projected_step_d2_kernel(tc, grad_bytes, grad_scale, basis_bytes
         def load_grad(upto):
             while loads and loads[0][0] <= upto:
                 first, count = loads.pop(0)
-                g = keep.tile([P, count, K + PAD], U8, name="g%d" % first, tag="bytes%d" % (first + count - 1))
-                nc.sync.dma_start(out=g[:, :, 0:K], in_=grad_rows[:, first : first + count, :])
+                piece = K if count == 1 else PIECE
+                g = keep.tile([P, count * K // piece, piece + (0 if count == 1 else LINE)], U8, name="g%d" % first, tag="bytes%d" % (first + count - 1), align_bytes=LINE)
+                nc.sync.dma_start(out=g[:, :, 0:piece], in_=grad_rows[:, first : first + count, :].rearrange("p i k -> p (i k)").rearrange("p (a x) -> p a x", x=piece))
                 for t in range(count):
-                    raw[first + t] = g[:, t, 0:K]
+                    raw[first + t] = [g[:, (K * t + K // 2 * h) // piece, (K * t + K // 2 * h) % piece : (K * t + K // 2 * h) % piece + K // 2] for h in range(2)]
 
         def load_basis(g):
-            b = keep.tile([P, ROWS, PASS], U8, name="basis%d" % g)
+            b = keep.tile([P, ROWS, PASS], U8, name="basis%d" % g, tag="basis_bytes%d" % g, align_bytes=LINE)
             nc.sync.dma_start(out=b[:], in_=basis_rows[:, :, PASS * g : PASS * g + PASS])
             raw["basis", g] = b[:].rearrange("p j k -> p (j k)")
 
         def load_mom(m):
             if m < TILES // MOM_TILES:
-                mo = keep.tile([P, MOM_TILES, RANK], BF16, name="mom%d" % m)
+                mo = keep.tile([P, MOM_TILES, RANK], BF16, name="mom%d" % m, align_bytes=LINE)
                 nc.sync.dma_start(out=mo[:], in_=mom_rows[:, MOM_TILES * m : MOM_TILES * m + MOM_TILES, :])
                 for t in range(MOM_TILES):
                     mom_raw[MOM_TILES * m + t] = mo[:, t, :]
@@ -124,13 +126,16 @@ def tile_galore_projected_step_d2_kernel(tc, grad_bytes, grad_scale, basis_bytes
         def columns(c):
             return slice(BLOCK * c, BLOCK * c + BLOCK)
 
+        def block_bytes(i, c):
+            return raw[i][c // (BLOCKS // 2)][:, columns(c % (BLOCKS // 2))].bitcast(FP8)
+
         def scale_of(i, c):
             tile, first = (first_scales, 0) if i < SINGLE_LOADS else (other_scales, SINGLE_LOADS)
             return tile[:, BLOCKS * (i - first) + c : BLOCKS * (i - first) + c + 1]
 
         def cast(key, passes):
             values = work.tile([P, PASS * passes], BF16, name="values", align_bytes=64)
-            nc.scalar.copy(out=values[:], in_=raw[key][:, 0 : PASS * passes].bitcast(FP8))
+            nc.scalar.copy(out=values[:], in_=(raw[key] if isinstance(key, tuple) else raw[key][0])[:, 0 : PASS * passes].bitcast(FP8))
             cast_values[key] = (values, PASS_BLOCKS * passes)
 
         def scaled_tile(key):
@@ -143,7 +148,7 @@ def tile_galore_projected_step_d2_kernel(tc, grad_bytes, grad_scale, basis_bytes
             values, cast_blocks = cast_values.get(i, (None, 0))
             for g in passes:
                 for c in range(PASS_BLOCKS * g, PASS_BLOCKS * g + PASS_BLOCKS):
-                    src = values[:, columns(c)] if c < cast_blocks else raw[i][:, columns(c)].bitcast(FP8)
+                    src = values[:, columns(c)] if c < cast_blocks else block_bytes(i, c)
                     dst = scaled_tile(i)[:, columns(c)]
                     if g != IN_ORDER:
                         halves = scaled[i][:, PASS * g : PASS * g + PASS].rearrange("p (u b j) -> p b u j", u=2, j=16)
@@ -153,7 +158,7 @@ def tile_galore_projected_step_d2_kernel(tc, grad_bytes, grad_scale, basis_bytes
 
         def scale_on_scalar(i):
             for c in range(PASS_BLOCKS * IN_ORDER, BLOCKS):
-                nc.scalar.activation(out=scaled_tile(i)[:, columns(c)], in_=raw[i][:, columns(c)].bitcast(FP8), func=COPY, scale=scale_of(i, c))
+                nc.scalar.activation(out=scaled_tile(i)[:, columns(c)], in_=block_bytes(i, c), func=COPY, scale=scale_of(i, c))
 
         def scale_basis(g):
             src, dst = cast_values["basis", g][0][:], scaled_tile(("basis", g))[:]
@@ -238,16 +243,16 @@ def tile_galore_projected_step_d2_kernel(tc, grad_bytes, grad_scale, basis_bytes
         def momentum(i, cols=ALL):
             if i not in new:
                 if i < IN_RUNS:
-                    buffer = work.tile([P, RUN, RANK], F32, name="new_run", bufs=3)
+                    buffer = work.tile([P, RUN, RANK], F32, name="new_run", bufs=3, align_bytes=LINE)
                     assign(new, buffer, i, RUN)
                 else:
-                    buffer = work.tile([P, 1, RANK], F32, name="new_one")
+                    buffer = work.tile([P, 1, RANK], F32, name="new_one", align_bytes=LINE)
                     assign(new, buffer, i, 1)
             buffer, first, count = new[i]
             nc.vector.scalar_tensor_tensor(out=buffer[:, i - first, cols], in0=mom_raw[i][:, cols], scalar=BETA, in1=sums[i, cols.start][:, cols], op0=MULT, op1=ADD)
 
         def step_buffer(first, count, after_tile):
-            buffer = keep.tile([P, RUN if count > 1 else 1, RANK], F32, name="step%d" % first, tag="bytes%d" % after_tile)
+            buffer = keep.tile([P, RUN if count > 1 else 1, RANK], F32, name="step%d" % first, tag="bytes%d" % after_tile, align_bytes=LINE)
             assign(step, buffer, first, count)
 
         def step_on_gpsimd(i):
@@ -255,14 +260,14 @@ def tile_galore_projected_step_d2_kernel(tc, grad_bytes, grad_scale, basis_bytes
             nc.gpsimd.tensor_scalar(out=dst, in0=src, scalar1=lr_f[:, i : i + 1], scalar2=0.0, op0=MULT, op1=ADD)
 
         def step_on_vector(i):
-            buffer = keep.tile([P, 1, RANK], F32, name="step%d" % i)
+            buffer = keep.tile([P, 1, RANK], F32, name="step%d" % i, tag="bytes%d" % (i % SINGLE_LOADS), align_bytes=LINE)
             assign(step, buffer, i, 1)
             nc.vector.tensor_scalar(out=buffer[:, 0, :], in0=new[i][0][:, 0, :], scalar1=lr_f[:, i : i + 1], scalar2=None, op0=MULT)
             store(step, step_rows, i)
 
         def step_on_scalar(i):
             if i not in step:
-                buffer = keep.tile([P, 1, RANK], F32, name="step%d" % i)
+                buffer = keep.tile([P, 1, RANK], F32, name="step%d" % i, tag="basis_bytes%d" % (i % PASSES), align_bytes=LINE)
                 assign(step, buffer, i, 1)
             dst, src = step[i][0][:, i - step[i][1], :], new[i][0][:, i - new[i][1], :]
             nc.scalar.activation(out=dst, in_=src, func=COPY, scale=lr_f[:, i : i + 1])
@@ -334,7 +339,7 @@ def tile_galore_projected_step_d2_kernel(tc, grad_bytes, grad_scale, basis_bytes
         scale_on_scalar(6)
         scale_on_vector(6, 2, 0, 1)
         multiply(3, (0, 1))
-        first_steps = keep.tile([P, RUN - 1, RANK], F32, name="first_steps")
+        first_steps = keep.tile([P, RUN - 1, RANK], F32, name="first_steps", align_bytes=LINE)
         assign(step, first_steps, 0, RUN - 1)
 
         for first in range(0, IN_RUNS, RUN):

@@ -28,6 +28,7 @@ COPY = mybir.ActivationFunctionType.Copy
 IN_ORDER = PASSES - 1
 BASIS_ORDER = (IN_ORDER, 0, 1, 2)
 LEAD = 2
+SUM_BANKS = 4
 RUN = 3
 IN_RUNS = 24
 SINGLE_LOADS = 4
@@ -35,7 +36,7 @@ PRELOAD = 16
 MOM_TILES = 8
 LINE = 256
 PIECE = RUN * K // 2
-CAST_PASSES = {0: 2, 5: 1, 6: 2, TILES - 3: 1}
+CAST_PASSES = {0: 1, 1: 3, TILES - 3: 1}
 CAST_PASSES_IN_RUNS = 2
 HALVES = (slice(0, RANK // 2), slice(RANK // 2, RANK))
 ALL = slice(0, RANK)
@@ -58,10 +59,11 @@ def tile_galore_projected_step_d2_kernel(tc, grad_bytes, grad_scale, basis_bytes
         keep = ctx.enter_context(tc.tile_pool(name="keep", bufs=1))
         work = ctx.enter_context(tc.tile_pool(name="work", bufs=4))
         psum_t = ctx.enter_context(tc.psum_pool(name="psum_t", bufs=4))
-        psum_m = ctx.enter_context(tc.psum_pool(name="psum_m", bufs=4))
+        psum_m = ctx.enter_context(tc.psum_pool(name="psum_m", bufs=1))
         ctx.enter_context(tc.manual_schedule())
 
         raw = {}
+        first_bytes = {}
         cast_values = {}
         scaled = {}
         banks = {}
@@ -71,6 +73,7 @@ def tile_galore_projected_step_d2_kernel(tc, grad_bytes, grad_scale, basis_bytes
         mom_raw = {}
         new = {}
         step = {}
+        spare = ["bytes%d" % i for i in range(SINGLE_LOADS)] + ["basis_bytes%d" % g for g in range(PASSES)]
 
         by_column = keep.tile([BLOCKS, ROWS], F32, name="by_column")
         by_partition = keep.tile([P, ROWS, P // ROWS], F32, name="by_partition")
@@ -85,12 +88,13 @@ def tile_galore_projected_step_d2_kernel(tc, grad_bytes, grad_scale, basis_bytes
                 g = keep.tile([P, count * K // piece, piece + (0 if count == 1 else LINE)], U8, name="g%d" % first, tag="bytes%d" % (first + count - 1), align_bytes=LINE)
                 nc.sync.dma_start(out=g[:, :, 0:piece], in_=grad_rows[:, first : first + count, :].rearrange("p i k -> p (i k)").rearrange("p (a x) -> p a x", x=piece))
                 for t in range(count):
+                    first_bytes[first + t] = g[:, K * t // piece, K * t % piece : piece]
                     raw[first + t] = [g[:, (K * t + K // 2 * h) // piece, (K * t + K // 2 * h) % piece : (K * t + K // 2 * h) % piece + K // 2] for h in range(2)]
 
         def load_basis(g):
             b = keep.tile([P, ROWS, PASS], U8, name="basis%d" % g, tag="basis_bytes%d" % g, align_bytes=LINE)
             nc.sync.dma_start(out=b[:], in_=basis_rows[:, :, PASS * g : PASS * g + PASS])
-            raw["basis", g] = b[:].rearrange("p j k -> p (j k)")
+            first_bytes["basis", g] = b[:].rearrange("p j k -> p (j k)")
 
         def load_mom(m):
             if m < TILES // MOM_TILES:
@@ -101,11 +105,11 @@ def tile_galore_projected_step_d2_kernel(tc, grad_bytes, grad_scale, basis_bytes
 
         first_scales = keep.tile([P, SINGLE_LOADS * BLOCKS], F32, name="first_scales")
         nc.sync.dma_start(out=first_scales[:], in_=scale_rows[:, 0 : SINGLE_LOADS * BLOCKS])
-        load_grad(0)
+        load_grad(1)
         with nc.allow_non_contiguous_dma(reason="the 64 basis scales, a column block to a partition"):
             nc.sync.dma_start(out=by_column[:], in_=basis_scale.rearrange("b c -> c b"))
         for n, g in enumerate(BASIS_ORDER):
-            load_grad(n)
+            load_grad(min(n + 1, SINGLE_LOADS - 1))
             load_basis(g)
         other_scales = keep.tile([P, (TILES - SINGLE_LOADS) * BLOCKS], F32, name="other_scales")
         nc.sync.dma_start(out=other_scales[:], in_=scale_rows[:, SINGLE_LOADS * BLOCKS :])
@@ -135,12 +139,12 @@ def tile_galore_projected_step_d2_kernel(tc, grad_bytes, grad_scale, basis_bytes
 
         def cast(key, passes):
             values = work.tile([P, PASS * passes], BF16, name="values", align_bytes=64)
-            nc.scalar.copy(out=values[:], in_=(raw[key] if isinstance(key, tuple) else raw[key][0])[:, 0 : PASS * passes].bitcast(FP8))
+            nc.scalar.copy(out=values[:], in_=first_bytes[key][:, 0 : PASS * passes].bitcast(FP8))
             cast_values[key] = (values, PASS_BLOCKS * passes)
 
         def scaled_tile(key):
             if key not in scaled:
-                dst = work.tile([P, K], BF16, name="scaled", align_bytes=64, bufs=6)
+                dst = work.tile([P, K], BF16, name="scaled", align_bytes=64, bufs=7)
                 scaled[key] = dst
             return scaled[key]
 
@@ -173,10 +177,13 @@ def tile_galore_projected_step_d2_kernel(tc, grad_bytes, grad_scale, basis_bytes
                 for out, in0 in pieces:
                     nc.vector.tensor_scalar(out=out, in0=in0, scalar1=scale, scalar2=None, op0=MULT)
 
-        def turn(key, *sides):
+        def turn(key, *sides, order=(1, 0), in_sum_banks=False):
             for h in sides:
-                bank = psum_t.tile([P, 2, 2, P], F32, name="bank")
-                for a in range(2):
+                if in_sum_banks:
+                    bank = psum_m.tile([P, 2, 2, P], F32, name="bank", tag="sum%d" % (LEAD + h))
+                else:
+                    bank = psum_t.tile([P, 2, 2, P], F32, name="bank")
+                for a in order:
                     words = scaled[key][:, PASS * (2 * h + a) : PASS * (2 * h + a) + PASS].bitcast(F32)
                     g = key[1] if isinstance(key, tuple) else 2 * h + a
                     for u in range(2):
@@ -209,7 +216,7 @@ def tile_galore_projected_step_d2_kernel(tc, grad_bytes, grad_scale, basis_bytes
 
         def multiply(i, passes=range(PASSES), cols=ALL):
             if (i, cols.start) not in sums:
-                acc = psum_m.tile([P, RANK], F32, name="acc")
+                acc = psum_m.tile([P, RANK], F32, name="acc", tag="sum%d" % (len(sums) % SUM_BANKS))
                 sums[i, cols.start] = acc
             cod, scl = codes[i]
             order = BASIS_ORDER if i < LEAD else range(PASSES)
@@ -259,85 +266,88 @@ def tile_galore_projected_step_d2_kernel(tc, grad_bytes, grad_scale, basis_bytes
             dst, src = step[i][0][:, i - step[i][1], :], new[i][0][:, i - new[i][1], :]
             nc.gpsimd.tensor_scalar(out=dst, in0=src, scalar1=lr_f[:, i : i + 1], scalar2=0.0, op0=MULT, op1=ADD)
 
-        def step_on_vector(i):
-            buffer = keep.tile([P, 1, RANK], F32, name="step%d" % i, tag="bytes%d" % (i % SINGLE_LOADS), align_bytes=LINE)
+        def step_on_vector(i, parts=(ALL,)):
+            buffer = keep.tile([P, 1, RANK], F32, name="step%d" % i, tag=spare.pop(), align_bytes=LINE)
             assign(step, buffer, i, 1)
-            nc.vector.tensor_scalar(out=buffer[:, 0, :], in0=new[i][0][:, 0, :], scalar1=lr_f[:, i : i + 1], scalar2=None, op0=MULT)
+            for cols in parts:
+                nc.vector.tensor_scalar(out=buffer[:, 0, cols], in0=new[i][0][:, 0, cols], scalar1=lr_f[:, i : i + 1], scalar2=None, op0=MULT)
             store(step, step_rows, i)
 
         def step_on_scalar(i):
             if i not in step:
-                buffer = keep.tile([P, 1, RANK], F32, name="step%d" % i, tag="basis_bytes%d" % (i % PASSES), align_bytes=LINE)
+                buffer = keep.tile([P, 1, RANK], F32, name="step%d" % i, tag=spare.pop(), align_bytes=LINE)
                 assign(step, buffer, i, 1)
             dst, src = step[i][0][:, i - step[i][1], :], new[i][0][:, i - new[i][1], :]
             nc.scalar.activation(out=dst, in_=src, func=COPY, scale=lr_f[:, i : i + 1])
 
         basis = [("basis", g) for g in BASIS_ORDER]
         cast(0, CAST_PASSES[0])
-        scale_on_vector(0, 2, 3)
-        turn(0, 1)
-        scale_on_vector(0, 0, 1)
+        scale_on_vector(0, 3, 2, 1, 0)
         nc.vector.tensor_copy(out=by_partition[0:BLOCKS], in_=by_column[:].unsqueeze(2).to_broadcast([BLOCKS, ROWS, P // ROWS]))
-        turn(0, 0)
-        spread = psum_m.tile([P, RANK], F32, name="acc")
+        turn(0, 1, 0)
+        spread = psum_m.tile([P, RANK], F32, name="spread", tag="sum%d" % LEAD)
         nc.tensor.transpose(spread[:, 0:P], by_partition[:].rearrange("p b r -> p (b r)"), ident[:])
+        cast(1, CAST_PASSES[1])
         cast(basis[0], ROWS)
-        scale_on_vector(1, 0, 1, 2)
+        scale_on_vector(1, 3, 0, 1, 2)
+        scale_on_vector(2, 3)
         nc.vector.tensor_copy(out=basis_sc[:], in_=spread[:, 0:BLOCKS])
-        scale_on_vector(1, 3)
+        scale_on_vector(2, 2)
         empty(0, 1, 0)
-        turn(1, 0, 1)
-        cast(basis[1], ROWS)
+        turn(1, 1, 0)
         scale_basis(BASIS_ORDER[0])
+        cast(basis[1], ROWS)
+        scale_on_vector(2, 1)
         quantise(0)
-        empty(1, 0, 1)
+        scale_on_vector(2, 0)
+        scale_on_vector(3, 3)
+        empty(1, 1, 0)
         turn(basis[0], 0, 1)
-        scale_on_vector(2, 0, 1, 2, 3)
-        cast(basis[2], ROWS)
         scale_basis(BASIS_ORDER[1])
+        scale_on_vector(3, 2)
         quantise(1)
+        cast(basis[2], ROWS)
         empty(basis[0], 0, 1)
         turn(basis[1], 0, 1)
-        cast(basis[3], ROWS)
+        scale_on_vector(3, 1)
         scale_basis(BASIS_ORDER[2])
         scale_on_vector(3, 0)
         quantise_basis(BASIS_ORDER[0])
-        scale_on_vector(3, 1)
-        scale_basis(BASIS_ORDER[3])
-        scale_on_vector(3, 2, 3)
+        cast(basis[3], ROWS)
+        scale_on_vector(4, 3, 2)
         empty(basis[1], 0, 1)
         turn(basis[2], 0, 1)
+        scale_basis(BASIS_ORDER[3])
         multiply_lead(BASIS_ORDER[0])
+        scale_on_vector(4, 1)
         quantise_basis(BASIS_ORDER[1])
         empty(basis[2], 0, 1)
         turn(basis[3], 0, 1)
+        turn(2, 1, 0, in_sum_banks=True)
         scale_on_vector(4, 0)
         quantise_basis(BASIS_ORDER[2])
-        scale_on_vector(4, 1)
+        scale_on_vector(5, 0, 1)
         empty(basis[3], 0, 1)
-        turn(2, 0, 1)
-        multiply_lead(BASIS_ORDER[1])
-        turn(3, 0, 1)
-        multiply_lead(BASIS_ORDER[2])
+        turn(3, 1, 0)
         quantise_basis(BASIS_ORDER[3])
+        for g in BASIS_ORDER[1:]:
+            multiply_lead(g)
 
-        empty(2, 0, 1)
-        cast(5, CAST_PASSES[5])
-        scale_on_vector(4, 2, 3)
-        multiply_lead(BASIS_ORDER[3])
-        turn(4, 0, 1)
+        empty(2, 1, 0)
+        scale_on_vector(5, 2)
+        scale_on_vector(6, 2)
+        turn(4, 1, 0)
         quantise(2)
-        empty(3, 0, 1)
-        scale_on_vector(5, 1, 2, 0)
+        empty(3, 1, 0)
+        scale_on_vector(6, 1)
         turn(5, 0)
-        cast(6, CAST_PASSES[6])
         scale_on_scalar(5)
         quantise(3)
         multiply(2)
         nc.scalar.copy(out=lr_f[:], in_=lr_raw[:])
-        empty(4, 0)
+        empty(4, 1)
         scale_on_scalar(6)
-        scale_on_vector(6, 2, 0, 1)
+        scale_on_vector(6, 0)
         multiply(3, (0, 1))
         first_steps = keep.tile([P, RUN - 1, RANK], F32, name="first_steps", align_bytes=LINE)
         assign(step, first_steps, 0, RUN - 1)
@@ -348,7 +358,7 @@ def tile_galore_projected_step_d2_kernel(tc, grad_bytes, grad_scale, basis_bytes
             load_grad(q + PRELOAD + 2)
             load_mom(first // RUN + 1)
             turn(q + 1, 1)
-            empty(q, 1)
+            empty(q, 0)
             turn(q + 2, 0)
             empty(q + 1, 0)
             turn(q + 2, 1)
@@ -368,11 +378,12 @@ def tile_galore_projected_step_d2_kernel(tc, grad_bytes, grad_scale, basis_bytes
             multiply(q)
             empty(q + 1, 1)
             scale_on_scalar(q + 3)
-            scale_on_vector(q + 3, 0, 1, 2)
+            scale_on_vector(q + 3, 0, 1)
             if last_run:
                 break
             scale_on_vector(q + 4, 0, 1)
-            turn(q + 3, 0, 1)
+            scale_on_vector(q + 3, 2)
+            turn(q + 3, 1, 0)
             empty(q + 2, 0)
             turn(q + 4, 0)
             empty(q + 2, 1)
@@ -386,7 +397,7 @@ def tile_galore_projected_step_d2_kernel(tc, grad_bytes, grad_scale, basis_bytes
             multiply(q + 2, (0, 1))
             step_on_scalar(first + 1)
             store(step, step_rows, first + 1)
-            empty(q + 3, 0)
+            empty(q + 3, 1)
 
         def finish(i):
             momentum(i)
@@ -401,7 +412,8 @@ def tile_galore_projected_step_d2_kernel(tc, grad_bytes, grad_scale, basis_bytes
             step_on_scalar(i)
             store(step, step_rows, i)
 
-        turn(28, 0, 1)
+        scale_on_vector(28, 2)
+        turn(28, 1, 0)
         empty(27, 0, 1)
         quantise(26)
         multiply(26)
@@ -412,49 +424,50 @@ def tile_galore_projected_step_d2_kernel(tc, grad_bytes, grad_scale, basis_bytes
         finish(25)
         store(step, step_rows, 22)
 
-        empty(28, 0)
+        empty(28, 1)
         scale_on_vector(29, 0, 1, 2)
         quantise(27)
-        turn(29, 0, 1)
+        turn(29, 1, 0)
         multiply(27)
-        empty(28, 1)
+        empty(28, 0)
         scale_on_scalar(30)
-        step_beside_momentum(24, 29)
-        finish(26)
-        step_and_store(25)
+        step_and_store(24)
 
-        empty(29, 0)
-        scale_on_vector(30, 0, 1, 2)
-        turn(30, 0)
-        quantise(28)
         empty(29, 1)
+        scale_on_vector(30, 0, 1, 2)
         turn(30, 1)
+        quantise(28)
+        empty(29, 0)
+        turn(30, 0)
         scale_on_scalar(31)
-        step_beside_momentum(26, 30)
+        step_beside_momentum(25, 30)
+        finish(26)
         finish(27)
-        step_and_store(27)
+        step_and_store(26)
         multiply(28)
-
         scale_on_vector(31, 0, 1, 2)
         quantise(29)
-        empty(30, 0, 1)
+        step_on_vector(27)
+        empty(30, 1, 0)
         finish(28)
         turn(31, 0, 1)
         multiply_in_halves(29)
         quantise(30)
-        empty(31, 0)
-        step_and_store(28)
-        empty(31, 1)
-
+        empty(31, 0, 1)
+        step_on_vector(28)
         momentum(29, HALVES[0])
-        quantise(31, slice(0, 2 * P))
         momentum(29, HALVES[1])
         store(new, new_rows, 29)
+        quantise(31, slice(0, 2 * P))
         quantise(31, slice(2 * P, PASSES * P))
-        step_on_vector(29)
-        multiply(30)
-        finish(30)
-        multiply(31)
-        step_on_vector(30)
-        finish(31)
-        step_on_vector(31)
+        step_and_store(29)
+        multiply_in_halves(30)
+        momentum(30, HALVES[0])
+        momentum(30, HALVES[1])
+        store(new, new_rows, 30)
+        step_on_vector(30, HALVES)
+        multiply_in_halves(31)
+        momentum(31, HALVES[0])
+        momentum(31, HALVES[1])
+        store(new, new_rows, 31)
+        step_on_vector(31, HALVES)

@@ -273,12 +273,13 @@ def tile_galore_projected_step_d2_kernel(tc, grad_bytes, grad_scale, basis_bytes
                 nc.vector.tensor_scalar(out=buffer[:, 0, cols], in0=new[i][0][:, 0, cols], scalar1=lr_f[:, i : i + 1], scalar2=None, op0=MULT)
             store(step, step_rows, i)
 
-        def step_on_scalar(i):
+        def step_on_scalar(i, parts=(ALL,)):
             if i not in step:
                 buffer = keep.tile([P, 1, RANK], F32, name="step%d" % i, tag=spare.pop(), align_bytes=LINE)
                 assign(step, buffer, i, 1)
-            dst, src = step[i][0][:, i - step[i][1], :], new[i][0][:, i - new[i][1], :]
-            nc.scalar.activation(out=dst, in_=src, func=COPY, scale=lr_f[:, i : i + 1])
+            for cols in parts:
+                dst, src = step[i][0][:, i - step[i][1], cols], new[i][0][:, i - new[i][1], cols]
+                nc.scalar.activation(out=dst, in_=src, func=COPY, scale=lr_f[:, i : i + 1])
 
         basis = [("basis", g) for g in BASIS_ORDER]
         cast(0, CAST_PASSES[0])
@@ -408,8 +409,8 @@ def tile_galore_projected_step_d2_kernel(tc, grad_bytes, grad_scale, basis_bytes
             step_on_gpsimd(i)
             store(step, step_rows, i)
 
-        def step_and_store(i):
-            step_on_scalar(i)
+        def step_and_store(i, parts=(ALL,)):
+            step_on_scalar(i, parts)
             store(step, step_rows, i)
 
         scale_on_vector(28, 2)
@@ -460,7 +461,7 @@ def tile_galore_projected_step_d2_kernel(tc, grad_bytes, grad_scale, basis_bytes
         store(new, new_rows, 29)
         quantise(31, slice(0, 2 * P))
         quantise(31, slice(2 * P, PASSES * P))
-        step_and_store(29)
+        step_and_store(29, HALVES)
         multiply_in_halves(30)
         momentum(30, HALVES[0])
         momentum(30, HALVES[1])

from contextlib import ExitStack

import concourse.mybir as mybir
from concourse.masks import make_identity

TOKENS, K, RANK = 4096, 2048, 512
P = 128
TILES = TOKENS // P
PASS = 512
PASSES = K // PASS
BLOCK = 128
BLOCKS = K // BLOCK
PASS_BLOCKS = PASS // BLOCK
ROWS = RANK // P
BETA = 0.9
FLOPS = 2 * TOKENS * K * RANK

F32 = mybir.dt.float32
BF16 = mybir.dt.bfloat16
U32 = mybir.dt.uint32
U8 = mybir.dt.uint8
FP8 = mybir.dt.float8_e4m3fn
FP8X4 = mybir.dt.float8_e4m3fn_x4
MULT = mybir.AluOpType.mult
ADD = mybir.AluOpType.add
COPY = mybir.ActivationFunctionType.Copy

IN_ORDER = PASSES - 1
BASIS_ORDER = (IN_ORDER, 0, 1, 2)
LEAD = 2
SUM_BANKS = 4
RUN = 3
IN_RUNS = 24
SINGLE_LOADS = 4
PRELOAD = 16
MOM_TILES = 8
LINE = 256
PIECE = RUN * K // 2
CAST_PASSES = {0: 1, 1: 3, TILES - 3: 1}
CAST_PASSES_IN_RUNS = 2
HALVES = (slice(0, RANK // 2), slice(RANK // 2, RANK))
ALL = slice(0, RANK)


def tile_galore_projected_step_d2_kernel(tc, grad_bytes, grad_scale, basis_bytes, basis_scale, mom, lr, out_0, out_1):
    nc = tc.nc
    grad_rows = grad_bytes.rearrange("(p i) k -> p i k", p=P)
    scale_rows = grad_scale.rearrange("(p i) c -> p (i c)", p=P)
    basis_rows = basis_bytes.rearrange("(p j) k -> p j k", p=P)
    mom_rows = mom.rearrange("(p i) n -> p i n", p=P)
    step_rows = out_0.rearrange("(p i) n -> p i n", p=P)
    new_rows = out_1.rearrange("(p i) n -> p i n", p=P)

    loads = [(i, 1) for i in range(SINGLE_LOADS)]
    loads.extend((i, RUN) for i in range(SINGLE_LOADS, TILES - SINGLE_LOADS, RUN))
    loads.extend((i, 1) for i in range(TILES - SINGLE_LOADS, TILES))

    with ExitStack() as ctx:
        keep = ctx.enter_context(tc.tile_pool(name="keep", bufs=1))
        work = ctx.enter_context(tc.tile_pool(name="work", bufs=4))
        psum_t = ctx.enter_context(tc.psum_pool(name="psum_t", bufs=4))
        psum_m = ctx.enter_context(tc.psum_pool(name="psum_m", bufs=1))
        ctx.enter_context(tc.manual_schedule())

        raw = {}
        first_bytes = {}
        cast_values = {}
        scaled = {}
        banks = {}
        turned = {}
        codes = {}
        sums = {}
        mom_raw = {}
        new = {}
        step = {}
        spare = ["bytes%d" % i for i in range(SINGLE_LOADS)] + ["basis_bytes%d" % g for g in range(PASSES)]

        by_column = keep.tile([BLOCKS, ROWS], F32, name="by_column")
        by_partition = keep.tile([P, ROWS, P // ROWS], F32, name="by_partition")
        nc.vector.memset(by_partition[:], 0.0)
        ident = keep.tile([P, P], F32, name="ident")
        make_identity(nc, ident[:])

        def load_grad(upto):
            while loads and loads[0][0] <= upto:
                first, count = loads.pop(0)
                piece = K if count == 1 else PIECE
                g = keep.tile([P, count * K // piece, piece + (0 if count == 1 else LINE)], U8, name="g%d" % first, tag="bytes%d" % (first + count - 1), align_bytes=LINE)
                nc.sync.dma_start(out=g[:, :, 0:piece], in_=grad_rows[:, first : first + count, :].rearrange("p i k -> p (i k)").rearrange("p (a x) -> p a x", x=piece))
                for t in range(count):
                    first_bytes[first + t] = g[:, K * t // piece, K * t % piece : piece]
                    raw[first + t] = [g[:, (K * t + K // 2 * h) // piece, (K * t + K // 2 * h) % piece : (K * t + K // 2 * h) % piece + K // 2] for h in range(2)]

        def load_basis(g):
            b = keep.tile([P, ROWS, PASS], U8, name="basis%d" % g, tag="basis_bytes%d" % g, align_bytes=LINE)
            nc.sync.dma_start(out=b[:], in_=basis_rows[:, :, PASS * g : PASS * g + PASS])
            first_bytes["basis", g] = b[:].rearrange("p j k -> p (j k)")

        def load_mom(m):
            if m < TILES // MOM_TILES:
                mo = keep.tile([P, MOM_TILES, RANK], BF16, name="mom%d" % m, align_bytes=LINE)
                nc.sync.dma_start(out=mo[:], in_=mom_rows[:, MOM_TILES * m : MOM_TILES * m + MOM_TILES, :])
                for t in range(MOM_TILES):
                    mom_raw[MOM_TILES * m + t] = mo[:, t, :]

        first_scales = keep.tile([P, SINGLE_LOADS * BLOCKS], F32, name="first_scales")
        nc.sync.dma_start(out=first_scales[:], in_=scale_rows[:, 0 : SINGLE_LOADS * BLOCKS])
        load_grad(1)
        with nc.allow_non_contiguous_dma(reason="the 64 basis scales, a column block to a partition"):
            nc.sync.dma_start(out=by_column[:], in_=basis_scale.rearrange("b c -> c b"))
        for n, g in enumerate(BASIS_ORDER):
            load_grad(min(n + 1, SINGLE_LOADS - 1))
            load_basis(g)
        other_scales = keep.tile([P, (TILES - SINGLE_LOADS) * BLOCKS], F32, name="other_scales")
        nc.sync.dma_start(out=other_scales[:], in_=scale_rows[:, SINGLE_LOADS * BLOCKS :])
        load_grad(SINGLE_LOADS)
        load_mom(0)
        lr_raw = keep.tile([P, TILES], BF16, name="lr_raw")
        nc.sync.dma_start(out=lr_raw[:], in_=lr.rearrange("(p i) -> p i", p=P))
        load_grad(PRELOAD)

        warm_up = keep.tile([P, 1], F32, name="warm_up")
        nc.scalar.activation(out=warm_up[:], in_=ident[:, 0:1], func=COPY)

        basis_sc = keep.tile([P, BLOCKS], F32, name="basis_sc")
        lr_f = keep.tile([P, TILES], F32, name="lr_f")
        basis_codes = keep.tile([P, PASSES, RANK], U32, name="basis_codes", align_bytes=64)
        basis_mx_scales = keep.tile([P, PASSES, RANK], U8, name="basis_mx_scales", align_bytes=64)

        def columns(c):
            return slice(BLOCK * c, BLOCK * c + BLOCK)

        def block_bytes(i, c):
            return raw[i][c // (BLOCKS // 2)][:, columns(c % (BLOCKS // 2))].bitcast(FP8)

        def scale_of(i, c):
            tile, first = (first_scales, 0) if i < SINGLE_LOADS else (other_scales, SINGLE_LOADS)
            return tile[:, BLOCKS * (i - first) + c : BLOCKS * (i - first) + c + 1]

        def cast(key, passes):
            values = work.tile([P, PASS * passes], BF16, name="values", align_bytes=64)
            nc.scalar.copy(out=values[:], in_=first_bytes[key][:, 0 : PASS * passes].bitcast(FP8))
            cast_values[key] = (values, PASS_BLOCKS * passes)

        def scaled_tile(key):
            if key not in scaled:
                dst = work.tile([P, K], BF16, name="scaled", align_bytes=64, bufs=7)
                scaled[key] = dst
            return scaled[key]

        def scale_on_vector(i, *passes):
            values, cast_blocks = cast_values.get(i, (None, 0))
            for g in passes:
                for c in range(PASS_BLOCKS * g, PASS_BLOCKS * g + PASS_BLOCKS):
                    src = values[:, columns(c)] if c < cast_blocks else block_bytes(i, c)
                    dst = scaled_tile(i)[:, columns(c)]
                    if g != IN_ORDER:
                        halves = scaled[i][:, PASS * g : PASS * g + PASS].rearrange("p (u b j) -> p b u j", u=2, j=16)
                        dst = halves[:, 4 * (c % PASS_BLOCKS) : 4 * (c % PASS_BLOCKS) + 4]
                        src = src.rearrange("p (b u j) -> p b u j", u=2, j=16)
                    nc.vector.tensor_scalar(out=dst, in0=src, scalar1=scale_of(i, c), scalar2=None, op0=MULT)

        def scale_on_scalar(i):
            for c in range(PASS_BLOCKS * IN_ORDER, BLOCKS):
                nc.scalar.activation(out=scaled_tile(i)[:, columns(c)], in_=block_bytes(i, c), func=COPY, scale=scale_of(i, c))

        def scale_basis(g):
            src, dst = cast_values["basis", g][0][:], scaled_tile(("basis", g))[:]
            for c in range(PASS_BLOCKS):
                scale = basis_sc[:, PASS_BLOCKS * g + c : PASS_BLOCKS * g + c + 1]
                if g == IN_ORDER:
                    pieces = [[x.rearrange("p (j k) -> p j k", j=ROWS)[:, :, columns(c)] for x in (dst, src)]]
                else:
                    to = dst.rearrange("p (j u b x) -> p j b u x", j=ROWS, u=2, x=16)
                    of = src.rearrange("p (j b u x) -> p j b u x", j=ROWS, u=2, x=16)
                    pieces = [[x[:, :, 4 * c : 4 * c + 4, u, :] for x in (to, of)] for u in range(2)]
                for out, in0 in pieces:
                    nc.vector.tensor_scalar(out=out, in0=in0, scalar1=scale, scalar2=None, op0=MULT)

        def turn(key, *sides, order=(1, 0), in_sum_banks=False):
            for h in sides:
                if in_sum_banks:
                    bank = psum_m.tile([P, 2, 2, P], F32, name="bank", tag="sum%d" % (LEAD + h))
                else:
                    bank = psum_t.tile([P, 2, 2, P], F32, name="bank")
                for a in order:
                    words = scaled[key][:, PASS * (2 * h + a) : PASS * (2 * h + a) + PASS].bitcast(F32)
                    g = key[1] if isinstance(key, tuple) else 2 * h + a
                    for u in range(2):
                        nc.tensor.transpose(bank[:, a, u, :], words[:, u : 2 * P : 2] if g == IN_ORDER else words[:, P * u : P * u + P], ident[:])
                banks[key, h] = bank

        def empty(key, *sides):
            if key not in turned:
                dst = work.tile([P, K], BF16, name="turned", align_bytes=64)
                turned[key] = dst
            for h in sides:
                words = turned[key][:].bitcast(F32)
                if isinstance(key, tuple):
                    out = words.rearrange("p (r j u) -> p r j u", j=ROWS, u=2)[:, :, 2 * h : 2 * h + 2, :]
                    nc.scalar.copy(out=out, in_=banks[key, h][:].rearrange("p a u r -> p r a u"))
                else:
                    out = words[:, PASS * h : PASS * h + PASS].rearrange("p (a r u) -> p a r u", a=2, u=2)
                    nc.scalar.copy(out=out, in_=banks[key, h][:].rearrange("p a u r -> p a r u"))

        def quantise_basis(g):
            nc.vector.quantize_mx(out=basis_codes[:, g, :].bitcast(FP8X4), scales=basis_mx_scales[:, g, :], in_=turned["basis", g][:])

        def quantise(i, words=slice(0, PASSES * P)):
            if i not in codes:
                cod = work.tile([P, PASSES * P], U32, name="cod", align_bytes=64, bufs=5)
                scl = work.tile([P, PASSES * P], U8, name="scl", align_bytes=64, bufs=5)
                codes[i] = (cod, scl)
            cod, scl = codes[i]
            nc.vector.quantize_mx(out=cod[:, words].bitcast(FP8X4), scales=scl[:, words], in_=turned[i][:, 4 * words.start : 4 * words.stop])

        def multiply(i, passes=range(PASSES), cols=ALL):
            if (i, cols.start) not in sums:
                acc = psum_m.tile([P, RANK], F32, name="acc", tag="sum%d" % (len(sums) % SUM_BANKS))
                sums[i, cols.start] = acc
            cod, scl = codes[i]
            order = BASIS_ORDER if i < LEAD else range(PASSES)
            for g in passes:
                nc.tensor.matmul_mx(
                    out=sums[i, cols.start][:, cols],
                    lhsT=cod[:, P * g : P * g + P].bitcast(FP8X4),
                    lhsT_scale=scl[:, P * g : P * g + P],
                    rhs=basis_codes[:, g, cols].bitcast(FP8X4),
                    rhs_scale=basis_mx_scales[:, g, cols],
                    start=(g == order[0]),
                    stop=(g == order[-1]),
                )

        def multiply_lead(g):
            for i in range(LEAD):
                multiply(i, (g,))

        def multiply_in_halves(i):
            for cols in HALVES:
                multiply(i, cols=cols)

        def assign(table, buffer, first, count):
            for i in range(first, first + count):
                table[i] = (buffer, first, count)

        def store(table, rows, i):
            buffer, first, count = table[i]
            nc.sync.dma_start(out=rows[:, first : first + count, :], in_=buffer[:, 0:count, :])

        def momentum(i, cols=ALL):
            if i not in new:
                if i < IN_RUNS:
                    buffer = work.tile([P, RUN, RANK], F32, name="new_run", bufs=3, align_bytes=LINE)
                    assign(new, buffer, i, RUN)
                else:
                    buffer = work.tile([P, 1, RANK], F32, name="new_one", align_bytes=LINE)
                    assign(new, buffer, i, 1)
            buffer, first, count = new[i]
            nc.vector.scalar_tensor_tensor(out=buffer[:, i - first, cols], in0=mom_raw[i][:, cols], scalar=BETA, in1=sums[i, cols.start][:, cols], op0=MULT, op1=ADD)

        def step_buffer(first, count, after_tile):
            buffer = keep.tile([P, RUN if count > 1 else 1, RANK], F32, name="step%d" % first, tag="bytes%d" % after_tile, align_bytes=LINE)
            assign(step, buffer, first, count)

        def step_on_gpsimd(i):
            dst, src = step[i][0][:, i - step[i][1], :], new[i][0][:, i - new[i][1], :]
            nc.gpsimd.tensor_scalar(out=dst, in0=src, scalar1=lr_f[:, i : i + 1], scalar2=0.0, op0=MULT, op1=ADD)

        def step_on_vector(i, parts=(ALL,)):
            buffer = keep.tile([P, 1, RANK], F32, name="step%d" % i, tag=spare.pop(), align_bytes=LINE)
            assign(step, buffer, i, 1)
            for cols in parts:
                nc.vector.tensor_scalar(out=buffer[:, 0, cols], in0=new[i][0][:, 0, cols], scalar1=lr_f[:, i : i + 1], scalar2=None, op0=MULT)
            store(step, step_rows, i)

        def step_on_scalar(i, parts=(ALL,)):
            if i not in step:
                buffer = keep.tile([P, 1, RANK], F32, name="step%d" % i, tag=spare.pop(), align_bytes=LINE)
                assign(step, buffer, i, 1)
            for cols in parts:
                dst, src = step[i][0][:, i - step[i][1], cols], new[i][0][:, i - new[i][1], cols]
                nc.scalar.activation(out=dst, in_=src, func=COPY, scale=lr_f[:, i : i + 1])

        basis = [("basis", g) for g in BASIS_ORDER]
        cast(0, CAST_PASSES[0])
        scale_on_vector(0, 3, 2, 1, 0)
        nc.vector.tensor_copy(out=by_partition[0:BLOCKS], in_=by_column[:].unsqueeze(2).to_broadcast([BLOCKS, ROWS, P // ROWS]))
        turn(0, 1, 0)
        spread = psum_m.tile([P, RANK], F32, name="spread", tag="sum%d" % LEAD)
        nc.tensor.transpose(spread[:, 0:P], by_partition[:].rearrange("p b r -> p (b r)"), ident[:])
        cast(1, CAST_PASSES[1])
        cast(basis[0], ROWS)
        scale_on_vector(1, 3, 0, 1, 2)
        scale_on_vector(2, 3)
        nc.vector.tensor_copy(out=basis_sc[:], in_=spread[:, 0:BLOCKS])
        scale_on_vector(2, 2)
        empty(0, 1, 0)
        turn(1, 1, 0)
        scale_basis(BASIS_ORDER[0])
        cast(basis[1], ROWS)
        scale_on_vector(2, 1)
        quantise(0)
        scale_on_vector(2, 0)
        scale_on_vector(3, 3)
        empty(1, 1, 0)
        turn(basis[0], 0, 1)
        scale_basis(BASIS_ORDER[1])
        scale_on_vector(3, 2)
        quantise(1)
        cast(basis[2], ROWS)
        empty(basis[0], 0, 1)
        turn(basis[1], 0, 1)
        scale_on_vector(3, 1)
        scale_basis(BASIS_ORDER[2])
        scale_on_vector(3, 0)
        quantise_basis(BASIS_ORDER[0])
        cast(basis[3], ROWS)
        scale_on_vector(4, 3, 2)
        empty(basis[1], 0, 1)
        turn(basis[2], 0, 1)
        scale_basis(BASIS_ORDER[3])
        multiply_lead(BASIS_ORDER[0])
        scale_on_vector(4, 1)
        quantise_basis(BASIS_ORDER[1])
        empty(basis[2], 0, 1)
        turn(basis[3], 0, 1)
        turn(2, 1, 0, in_sum_banks=True)
        scale_on_vector(4, 0)
        quantise_basis(BASIS_ORDER[2])
        scale_on_vector(5, 0, 1)
        empty(basis[3], 0, 1)
        turn(3, 1, 0)
        quantise_basis(BASIS_ORDER[3])
        for g in BASIS_ORDER[1:]:
            multiply_lead(g)

        empty(2, 1, 0)
        scale_on_vector(5, 2)
        scale_on_vector(6, 2)
        turn(4, 1, 0)
        quantise(2)
        empty(3, 1, 0)
        scale_on_vector(6, 1)
        turn(5, 0)
        scale_on_scalar(5)
        quantise(3)
        multiply(2)
        nc.scalar.copy(out=lr_f[:], in_=lr_raw[:])
        empty(4, 1)
        scale_on_scalar(6)
        scale_on_vector(6, 0)
        multiply(3, (0, 1))
        first_steps = keep.tile([P, RUN - 1, RANK], F32, name="first_steps", align_bytes=LINE)
        assign(step, first_steps, 0, RUN - 1)

        for first in range(0, IN_RUNS, RUN):
            q = first + 4
            last_run = first + RUN == IN_RUNS
            load_grad(q + PRELOAD + 2)
            load_mom(first // RUN + 1)
            turn(q + 1, 1)
            empty(q, 0)
            turn(q + 2, 0)
            empty(q + 1, 0)
            turn(q + 2, 1)
            cast(q + 4, CAST_PASSES.get(q + 4, CAST_PASSES_IN_RUNS))
            if first > 0:
                step_buffer(first - 1, RUN - 1 if last_run else RUN, q + 2)
                step_on_gpsimd(first - 1)
            momentum(first)
            step_on_gpsimd(first)
            if last_run:
                store(step, step_rows, first)
            momentum(first + 1)
            momentum(first + 2)
            store(new, new_rows, first)
            quantise(q)
            multiply(q - 1, (2, 3))
            multiply(q)
            empty(q + 1, 1)
            scale_on_scalar(q + 3)
            scale_on_vector(q + 3, 0, 1)
            if last_run:
                break
            scale_on_vector(q + 4, 0, 1)
            scale_on_vector(q + 3, 2)
            turn(q + 3, 1, 0)
            empty(q + 2, 0)
            turn(q + 4, 0)
            empty(q + 2, 1)
            quantise(q + 1)
            scale_on_scalar(q + 4)
            scale_on_vector(q + 4, 2)
            scale_on_scalar(q + 5)
            scale_on_vector(q + 5, 0, 1, 2)
            quantise(q + 2)
            multiply(q + 1)
            multiply(q + 2, (0, 1))
            step_on_scalar(first + 1)
            store(step, step_rows, first + 1)
            empty(q + 3, 1)

        def finish(i):
            momentum(i)
            store(new, new_rows, i)

        def step_beside_momentum(i, after_tile):
            step_buffer(i, 1, after_tile)
            step_on_gpsimd(i)
            store(step, step_rows, i)

        def step_and_store(i, parts=(ALL,)):
            step_on_scalar(i, parts)
            store(step, step_rows, i)

        scale_on_vector(28, 2)
        turn(28, 1, 0)
        empty(27, 0, 1)
        quantise(26)
        multiply(26)
        scale_on_scalar(29)
        step_on_scalar(22)
        step_beside_momentum(23, 28)
        finish(24)
        finish(25)
        store(step, step_rows, 22)

        empty(28, 1)
        scale_on_vector(29, 0, 1, 2)
        quantise(27)
        turn(29, 1, 0)
        multiply(27)
        empty(28, 0)
        scale_on_scalar(30)
        step_and_store(24)

        empty(29, 1)
        scale_on_vector(30, 0, 1, 2)
        turn(30, 1)
        quantise(28)
        empty(29, 0)
        turn(30, 0)
        scale_on_scalar(31)
        step_beside_momentum(25, 30)
        finish(26)
        finish(27)
        step_and_store(26)
        multiply(28)
        scale_on_vector(31, 0, 1, 2)
        quantise(29)
        step_on_vector(27)
        empty(30, 1, 0)
        finish(28)
        turn(31, 0, 1)
        multiply_in_halves(29)
        quantise(30)
        empty(31, 0, 1)
        step_on_vector(28)
        momentum(29, HALVES[0])
        momentum(29, HALVES[1])
        store(new, new_rows, 29)
        quantise(31, slice(0, 2 * P))
        quantise(31, slice(2 * P, PASSES * P))
        step_and_store(29, HALVES)
        multiply_in_halves(30)
        momentum(30, HALVES[0])
        momentum(30, HALVES[1])
        store(new, new_rows, 30)
        step_on_vector(30, HALVES)
        multiply_in_halves(31)
        momentum(31, HALVES[0])
        momentum(31, HALVES[1])
        store(new, new_rows, 31)
        step_on_vector(31, HALVES)
